import numpy as np, ml_dtypes
CORES = [3,11,19,27,35,43,51,59]
N = 8
BF = ml_dtypes.bfloat16
def gentries(a):
    return np.ascontiguousarray(a.reshape(8, 16, -1).transpose(0, 2, 1)).reshape(8, -1)
def gtable(e):
    e = np.asarray(e); return np.ascontiguousarray(e.reshape(8, -1, 16).transpose(0, 2, 1)).reshape(128, -1).astype(np.int32)
F, M, T, H = 512, 6, 3, 8
W = N * F
def pack(x, m, nm):
    return {"x": np.ascontiguousarray(x.reshape(128, N, F).transpose(1, 0, 2)).astype(BF), "mix": np.ascontiguousarray(m.reshape(16, N, F).transpose(1, 0, 2)).astype(BF),
            "nb": np.stack([gtable(np.ascontiguousarray(nm[:, q * F:(q + 1) * F].transpose(0, 2, 1)).reshape(8, -1)) for q in range(N)])}
def spaced(nm):
    nm = nm.astype(np.int64) % W; own = np.arange(W)[None, :]
    for j in range(M):
        for i in range(M + 1):
            clash = nm[:, :, j] == own
            for h in range(j): clash = clash | (nm[:, :, j] == nm[:, :, h])
            nm[:, :, j] = (nm[:, :, j] + clash) % W
    return nm
def links(rng):
    far = rng.integers(0, W, (8, W, M)); by = np.arange(W)[None, :, None] + rng.integers(-24, 25, (8, W, M))
    return spaced(np.where(rng.random((8, W, M)) < 0.5, far, by))
def among(rng, pool, own):
    keys = np.where(pool[None, :] == own[:, None], 2.0, rng.random((len(own), len(pool))))
    return pool[np.argsort(keys, axis=1)[:, :M]]
def setup_inputs(rng):
    form = rng.integers(0, 16, (8, 16, 24)); kind = rng.integers(0, 24, (8, W))
    x = np.clip(np.stack([form[g][:, kind[g]] for g in range(8)]) + rng.integers(-3, 4, (8, 16, W)), 0, 15)
    m = np.clip(np.add.reduce(x, axis=0) + rng.integers(-40, 41, (16, W)), 0, 120)
    return pack(x, m, links(rng))
def setup_inputs_spread(rng):
    s = 0.5 + 0.5 * rng.random((1, 1, W))
    x = np.floor(16 * s * rng.random((8, 16, W))).astype(np.int64) * (rng.random((1, 1, W)) > 0.0625)
    m = np.floor(121 * (0.6 + 0.4 * rng.random((1, W))) * rng.random((16, W))).astype(np.int64)
    c = np.floor(W * rng.random((8, W, M)) ** 3).astype(np.int64); c[1::2] = W - 1 - c[1::2]
    return pack(x, m, spaced(c))
def setup_inputs_ends(rng):
    one = np.concatenate([np.repeat(np.arange(8), F // 64), np.full(F // 8, 8), np.full(F // 32, 9), np.full(F // 8, 10)])
    one = np.concatenate([one, np.full(F - len(one), 11)])
    kind = np.concatenate([rng.permutation(one) for q in range(N)])
    kind[:60] = np.tile(np.arange(10), 6); kind[W - 60:] = np.tile(np.arange(10), 6)
    edge = np.concatenate([np.arange(60), np.arange(W - 60, W)])
    x = 15 * rng.integers(0, 2, (8, 16, W)); m = 120 * rng.integers(0, 2, (16, W))
    x[:, :, kind < 9] = 0; i = np.flatnonzero(kind < 8); x[kind[i], :, i] = 15
    m[:, kind < 8] = 120; m[:, kind == 8] = 0
    x[:, :, kind == 10] = 15; m[:, kind == 10] = 120 * rng.integers(0, 2, (1, int(np.sum(kind == 10))))
    c = np.where(rng.random((8, W, M)) < 0.5, edge[rng.integers(0, 120, (8, W, M))], rng.integers(0, W, (8, W, M)))
    c[:, :, 0] = 0; c[:, :, M - 1] = W - 1
    nm = spaced(np.take_along_axis(c, np.argsort(rng.random(c.shape), axis=-1), -1))
    full = np.flatnonzero(kind == 10); quiet = edge[kind[edge] == 8]
    for g in range(8):
        loud = edge[kind[edge] == g]
        for who, pool in ((kind == g, loud), ((kind < 9) & (kind != g), quiet), (kind == 9, loud), (kind == 10, full)):
            nm[g, who] = among(rng, pool, np.flatnonzero(who))
    return pack(x, m, nm)
def setup_inputs_corners(rng):
    own = np.arange(W)[:, None]; j = np.arange(M)[None, :]; b = own // (M + 1) * (M + 1)
    ways = [own + 1 + j, own - 1 - j, b + (own - b + 1 + j) % (M + 1), 0 * own + j, 0 * own + W - 1 - j, 0 * own + np.where(j % 2 == 0, j // 2, W - 1 - j // 2),
            np.where(j == 0, own ^ 1, own + W // 2 + 2 * j), own + F * (j + 1)]
    p = rng.permutation(8)
    c = np.stack([np.concatenate([ways[(int(p[g]) + q) % 8][q * F:(q + 1) * F] for q in range(N)]) for g in range(8)])
    z = rng.integers(4, 12, (8, 16, 1)); kind = rng.integers(0, 4, (8, 1, W)); o = np.argsort(rng.random((8, 16, W)), axis=1)
    size = np.where(kind == 0, 0, np.where(kind == 1, 2, np.where(o < np.where(kind == 2, H, H - 1), 1, 3)))
    x = z + size * (2 * rng.integers(0, 2, (8, 16, W)) - 1)
    m = np.clip(np.add.reduce(x, axis=0) + rng.choice(np.array([-24, 0, 24]), (1, W)), 0, 120)
    return pack(x, m, spaced(c))
def setup_inputs_calm(rng):
    x = rng.integers(4, 12, (8, 16, 1)) + rng.integers(0, 2, (8, 16, W))
    m = np.clip(np.add.reduce(x, axis=0) + rng.integers(-3, 4, (16, W)), 0, 120)
    return pack(x, m, links(rng))
def steps(rng, x, m, nm, kind, quiet):
    left = rng.permutation(np.flatnonzero(kind == 33)); h, h2 = [int(g) for g in rng.permutation(8)[:2]]; others = [g for g in range(8) if g != h]
    cut = np.add.accumulate(np.array([M, M, M, M, M + 1, M + 1, 7, 7, 8, 8])); who = left[:int(cut[-1]) + 8 * N]
    p1a, p1b, p2a, p2b, p3a, p3b, da, db, sa, sb, ask = np.split(who, cut)
    x[:, :, who] = 0; m[:, who] = 0
    for g in range(8): nm[g, who] = among(rng, quiet, who)
    m1 = rng.integers(20, 60, 16); m2 = rng.integers(40, 80, (16, 1)); m3 = rng.integers(40, 70, (16, 1))
    up = np.where(rng.permutation(16) < H, 1, rng.integers(-1, 1, 16))
    m[:, p1a] = m1[:, None]; m[:, p1b] = (m1 + up)[:, None]
    md = rng.integers(80, 99, (16, 7)); ms = rng.integers(104, 121, (16, 8))
    for p1, p2, p3, d, s in ((p1a, p2a, p3a, da, sa), (p1b, p2b, p3b, db, sb)):
        m[:, p2] = m2; m[:, p3] = m3; m[:, d] = md; m[:, s] = ms
        nm[h, p2] = among(rng, p1, p2); nm[h2, p3] = among(rng, p2, p3); nm[h, p3] = among(rng, p3, p3)
        nm[h, d] = among(rng, p3, d); nm[h, s] = among(rng, p3, s)
    j = int(rng.integers(0, M)); k = (j + T - 1) % M
    for i, g in enumerate(others):
        two = np.array([da[i], db[i]]); nm[g, two] = among(rng, np.flatnonzero(kind == g + 16), two); nm[g, da[i], k] = db[i]
        for n in range(8):
            two = np.array([sa[n], sb[n]]); nm[g, two] = among(rng, np.flatnonzero(kind == g + 16 * int(rng.integers(0, 2))), two); nm[g, sa[n], k] = sb[n]
        nm[g, ask[::2], j] = da[i]; nm[g, ask[1::2], j] = sa[(np.arange(len(ask[1::2])) + i) % 8]
def setup_inputs_loud(rng):
    one = np.concatenate([np.repeat(np.arange(24), F // 64), np.repeat(np.arange(24, 32), F // 20), np.full(F // 16, 32)])
    one = np.concatenate([one, np.full(F - len(one), 33)])
    kind = np.concatenate([rng.permutation(one) for q in range(N)])
    x = rng.integers(0, 16, (8, 16, W)); x[:, :, kind < 33] = 0
    i = np.flatnonzero(kind < 32); x[kind[i] % 8, :, i] = 15
    m = np.clip(np.add.reduce(x, axis=0) + rng.integers(-40, 41, (16, W)), 0, 120); m[:, kind == 32] = 0
    nm = spaced(rng.integers(0, W, (8, W, M)))
    quiet = rng.permutation(np.flatnonzero(kind == 32))[:64]
    width = rng.permutation(np.array([3, 4, 6, 8, 12, 16, 25, 25]))
    for g in range(8):
        low, mid, high, free = [np.flatnonzero(kind == g + 8 * h) for h in range(4)]
        still = np.flatnonzero((kind == 32) | ((kind < 32) & (kind % 8 != g)))
        nm[g, still] = among(rng, quiet, still)
        nm[g, free] = among(rng, free, free); nm[g, high] = among(rng, high, high); nm[g, low] = among(rng, low, low)
        nm[g, low, np.arange(len(low)) % M] = rng.choice(high, len(low))
        nm[g, mid] = among(rng, high, mid)
        half = np.argsort(rng.random((len(mid), M)), axis=1) < M // 2
        for j in range(M):
            s = mid[half[:, j]]; nm[g, s, j] = rng.choice(low[(j + T - 1) % M::M], len(s))
        c = rng.integers(98, 120, 16); step = 1 + (rng.permutation(16) < H - 1)
        m[:, low] = (c - step)[:, None]; m[:, mid] = c[:, None]; m[:, high] = (c + 1)[:, None]
        w = int(width[g]); m[:, free] = rng.integers(96, 122 - w, (16, 1)) + rng.integers(0, w, (16, len(free)))
    steps(rng, x, m, nm, kind, quiet)
    return pack(x, m, nm)
def check_ranges(d):
    bad = []
    for k, hi in (("x", 15), ("mix", 120), ("nb", W - 1)):
        v = np.asarray(d[k]).astype(np.float64)
        if not np.all((v >= 0) & (v <= hi)): bad.append("range of " + k)
        elif np.any(v != np.floor(v)): bad.append("whole numbers of " + k)
    nm = np.stack([gentries(a) for a in d["nb"]]).astype(np.int64).reshape(N, 8, M, F)
    if np.any(nm == np.arange(W).reshape(N, 1, 1, F)): bad.append("a frame names itself in nb")
    s = np.sort(nm, axis=2)
    if np.any(s[:, :, 1:] == s[:, :, :-1]): bad.append("a frame's names in nb repeat")
    return bad
def reference(x, mix, nb):
    a = np.ascontiguousarray(x.astype(np.float64).reshape(N, 8, 16, F).transpose(1, 2, 0, 3)).reshape(8, 16, W)
    m = np.ascontiguousarray(mix.astype(np.float64).transpose(1, 0, 2)).reshape(16, W)
    nm = np.stack([gentries(b) for b in nb]).astype(np.int64).reshape(N, 8, M, F)
    nm = np.ascontiguousarray(nm.transpose(1, 2, 0, 3)).reshape(8, M, W)
    own = np.arange(W)
    for t in range(T):
        v = np.stack([a[g][:, nm[g]] for g in range(8)])
        e = np.sort(np.concatenate([a[:, :, None], v], axis=2), axis=2)[:, :, M // 2]
        c = np.take_along_axis(np.roll(nm, -(t % M), axis=1), nm, 2)
        void = c == own
        for i in range(M): void = void | (c == nm[:, i:i + 1])
        for j in range(1, M): void[:, j] = void[:, j] | np.any(c[:, :j] == c[:, j:j + 1], axis=1)
        u = np.stack([a[g][:, c[g]] for g in range(8)])
        near = np.abs(u - a[:, :, None]) < np.abs(v - a[:, :, None])
        n = np.add.reduce(near.astype(np.int64), axis=1)
        nm = np.where((n >= H) & ~void, c, nm)
        if t < T - 1: a = np.maximum(e + 0.125 * (m - np.add.reduce(e, axis=0)), 0.0)
    e2 = e * e
    return {"ye": np.ascontiguousarray(e2.reshape(128, N, F).transpose(1, 0, 2)).astype(np.float32),
            "yd": np.ascontiguousarray(np.add.reduce(e2, axis=0).reshape(16, N, F).transpose(1, 0, 2)).astype(np.float32),
            "yn": np.stack([gtable(np.ascontiguousarray(nm[:, :, q * F:(q + 1) * F]).reshape(8, -1)) for q in range(N)]).astype(np.float32)}

def check_inputs(d):
    bad = list(check_ranges(d))
    if not bad:
        for name, y in reference(**d).items():
            for q in range(N):
                v = np.abs(np.asarray(y[q], np.float64)); s = np.sqrt(np.mean(v * v))
                if v.max() > 12 * s or s < 2.0 ** 4: bad.append('%s of rank %d is uneven or too small' % (name, q))
    return bad

@@ -1,0 +1,486 @@
+from concourse.bass import DstId, RemoteDMATransfer
+from concourse.mybir import AluOpType as A, ActivationFunctionType as AF
+
+NR, F, NM, ROUNDS = 8, 512, 6, 3
+MAG = 12582912.0
+CEN = 1280.0
+PRE = 4
+ZERO_FIRST = False
+STRICT = True
+
+SCRATCH = {
+    "dx": ("dram", [8, 128, 64], "bfloat16"), "lx": ("dram", [8, 128, 64], "bfloat16"),
+    "dn": ("dram", [8, 128, 24], "int32"), "ln": ("dram", [8, 128, 24], "int32"),
+    "dm": ("dram", [128, 64], "bfloat16"), "lm": ("dram", [8, 128, 64], "bfloat16"),
+    "de": ("dram", [8, 128, 64], "float32"), "le": ("dram", [8, 128, 64], "float32"),
+    "dw": ("dram", [8, 128, 24], "float32"), "lw": ("dram", [8, 128, 24], "float32"),
+    "io1": ("sbuf", [128, 128], "int32"), "io2": ("sbuf", [128, 128], "int32"), "io3": ("sbuf", [128, 32], "float32"),
+    "tq": ("sbuf", [128, 128], "int32"), "tk": ("sbuf", [128, 8], "int32"), "col": ("sbuf", [128, 8], "float32"),
+    "b8": ("sbuf", [128, 8], "float32"), "jf": ("sbuf", [128, 128], "float32"),
+    "idh": ("sbuf", [128, 128], "float16"), "idn": ("sbuf", [128, 128], "float16"),
+    "idn8": ("sbuf", [128, 128], "float16"),
+    "id8": ("sbuf", [128, 128], "bfloat16"), "idm16": ("sbuf", [128, 128], "bfloat16"),
+    "idp": ("sbuf", [128, 128], "float16"), "selk": ("sbuf", [128, 1024], "float16"),
+    "idf": ("sbuf", [128, 128], "float32"), "idm": ("sbuf", [128, 128], "bfloat16"),
+    "ones": ("sbuf", [128, 512], "bfloat16"),
+    "zq": ("sbuf", [128, 144], "bfloat16"), "zero": ("sbuf", [128, 512], "float32"),
+    "win": ("sbuf", [128, 4096], "float32"),
+    "xb": ("sbuf", [128, 512], "bfloat16"), "x16": ("sbuf", [128, 512], "float16"),
+    "na": ("sbuf", [128, 512], "float32"),
+    "nbi": ("sbuf", [128, 192], "int32"), "t1": ("sbuf", [128, 192], "int32"), "t2": ("sbuf", [128, 192], "float32"),
+    "t3": ("sbuf", [128, 192], "float32"), "t4": ("sbuf", [128, 192], "float32"),
+    "wh": ("sbuf", [128, 384], "float16"), "wl": ("sbuf", [128, 192], "uint16"),
+    "wrep": ("sbuf", [128, 4096], "float16"),
+    "vv": ("sbuf", [128, 3072], "float32"), "uu": ("sbuf", [128, 3072], "float32"),
+    "net": ("sbuf", [128, 12 * 512], "float32"),
+    "near": ("sbuf", [128, 3072], "bfloat16"),
+    "ct": ("sbuf", [128, 192], "float32"), "cw": ("sbuf", [128, 192], "float32"),
+    "cj": ("sbuf", [128, 192], "int32"), "ci": ("sbuf", [128, 192], "int32"), "cl": ("sbuf", [128, 192], "uint16"),
+    "ch": ("sbuf", [128, 192], "float16"), "eq": ("sbuf", [128, 1632], "bfloat16"),
+    "mixc": ("sbuf", [128, 64], "bfloat16"),
+    "e0": ("sbuf", [128, 512], "float16"), "e1": ("sbuf", [128, 512], "float16"),
+    "lr0": ("sbuf", [128, 512], "float16"), "lr1": ("sbuf", [128, 512], "float16"),
+    "ra0": ("sbuf", [128, 512], "float16"), "ra1": ("sbuf", [128, 512], "float16"),
+    "ef": ("sbuf", [128, 512], "float32"), "sq": ("sbuf", [128, 512], "float32"),
+    "sg": ("sbuf", [128, 512], "float32"), "ydt": ("sbuf", [128, 512], "float32"),
+    "wf": ("sbuf", [128, 192], "float32"),
+}
+for _b in range(8):
+    SCRATCH["pb%d" % _b] = ("psum", [128, 512], "float32")
+SEMAPHORES = ["qv", "qa", "qp", "qg"] + ["s%d" % _i for _i in range(90)]
+
+
+def rank_program(g, core, T, topo):
+    r = T.rank_of(core)
+    if r is None:
+        return
+    cores = list(T.cores)
+    peers = [(r + d) % NR for d in range(1, NR)]
+    Q = {"v": g.vector, "a": g.scalar, "p": g.tensor, "g": g, "s": g.sync}
+    V, ACT, PE = g.vector, g.scalar, g.tensor
+    cnt = {"qv": 0, "qa": 0, "qp": 0, "qg": 0}
+    seen = {e: {} for e in Q}
+    wr, rd, nsem = {}, {}, [0]
+
+    def newsem():
+        nsem[0] += 1
+        cnt["s%d" % (nsem[0] - 1)] = 0
+        return "s%d" % (nsem[0] - 1)
+
+    def deps(e, R, W, dma):
+        need = {}
+
+        def add(tok, raw):
+            if tok[2] == e and not dma and (e == "p" or not (raw or STRICT)):
+                return
+            need[tok[0]] = max(need.get(tok[0], 0), tok[1])
+        for k in R:
+            for tok in wr.get(k, []):
+                add(tok, True)
+            if k[0] == "B":
+                for tok in rd.get(k, []):
+                    if tok[2] != e:
+                        add(tok, False)
+        for k in W:
+            for tok in wr.get(k, []) + rd.get(k, []):
+                add(tok, False)
+        for s, val in need.items():
+            if seen[e].get(s, 0) < val:
+                Q[e].wait_ge(T.sem[s], val)
+                seen[e][s] = val
+
+    def note(tok, R, W):
+        for k in R:
+            rd.setdefault(k, []).append(tok)
+        for k in W:
+            wr[k] = [tok]
+            rd[k] = []
+
+    def op(e, f, R, W, inc=True):
+        deps(e, R, W, False)
+        ins = f()
+        s = "q" + e
+        tok = (s, cnt[s] + 1, e)
+        if inc:
+            ins.then_inc(T.sem[s], 1)
+            cnt[s] += 1
+        note(tok, R, W)
+
+    def dma(e, out, in_, R, W, sem=None, total=16, **kw):
+        deps(e, R, W, True)
+        s = sem or newsem()
+        Q[e].dma_start(out, in_, **kw).then_inc(T.sem[s], 16)
+        cnt[s] += 16
+        note((s, total, "d"), R, W)
+
+    def send(src, dst, R, W):
+        deps("g", R, [], True)
+        rs, ls = newsem(), newsem()
+        tr = []
+        for i, k in enumerate(peers):
+            rid, pid, _ = topo.addr(cores[k])
+            eng = topo.engines(core, cores[k])
+            tr.append(RemoteDMATransfer(dst_ids=[DstId(rid=rid, pnc=pid)], dma_engine_mask=1 << eng[i],
+                                        remote_sem=T.sem[rs], src=src(k), dst=dst))
+        g.remote_dma_fused(tr, local_sem=T.sem[ls])
+        cnt[rs] = cnt[ls] = NR - 1
+        note((ls, NR - 1, "d"), R, [])
+        note((rs, NR - 1, "d"), [], W)
+
+    def ts(out, in0, s1, s2, o0, o1, R, W):
+        if s2 is None:
+            op("v", lambda: V.tensor_scalar(out, in0, s1, None, o0), R, W)
+        else:
+            op("v", lambda: V.tensor_scalar(out, in0, s1, s2, o0, o1), R, W)
+
+    def tt(out, in0, in1, o, R, W):
+        op("v", lambda: V.tensor_tensor(out, in0, in1, o), R, W)
+
+    def cp(out, in_, R, W):
+        op("v", lambda: V.tensor_copy(out, in_), R, W)
+
+    def act(out, in_, fn, R, W, bias=0.0, scale=1.0):
+        op("a", lambda: ACT.activation(out, in_, fn, bias=bias, scale=scale), R, W)
+
+    def mm(out, lhsT, rhs, start, stop, R, W, inc=False):
+        op("p", lambda: PE.matmul(out, lhsT, rhs, start, stop), R, W, inc)
+
+    def blk(t, j, w=F):
+        return t[:, j * w:(j + 1) * w]
+
+    def PB(b):
+        return T["pb%d" % b]
+
+    def BK(b):
+        return "B%d" % b
+
+    own = slice(16 * r, 16 * r + 16)
+
+    dma("s", T.dx[:], T.x[:], [], ["dx"])
+    dma("a", T.dn[:], T.nb[:], [], ["dn"])
+    dma("s", T.lx[r], T.x[own, :], [], ["lx0"])
+    dma("a", T.ln[r], T.nb[own, :], [], ["ln0"])
+    dma("s", T.dm[:], T.mix[:], [], ["dm"])
+    dma("a", T.lm[r], T.mix[:], [], ["lm0"])
+    op("g", lambda: g.iota(T.io1[:], [[-1, 128]], 0, 1), [], ["io1"])
+    op("g", lambda: g.iota(T.io2[:], [[-1, 16], [-16, 8]], 0, 1), [], ["io2"])
+    op("g", lambda: g.iota(T.io3[:], [[128, 32]], -2048, 0, allow_small_or_imprecise_dtypes=True), [], ["io3"])
+    send(lambda k: T.dx[k], T.lx[r], ["dx"], ["lx"])
+    send(lambda k: T.dn[k], T.ln[r], ["dn"], ["ln"])
+    send(lambda k: T.dm[:], T.lm[r], ["dm"], ["lm"])
+    dma("a", T.xb[:], T.lx[:], ["lx", "lx0"], ["xb"])
+    dma("s", T.nbi[:], T.ln[:], ["ln", "ln0"], ["nbi"])
+    dma("s", T.mixc[:], T.lm[:, r::8, :], ["lm", "lm0"], ["mixc"])
+
+    op("v", lambda: V.memset(T.zero[:], 0.0), [], ["zero"])
+    op("v", lambda: V.memset(T.zq[:], 0.0), [], ["zq"])
+    ts(T.tq[:], T.io1[:], 15, None, A.bitwise_and, None, ["io1"], ["tq"])
+    ts(T.tk[:], T.io1[:, 0::16], 4, None, A.arith_shift_right, None, ["io1"], ["tk"])
+    cp(blk(T.wrep, 0), T.zero[:], ["zero"], ["wrep0"])
+    ts(T.idh[:], T.io1[:], 0.0, None, A.is_equal, None, ["io1"], ["idh"])
+    for k in range(1, 8):
+        cp(T.wrep[:, 512 * k + 192:512 * k + 512], T.wrep[:, 192:512], ["wrep0"], ["wrep%d" % k])
+    ts(T.idn[:], T.io1[:], 0.0, -1.0, A.is_equal, A.mult, ["io1"], ["idn"])
+    ts(T.idn8[:], T.io1[:], 0.0, -0.125, A.is_equal, A.mult, ["io1"], ["idn8"])
+    ts(T.id8[:], T.io1[:], 0.0, 8.0, A.is_equal, A.mult, ["io1"], ["id8"])
+    ts(T.idm16[:], T.io1[:], 0.0, -16.0, A.is_equal, A.mult, ["io1"], ["idm16"])
+    ts(T.idp[:], T.io2[:], 0.0, 2.0 ** -13, A.is_equal, A.mult, ["io2"], ["idp"])
+    ts(T.idf[:], T.io1[:], 0.0, None, A.is_equal, None, ["io1"], ["idf"])
+    ts(T.idm[:], T.io1[:], 0.0, -MAG, A.is_equal, A.mult, ["io1"], ["idm"])
+    op("v", lambda: V.memset(T.ones[:], 1.0), [], ["ones"])
+    ts(T.jf[:], T.tq[:], 0.0, None, A.is_equal, None, ["tq"], ["jf"])
+    ts(T.b8[:], T.tk[:], 0.0, None, A.is_equal, None, ["tk"], ["b8"])
+    ts(T.col[:, 0:1], T.tq[:, 0:1], 8.0, None, A.mult, None, ["tq"], ["col0"])
+    cp(T.col[:, 1:2], T.tk[:, 0:1], ["tk"], ["col1"])
+    cp(T.zq[:, 15:128:16], T.b8[:], ["b8", "zq"], ["zq"])
+    for k in range(8):
+        ts(blk(T.selk, k, 128), T.jf[:], T.b8[:, k:k + 1], None, A.mult, None, ["jf", "b8"], ["selk%d" % k])
+    ts(T.wh[:, 192:224], T.io3[:], T.col[:, 0:1], T.col[:, 1:2], A.add, A.add, ["io3", "col0", "col1"], ["wF"])
+    SELK = ["selk%d" % k for k in range(8)]
+    WREP = ["wrep%d" % k for k in range(8)]
+    WIN = ["win%d" % m for m in range(8)]
+
+    def win_zero(b, first):
+        if ZERO_FIRST and first:
+            mm(PB(b)[:], T.wrep[:, 256:384], T.selk[:, 0:512], True, False, SELK + ["wrep0"], [BK(b)])
+        return first and not ZERO_FIRST
+
+    def win_n(m, b, first):
+        st = win_zero(b, first)
+        for i in range(4):
+            end = i == 3 and not first
+            mm(blk(PB(b), i, 128), T.wrep[:, 4 * m + i::32], T.idp[:], i == 0 and st, end,
+               WREP + ["idp"], [BK(b)], inc=end)
+
+    def win_x(m, b, first):
+        st = win_zero(b, first)
+        for k in range(8):
+            end = k == 7 and not first
+            mm(PB(b)[:, k::8], blk(T.selk, k, 128), blk(T.x16, m, 64), k == 0 and st, end,
+               ["x16"] + SELK, [BK(b)], inc=end)
+
+    def window(banks, pre, one, two):
+        for m in range(pre):
+            one(m, banks[m], True)
+        yield
+        for m in range(8):
+            b = banks[m % len(banks)]
+            if m >= pre:
+                one(m, b, True)
+            two(m, b, False)
+            if m % 2 == 0:
+                act(blk(T.win, m), PB(b)[:], AF.Copy, [BK(b)], ["win%d" % m])
+            else:
+                cp(blk(T.win, m), PB(b)[:], [BK(b)], ["win%d" % m])
+        yield
+
+    def spread_names():
+        for k in range(1, 8):
+            dst = T.wrep[:, 512 * k:512 * k + 192]
+            if k < 5:
+                cp(dst, T.wrep[:, 0:192], ["wrep0"], ["wrep%d" % k])
+            else:
+                act(dst, T.wrep[:, 0:192], AF.Copy, ["wrep0"], ["wrep%d" % k])
+
+    def name_list():
+        ts(T.t4[:], T.wrep[:, 0:192], 2048.0, None, A.add, None, ["wrep0"], ["t4"])
+        dma("s", T.wh[:, 0:192], T.wrep[:, 0:192], ["wrep0"], ["wh"])
+        dma("s", T.wh[:, 224:384], T.wrep[:, 0:160], ["wrep0"], ["wh2"])
+        ts(T.na[:], T.x16[:], -1.0, MAG, A.mult, A.add, ["x16"], ["na"])
+        cp(T.wl[:], T.t4[:], ["t4"], ["wl"])
+
+    def own_x(b, less):
+        mm(PB(b)[:], T.idh[:], T.x16[:], True, not less, ["idh", "x16"], [BK(b)], inc=not less)
+        if less:
+            mm(PB(b)[:], T.idm[:], T.ones[:], False, True, ["idm", "ones"], [BK(b)], inc=True)
+
+    aB, cB, D, Tb = 6, 7, [0, 1, 2], [3, 4, 5]
+    act(T.x16[:], T.xb[:], AF.Identity, ["xb"], ["x16"], scale=64.0)
+    w = window([0, 1, 2, 3, 4, 5, 7], 7, win_x, win_n)
+    next(w)
+    ts(T.t1[:], T.nbi[:], 9, None, A.arith_shift_right, None, ["nbi"], ["t1"])
+    ts(PB(aB)[:, 0:192], T.t1[:], -511.875, -256.0, A.mult, A.add, ["t1"], [BK(aB)])
+    tt(T.t3[:], T.nbi[:], PB(aB)[:, 0:192], A.add, [BK(aB), "nbi"], ["t3"])
+    ts(T.wrep[:, 0:192], T.t3[:], 8.0, None, A.mult, None, ["t3"], ["wrep0"])
+    spread_names()
+    name_list()
+    next(w)
+
+    for t in range(ROUNDS):
+        last = t == ROUNDS - 1
+        cen = 0.0 if t == 0 else CEN
+        aK, cK = BK(aB), BK(cB)
+        slot = {}
+
+        def S(name):
+            if name not in slot:
+                slot[name] = len(slot)
+            return blk(T.net, slot[name]), "n%d" % slot[name]
+
+        def P(b):
+            return PB(b)[:], BK(b)
+
+        def n2(o, a, b, fn):
+            tt(o[0], a[0], b[0], fn, [a[1], b[1]], [o[1]])
+
+        v = [(blk(T.vv, j), "v%d" % j) for j in range(NM)]
+        csem = [newsem(), newsem()]
+        AB = [D[1], D[2], Tb[2], D[1], D[0], D[2]]
+
+        def gather_v(j):
+            src = T.win[:, 0:4096].indirect(blk(T.wl, j, 32))
+            if j == 0:
+                cp(v[j][0], src, WIN + ["wl"], [v[j][1]])
+            else:
+                act(v[j][0], src, AF.Copy, WIN + ["wl"], [v[j][1]])
+            b = (j + t) % NM
+            for h in range(2):
+                dma("s", T.ct[:, 32 * j + 16 * h:32 * j + 16 * h + 16], T.vv[16 * h + b::32, j * F:(j + 1) * F],
+                    [v[j][1]], ["ct%d_%d" % (j, h)], sem=csem[j // 3], total=96)
+            if j in (3, 5):
+                mm(PB(D[j // 2])[:], T.idf[:], v[j][0], True, True, ["idf", v[j][1]], [BK(D[j // 2])], inc=True)
+
+        def sub_v(j):
+            tt(v[j][0], v[j][0], PB(aB)[:], A.subtract, [v[j][1], aK], [v[j][1]])
+
+        def sub_p(j):
+            mm(PB(AB[j])[:], T.idn[:], T.x16[:], True, False, ["idn", "x16"], [BK(AB[j])])
+            mm(PB(AB[j])[:], T.idm[:], T.ones[:], False, False, ["idm", "ones"], [BK(AB[j])])
+            mm(PB(AB[j])[:], T.idf[:], v[j][0], False, True, ["idf", v[j][1]], [BK(AB[j])], inc=True)
+
+        def abs_v(j):
+            if j in (3, 5):
+                act(PB(AB[j])[:], PB(AB[j])[:], AF.Abs, [BK(AB[j])], [BK(AB[j])], bias=MAG)
+            else:
+                act(PB(AB[j])[:], v[j][0], AF.Abs, [v[j][1]], [BK(AB[j])], bias=-MAG)
+
+        def chain(h, step):
+            c = slice(96 * h, 96 * h + 96)
+            if step == 0:
+                op("v", lambda: V.transpose(T.cw[:, c], T.ct[:, c]),
+                   ["ct%d_%d" % (j, i) for j in range(3 * h, 3 * h + 3) for i in range(2)], ["cw%d" % h])
+            elif step == 1:
+                ts(T.cj[:, c], T.cw[:, c], 8192.0, 2048.0, A.mult, A.add, ["cw%d" % h], ["cj%d" % h])
+            elif step == 2:
+                ts(T.ci[:, c], T.cj[:, c], 8191, None, A.bitwise_and, None, ["cj%d" % h], ["ci%d" % h])
+            else:
+                cp(T.cl[:, c], T.ci[:, c], ["ci%d" % h], ["cl%d" % h])
+
+        def gather_u(j):
+            act(blk(T.uu, j), T.win[:, 0:4096].indirect(blk(T.cl, j, 32)), AF.Copy,
+                WIN + ["cl%d" % (j // 3)], ["u%d" % j])
+            dma("g", blk(T.uu, j), T.na[:], ["na", "u%d" % j], ["u%d" % j], accum_op=A.add)
+
+        def abs_u(j):
+            act(blk(T.uu, j), blk(T.uu, j), AF.Abs, ["u%d" % j], ["u%d" % j], bias=-MAG)
+
+        def cmp(j):
+            tt(blk(T.near, j), blk(T.uu, j), PB(AB[j])[:], A.is_lt, ["u%d" % j, BK(AB[j])], ["near%d" % j])
+
+        def count(h):
+            for q in range(16):
+                mm(PB(cB)[:, 64 * h:64 * h + 64], T.zq[:, 15 - q:143 - q], T.near[:, 1024 * h + q:1024 * h + 1024:16],
+                   False, h == 0 and q == 15, ["zq", "near%d" % (2 * h), "near%d" % (2 * h + 1)], [cK], inc=(q == 15))
+
+        pairs = [[(192, T.ch[:], T.wh[:, 32 * i:32 * i + 192], 0) for i in (2 * c + 1, 2 * c + 2)] for c in range(3)]
+        pairs.append([(192 - 32 * d, T.ch[:, 0:192 - 32 * d], T.ch[:, 32 * d:192], 32 * d) for d in range(1, 6)])
+
+        def void_diff(c, b):
+            pos = 0
+            for i, (wd, lf, rt, _) in enumerate(pairs[c]):
+                end = i == len(pairs[c]) - 1
+                mm(PB(b)[:, pos:pos + wd], T.idh[:], lf, True, False, ["idh", "ch"], [BK(b)])
+                mm(PB(b)[:, pos:pos + wd], T.idn[:], rt, False, True, ["idn", "ch", "wh", "wh2", "wF"], [BK(b)], inc=end)
+                pos += wd
+            return pos
+
+        def void_eq(c, b, wd, e):
+            dst = T.eq[:, 384 * c:384 * c + wd]
+            if e == "v":
+                ts(dst, PB(b)[:, 0:wd], 0.0, None, A.is_equal, None, [BK(b)], ["eq%d" % c])
+            else:
+                act(PB(b)[:, 0:wd], PB(b)[:, 0:wd], AF.Abs, [BK(b)], [BK(b)])
+                act(dst, PB(b)[:, 0:wd], AF.Relu, [BK(b)], ["eq%d" % c], bias=1.0, scale=-1.0)
+
+        def void(c):
+            void_eq(c, D[0], void_diff(c, D[0]), "a")
+
+        def void_count():
+            for c in range(4):
+                pos = 384 * c
+                for i, (wd, _, _, c0) in enumerate(pairs[c]):
+                    mm(PB(cB)[:, c0:192], T.idm16[:], T.eq[:, pos:pos + wd], c == 0 and i == 0, False,
+                       ["eq%d" % c, "idm16"], [cK])
+                    pos += wd
+
+        T0, T1, T2, D0, D1, D2 = P(Tb[0]), P(Tb[1]), P(Tb[2]), P(D[0]), P(D[1]), P(D[2])
+        own_x(aB, False)
+        for j in range(NM):
+            gather_v(j)
+        n2(D0, v[0], P(aB), A.min)
+        n2(T0, v[0], P(aB), A.max)
+        own_x(aB, True)
+        n2(S("b3"), v[1], D0, A.max)
+        n2(T2, v[1], D0, A.min)
+        n2(T1, S("b3"), T0, A.min)
+        chain(0, 0); chain(0, 1); chain(0, 2); chain(0, 3)
+        gather_u(0); gather_u(1); gather_u(2)
+        n2(D0, v[1], T0, A.max)
+        n2(S("a1"), v[2], D1, A.min)
+        n2(T0, v[2], D1, A.max)
+        n2(S("c1"), S("a1"), T2, A.max)
+        sub_p(3)
+        chain(1, 0); chain(1, 1); chain(1, 2); chain(1, 3)
+        gather_u(3); gather_u(5); gather_u(4)
+        ts(T.ch[:], T.ci[:], -2048.0, None, A.add, None, ["ci0", "ci1"], ["ch"])
+        n2(S("a4"), v[4], D2, A.max)
+        n2(T2, S("a4"), D0, A.min)
+        n2(S("a2"), v[4], D2, A.min)
+        w0 = void_diff(0, D[0])
+        sub_p(5)
+        void_eq(0, D[0], w0, "a")
+        abs_v(3)
+        void(1); abs_v(5)
+        w2 = void_diff(2, D[0])
+        mm(PB(cB)[:, 192:384], T.idh[:], T.ch[:], True, False, ["idh", "ch"], [cK])
+        mm(PB(cB)[:, 192:384], T.idn[:], T.wh[:, 0:192], False, True, ["idn", "wh"], [cK])
+        abs_u(3); abs_u(5)
+        n2(S("c2"), S("a2"), T0, A.min)
+        n2(S("c6"), S("a2"), T0, A.max)
+        n2(S("f1"), S("c1"), T2, A.min)
+        n2(T0, S("c2"), T1, A.max)
+        n2(S("f4"), S("c1"), T2, A.max)
+        w3 = void_diff(3, Tb[2])
+        n2(T1, S("c6"), T0, A.min)
+        n2(T0, S("f1"), T1, A.max)
+        n2(S("fin"), S("f4"), T0, A.min)
+        et = T.ef if last else T["e%d" % t]
+        ts(et[:], S("fin")[0], MAG, -MAG, A.add, A.add, [S("fin")[1]], ["e"])
+        abs_u(2); abs_u(4)
+        if not last:
+            lr, ra = T["lr%d" % t], T["ra%d" % t]
+            send(lambda k: blk(et, k, 64), blk(lr, r, 64), ["e"], ["lr%d" % t])
+        else:
+            act(T.sq[:], T.ef[:], AF.Square, ["e"], ["sq"], bias=cen / 64.0, scale=1.0 / 64.0)
+            dma("s", T.de[:], T.sq[:], ["sq"], ["de"])
+            dma("s", T.le[r], T.sq[own, :], ["sq"], ["le0"])
+            send(lambda k: T.de[k], T.le[r], ["de"], ["le"])
+            dma("s", T.sg[:], T.le[:], ["le", "le0"], ["sg"])
+            dma("s", T.ye[:], T.le[:], ["le", "le0"], ["ye"])
+        sub_v(2)
+        void_eq(3, Tb[2], w3, "v")
+        abs_v(2)
+        void_eq(2, D[0], w2, "v")
+        void_count()
+        sub_v(4); abs_v(4)
+        cmp(3); sub_v(0); abs_u(0); abs_v(0)
+        cmp(2)
+        if not last:
+            sB, xB = BK(Tb[0]), BK(Tb[1])
+            mm(PB(Tb[1])[:], T.idh[:], et[:], True, False, ["idh", "e"], [xB])
+            mm(PB(Tb[0])[:, 0:64], T.id8[:], T.mixc[:], True, False, ["id8", "mixc"], [sB])
+            for k in range(8):
+                src = blk(et, r, 64) if k == r else blk(lr, k, 64)
+                mm(PB(Tb[0])[:, 0:64], T.idn8[:], src, False, k == 7, ["idn8", "e", "lr%d" % t], [sB], inc=(k == 7))
+        count(1)
+        sub_v(1)
+        if not last:
+            ts(blk(ra, r, 64), PB(Tb[0])[:, 0:64], 800.0 - cen, None, A.add, None, [sB], ["ro%d" % t])
+            send(lambda k: blk(ra, r, 64), blk(ra, r, 64), ["ro%d" % t], ["ra%d" % t])
+        cmp(5); abs_u(1); abs_v(1)
+        cmp(4)
+        count(2)
+        cmp(0); cmp(1)
+        count(0)
+        if not last:
+            mm(PB(Tb[1])[:], T.idh[:], ra[:], False, True, ["idh", "ra%d" % t, "ro%d" % t], [xB], inc=True)
+        dcw = PB(cB)[:, 192:384]
+        ts(T.t2[:], PB(cB)[:, 0:192], 7.5, None, A.is_ge, None, [cK], ["t2"])
+        tt(dcw, T.t2[:], dcw, A.mult, ["t2", cK], [cK])
+        if not last:
+            tt(T.wrep[:, 0:192], T.wh[:, 0:192], dcw, A.add, ["wh", cK], ["wrep0"])
+            spread_names()
+            w = window([Tb[0], Tb[2], aB, D[0], D[1], D[2], cB], PRE, win_n, win_x)
+            next(w)
+            ts(T.x16[:], PB(Tb[1])[:], cen - 800.0 - CEN, -CEN, A.add, A.max, [xB], ["x16"])
+            name_list()
+            next(w)
+            aB, Tb = Tb[1], [Tb[0], aB, Tb[2]]
+        else:
+            tt(T.t1[:], T.wh[:, 0:192], dcw, A.add, ["wh", cK], ["t1"])
+            ts(T.cj[:], T.t1[:], 7, None, A.bitwise_and, None, ["t1"], ["cj0", "cj1"])
+            ts(T.t4[:], T.t1[:], 0.125, 256.0, A.mult, A.add, ["t1"], ["t4"])
+            ts(dcw, T.cj[:], 511.875, None, A.mult, None, ["cj0", "cj1"], [cK])
+            tt(T.wf[:], T.t4[:], dcw, A.add, [cK, "t4"], ["wf"])
+            dma("a", T.dw[:], T.wf[:], ["wf"], ["dw"])
+            dma("a", T.lw[r], T.wf[own, :], ["wf"], ["lw0"])
+            yB = BK(Tb[0])
+            mm(PB(Tb[0])[0:16, :], T.jf[:, 0:16], T.sg[:], True, True, ["jf", "sg"], [yB], inc=True)
+            cp(T.ydt[0:16, :], PB(Tb[0])[0:16, :], [yB], ["ydt"])
+            dma("s", T.yd[:], T.ydt[0:16, :], ["ydt"], ["yd"])
+            send(lambda k: T.dw[k], T.lw[r], ["dw"], ["lw"])
+            dma("s", T.yn[:], T.lw[:], ["lw", "lw0"], ["yn"])
+
+    for s, val in cnt.items():
+        if val:
+            g.sync.wait_ge(T.sem[s], val)

@@ -4,7 +4,8 @@ from concourse.mybir import AluOpType as A, ActivationFunctionType as AF
 NR, F, NM, ROUNDS = 8, 512, 6, 3
 MAG = 12582912.0
 CEN = 1280.0
-PRE = 4
+PRE = 7
+MID = 0
 ZERO_FIRST = False
 STRICT = True
 
@@ -12,7 +13,7 @@ SCRATCH = {
     "dx": ("dram", [8, 128, 64], "bfloat16"), "lx": ("dram", [8, 128, 64], "bfloat16"),
     "dn": ("dram", [8, 128, 24], "int32"), "ln": ("dram", [8, 128, 24], "int32"),
     "dm": ("dram", [128, 64], "bfloat16"), "lm": ("dram", [8, 128, 64], "bfloat16"),
-    "de": ("dram", [8, 128, 64], "float32"), "le": ("dram", [8, 128, 64], "float32"),
+    "de": ("dram", [8, 128, 64], "float16"), "le": ("dram", [8, 128, 64], "float16"),
     "dw": ("dram", [8, 128, 24], "float32"), "lw": ("dram", [8, 128, 24], "float32"),
     "io1": ("sbuf", [128, 128], "int32"), "io2": ("sbuf", [128, 128], "int32"), "io3": ("sbuf", [128, 32], "float32"),
     "tq": ("sbuf", [128, 128], "int32"), "tk": ("sbuf", [128, 8], "int32"), "col": ("sbuf", [128, 8], "float32"),
@@ -22,6 +23,9 @@ SCRATCH = {
     "id8": ("sbuf", [128, 128], "bfloat16"), "idm16": ("sbuf", [128, 128], "bfloat16"),
     "idp": ("sbuf", [128, 128], "float16"), "selk": ("sbuf", [128, 1024], "float16"),
     "idf": ("sbuf", [128, 128], "float32"), "idm": ("sbuf", [128, 128], "bfloat16"),
+    "ip5": ("sbuf", [128, 128], "float16"), "in5": ("sbuf", [128, 128], "float16"),
+    "ip4": ("sbuf", [128, 128], "float32"), "in4": ("sbuf", [128, 128], "float32"),
+    "fl": ("sbuf", [128, 384], "float32"),
     "ones": ("sbuf", [128, 512], "bfloat16"),
     "zq": ("sbuf", [128, 144], "bfloat16"), "zero": ("sbuf", [128, 512], "float32"),
     "win": ("sbuf", [128, 4096], "float32"),
@@ -33,6 +37,8 @@ SCRATCH = {
     "wrep": ("sbuf", [128, 4096], "float16"),
     "vv": ("sbuf", [128, 3072], "float32"), "uu": ("sbuf", [128, 3072], "float32"),
     "net": ("sbuf", [128, 12 * 512], "float32"),
+    "sa": ("sbuf", [128, 1536], "float32"), "sb": ("sbuf", [128, 1536], "float32"),
+    "so": ("sbuf", [128, 1536], "float32"),
     "near": ("sbuf", [128, 3072], "bfloat16"),
     "ct": ("sbuf", [128, 192], "float32"), "cw": ("sbuf", [128, 192], "float32"),
     "cj": ("sbuf", [128, 192], "int32"), "ci": ("sbuf", [128, 192], "int32"), "cl": ("sbuf", [128, 192], "uint16"),
@@ -41,8 +47,8 @@ SCRATCH = {
     "e0": ("sbuf", [128, 512], "float16"), "e1": ("sbuf", [128, 512], "float16"),
     "lr0": ("sbuf", [128, 512], "float16"), "lr1": ("sbuf", [128, 512], "float16"),
     "ra0": ("sbuf", [128, 512], "float16"), "ra1": ("sbuf", [128, 512], "float16"),
-    "ef": ("sbuf", [128, 512], "float32"), "sq": ("sbuf", [128, 512], "float32"),
-    "sg": ("sbuf", [128, 512], "float32"), "ydt": ("sbuf", [128, 512], "float32"),
+    "e2": ("sbuf", [128, 512], "float16"), "sq": ("sbuf", [128, 512], "float32"),
+    "sg": ("sbuf", [128, 512], "float16"), "ydt": ("sbuf", [128, 512], "float32"),
     "wf": ("sbuf", [128, 192], "float32"),
 }
 for _b in range(8):
@@ -196,6 +202,9 @@ def rank_program(g, core, T, topo):
     for k in range(8):
         ts(blk(T.selk, k, 128), T.jf[:], T.b8[:, k:k + 1], None, A.mult, None, ["jf", "b8"], ["selk%d" % k])
     ts(T.wh[:, 192:224], T.io3[:], T.col[:, 0:1], T.col[:, 1:2], A.add, A.add, ["io3", "col0", "col1"], ["wF"])
+    for nm, val in (("ip5", 512.0), ("in5", -512.0), ("ip4", 4095.0), ("in4", -4095.0)):
+        ts(T[nm][:], T.io1[:], 0.0, val, A.is_equal, A.mult, ["io1"], [nm])
+    op("v", lambda: V.memset(T.sa[:, 0::3], 8192.0), [], ["big"])
     SELK = ["selk%d" % k for k in range(8)]
     WREP = ["wrep%d" % k for k in range(8)]
     WIN = ["win%d" % m for m in range(8)]
@@ -221,6 +230,8 @@ def rank_program(g, core, T, topo):
 
     def window(banks, pre, one, two):
         for m in range(pre):
+            if m == MID:
+                yield
             one(m, banks[m], True)
         yield
         for m in range(8):
@@ -246,22 +257,20 @@ def rank_program(g, core, T, topo):
         ts(T.t4[:], T.wrep[:, 0:192], 2048.0, None, A.add, None, ["wrep0"], ["t4"])
         dma("s", T.wh[:, 0:192], T.wrep[:, 0:192], ["wrep0"], ["wh"])
         dma("s", T.wh[:, 224:384], T.wrep[:, 0:160], ["wrep0"], ["wh2"])
-        ts(T.na[:], T.x16[:], -1.0, MAG, A.mult, A.add, ["x16"], ["na"])
         cp(T.wl[:], T.t4[:], ["t4"], ["wl"])
 
-    def own_x(b, less):
-        mm(PB(b)[:], T.idh[:], T.x16[:], True, not less, ["idh", "x16"], [BK(b)], inc=not less)
-        if less:
-            mm(PB(b)[:], T.idm[:], T.ones[:], False, True, ["idm", "ones"], [BK(b)], inc=True)
+    def minus_x():
+        ts(T.na[:], T.x16[:], -1.0, MAG, A.mult, A.add, ["x16"], ["na"])
 
     aB, cB, D, Tb = 6, 7, [0, 1, 2], [3, 4, 5]
     act(T.x16[:], T.xb[:], AF.Identity, ["xb"], ["x16"], scale=64.0)
     w = window([0, 1, 2, 3, 4, 5, 7], 7, win_x, win_n)
-    next(w)
+    next(w); next(w)
+    minus_x()
     ts(T.t1[:], T.nbi[:], 9, None, A.arith_shift_right, None, ["nbi"], ["t1"])
-    ts(PB(aB)[:, 0:192], T.t1[:], -511.875, -256.0, A.mult, A.add, ["t1"], [BK(aB)])
-    tt(T.t3[:], T.nbi[:], PB(aB)[:, 0:192], A.add, [BK(aB), "nbi"], ["t3"])
-    ts(T.wrep[:, 0:192], T.t3[:], 8.0, None, A.mult, None, ["t3"], ["wrep0"])
+    ts(T.t3[:], T.nbi[:], 8.0, -2048.0, A.mult, A.add, ["nbi"], ["t3"])
+    ts(PB(aB)[:, 0:192], T.t1[:], -4095.0, None, A.mult, None, ["t1"], [BK(aB)])
+    tt(T.wrep[:, 0:192], T.t3[:], PB(aB)[:, 0:192], A.add, [BK(aB), "t3"], ["wrep0"])
     spread_names()
     name_list()
     next(w)
@@ -285,7 +294,7 @@ def rank_program(g, core, T, topo):
 
         v = [(blk(T.vv, j), "v%d" % j) for j in range(NM)]
         csem = [newsem(), newsem()]
-        AB = [D[1], D[2], Tb[2], D[1], D[0], D[2]]
+        AB = [cB, D[1], Tb[2], D[1], D[0], D[2]]
 
         def gather_v(j):
             src = T.win[:, 0:4096].indirect(blk(T.wl, j, 32))
@@ -297,11 +306,10 @@ def rank_program(g, core, T, topo):
             for h in range(2):
                 dma("s", T.ct[:, 32 * j + 16 * h:32 * j + 16 * h + 16], T.vv[16 * h + b::32, j * F:(j + 1) * F],
                     [v[j][1]], ["ct%d_%d" % (j, h)], sem=csem[j // 3], total=96)
+            if j == 0:
+                sub_p(0)
             if j in (3, 5):
                 mm(PB(D[j // 2])[:], T.idf[:], v[j][0], True, True, ["idf", v[j][1]], [BK(D[j // 2])], inc=True)
-
-        def sub_v(j):
-            tt(v[j][0], v[j][0], PB(aB)[:], A.subtract, [v[j][1], aK], [v[j][1]])
 
         def sub_p(j):
             mm(PB(AB[j])[:], T.idn[:], T.x16[:], True, False, ["idn", "x16"], [BK(AB[j])])
@@ -309,10 +317,13 @@ def rank_program(g, core, T, topo):
             mm(PB(AB[j])[:], T.idf[:], v[j][0], False, True, ["idf", v[j][1]], [BK(AB[j])], inc=True)
 
         def abs_v(j):
-            if j in (3, 5):
+            if j in (0, 3, 5):
                 act(PB(AB[j])[:], PB(AB[j])[:], AF.Abs, [BK(AB[j])], [BK(AB[j])], bias=MAG)
             else:
                 act(PB(AB[j])[:], v[j][0], AF.Abs, [v[j][1]], [BK(AB[j])], bias=-MAG)
+
+        def sub_v(j):
+            tt(v[j][0], v[j][0], PB(aB)[:], A.subtract, [v[j][1], aK], [v[j][1]])
 
         def chain(h, step):
             c = slice(96 * h, 96 * h + 96)
@@ -374,15 +385,16 @@ def rank_program(g, core, T, topo):
                     pos += wd
 
         T0, T1, T2, D0, D1, D2 = P(Tb[0]), P(Tb[1]), P(Tb[2]), P(D[0]), P(D[1]), P(D[2])
-        own_x(aB, False)
+        mm(PB(aB)[:], T.idh[:], T.x16[:], True, True, ["idh", "x16"], [aK], inc=True)
         for j in range(NM):
             gather_v(j)
         n2(D0, v[0], P(aB), A.min)
         n2(T0, v[0], P(aB), A.max)
-        own_x(aB, True)
+        mm(PB(aB)[:], T.idh[:], T.x16[:], True, False, ["idh", "x16"], [aK])
+        mm(PB(aB)[:], T.idm[:], T.ones[:], False, True, ["idm", "ones"], [aK], inc=True)
         n2(S("b3"), v[1], D0, A.max)
         n2(T2, v[1], D0, A.min)
-        n2(T1, S("b3"), T0, A.min)
+        n2((T.sb[:, 0::3], "c3"), S("b3"), T0, A.min)
         chain(0, 0); chain(0, 1); chain(0, 2); chain(0, 3)
         gather_u(0); gather_u(1); gather_u(2)
         n2(D0, v[1], T0, A.max)
@@ -393,92 +405,100 @@ def rank_program(g, core, T, topo):
         chain(1, 0); chain(1, 1); chain(1, 2); chain(1, 3)
         gather_u(3); gather_u(5); gather_u(4)
         ts(T.ch[:], T.ci[:], -2048.0, None, A.add, None, ["ci0", "ci1"], ["ch"])
+        w0 = void_diff(0, Tb[1])
         n2(S("a4"), v[4], D2, A.max)
-        n2(T2, S("a4"), D0, A.min)
         n2(S("a2"), v[4], D2, A.min)
-        w0 = void_diff(0, D[0])
+        n2(T2, S("a4"), D0, A.min)
+        w1 = void_diff(1, D[0])
         sub_p(5)
-        void_eq(0, D[0], w0, "a")
+        void_eq(0, Tb[1], w0, "a")
         abs_v(3)
-        void(1); abs_v(5)
-        w2 = void_diff(2, D[0])
-        mm(PB(cB)[:, 192:384], T.idh[:], T.ch[:], True, False, ["idh", "ch"], [cK])
-        mm(PB(cB)[:, 192:384], T.idn[:], T.wh[:, 0:192], False, True, ["idn", "wh"], [cK])
-        abs_u(3); abs_u(5)
-        n2(S("c2"), S("a2"), T0, A.min)
-        n2(S("c6"), S("a2"), T0, A.max)
-        n2(S("f1"), S("c1"), T2, A.min)
-        n2(T0, S("c2"), T1, A.max)
-        n2(S("f4"), S("c1"), T2, A.max)
-        w3 = void_diff(3, Tb[2])
-        n2(T1, S("c6"), T0, A.min)
-        n2(T0, S("f1"), T1, A.max)
-        n2(S("fin"), S("f4"), T0, A.min)
-        et = T.ef if last else T["e%d" % t]
-        ts(et[:], S("fin")[0], MAG, -MAG, A.add, A.add, [S("fin")[1]], ["e"])
-        abs_u(2); abs_u(4)
+        w2 = void_diff(2, Tb[1])
+        abs_v(0); abs_u(0); abs_v(5); abs_u(2); abs_u(3)
+        if last:
+            act(T.fl[:, 0:192], T.wh[:, 0:192], AF.Identity, ["wh"], ["fl0"], bias=255.5625, scale=0.125)
+            act(T.fl[:, 192:384], T.ch[:], AF.Identity, ["ch"], ["fl1"], bias=255.5625, scale=0.125)
+            act(T.fl[:], T.fl[:], AF.Identity, ["fl0", "fl1"], ["fl0", "fl1"], bias=MAG)
+            act(T.fl[:], T.fl[:], AF.Identity, ["fl0", "fl1"], ["fl0", "fl1"], bias=-MAG)
+        n2((T.sa[:, 1::3], "c2"), S("a2"), T0, A.min)
+        n2((T.sb[:, 1::3], "c6"), S("a2"), T0, A.max)
+        w3 = void_diff(3, Tb[0])
+        n2((T.sa[:, 2::3], "f1"), S("c1"), T2, A.min)
+        n2((T.sb[:, 2::3], "f4"), S("c1"), T2, A.max)
+        op("v", lambda: V.tensor_tensor_scan(T.so[:], T.sa[:], T.sb[:], 0.0, A.max, A.min),
+           ["big", "c2", "c3", "c6", "f1", "f4"], ["so"])
+        et = T["e%d" % t]
+        ts(et[:], T.so[:, 2::3], MAG, -MAG, A.add, A.add, ["so"], ["e"])
         if not last:
             lr, ra = T["lr%d" % t], T["ra%d" % t]
             send(lambda k: blk(et, k, 64), blk(lr, r, 64), ["e"], ["lr%d" % t])
         else:
-            act(T.sq[:], T.ef[:], AF.Square, ["e"], ["sq"], bias=cen / 64.0, scale=1.0 / 64.0)
-            dma("s", T.de[:], T.sq[:], ["sq"], ["de"])
-            dma("s", T.le[r], T.sq[own, :], ["sq"], ["le0"])
+            dma("s", T.de[:], et[:], ["e"], ["de"])
+            dma("s", T.le[r], et[own, :], ["e"], ["le0"])
             send(lambda k: T.de[k], T.le[r], ["de"], ["le"])
             dma("s", T.sg[:], T.le[:], ["le", "le0"], ["sg"])
-            dma("s", T.ye[:], T.le[:], ["le", "le0"], ["ye"])
-        sub_v(2)
-        void_eq(3, Tb[2], w3, "v")
-        abs_v(2)
-        void_eq(2, D[0], w2, "v")
-        void_count()
-        sub_v(4); abs_v(4)
-        cmp(3); sub_v(0); abs_u(0); abs_v(0)
-        cmp(2)
+        dB, dcw = cK, PB(cB)[:, 192:384]
+        sub_v(2); abs_v(2); abs_u(5)
+        cmp(0)
         if not last:
+            mm(dcw, T.idh[:], T.ch[:], True, False, ["idh", "ch"], [cK])
+            mm(dcw, T.idn[:], T.wh[:, 0:192], False, True, ["idn", "wh"], [cK])
+        void_eq(1, D[0], w1, "v")
+        sub_v(4); abs_v(4); abs_u(4)
+        void_eq(3, Tb[0], w3, "v")
+        void_eq(2, Tb[1], w2, "v")
+        void_count()
+        cmp(3); sub_v(1); abs_u(1); abs_v(1)
+        if last:
+            dB, dcw, wn = BK(Tb[1]), PB(Tb[1])[:, 0:192], PB(Tb[0])[:, 0:192]
+            mm(wn, T.ip5[:], T.wh[:, 0:192], True, False, ["ip5", "wh"], [BK(Tb[0])])
+            mm(wn, T.in4[:], T.fl[:, 0:192], False, True, ["in4", "fl0"], [BK(Tb[0])], inc=True)
+            act(T.t4[:], wn, AF.Identity, [BK(Tb[0])], ["t4"], bias=512.0 * 2048.0)
+            mm(dcw, T.ip5[:], T.ch[:], True, False, ["ip5", "ch"], [dB])
+            mm(dcw, T.in5[:], T.wh[:, 0:192], False, False, ["in5", "wh"], [dB])
+            mm(dcw, T.in4[:], T.fl[:, 192:384], False, False, ["in4", "fl1"], [dB])
+            mm(dcw, T.ip4[:], T.fl[:, 0:192], False, True, ["ip4", "fl0"], [dB], inc=True)
+        else:
             sB, xB = BK(Tb[0]), BK(Tb[1])
-            mm(PB(Tb[1])[:], T.idh[:], et[:], True, False, ["idh", "e"], [xB])
             mm(PB(Tb[0])[:, 0:64], T.id8[:], T.mixc[:], True, False, ["id8", "mixc"], [sB])
             for k in range(8):
                 src = blk(et, r, 64) if k == r else blk(lr, k, 64)
                 mm(PB(Tb[0])[:, 0:64], T.idn8[:], src, False, k == 7, ["idn8", "e", "lr%d" % t], [sB], inc=(k == 7))
-        count(1)
-        sub_v(1)
+            mm(PB(Tb[1])[:], T.idh[:], et[:], True, False, ["idh", "e"], [xB])
+        cmp(2)
         if not last:
             ts(blk(ra, r, 64), PB(Tb[0])[:, 0:64], 800.0 - cen, None, A.add, None, [sB], ["ro%d" % t])
             send(lambda k: blk(ra, r, 64), blk(ra, r, 64), ["ro%d" % t], ["ra%d" % t])
-        cmp(5); abs_u(1); abs_v(1)
-        cmp(4)
+        count(1)
+        cmp(5); cmp(4)
         count(2)
-        cmp(0); cmp(1)
+        cmp(1)
         count(0)
-        if not last:
-            mm(PB(Tb[1])[:], T.idh[:], ra[:], False, True, ["idh", "ra%d" % t, "ro%d" % t], [xB], inc=True)
-        dcw = PB(cB)[:, 192:384]
         ts(T.t2[:], PB(cB)[:, 0:192], 7.5, None, A.is_ge, None, [cK], ["t2"])
-        tt(dcw, T.t2[:], dcw, A.mult, ["t2", cK], [cK])
+        tt(dcw, T.t2[:], dcw, A.mult, ["t2", dB], [dB])
         if not last:
-            tt(T.wrep[:, 0:192], T.wh[:, 0:192], dcw, A.add, ["wh", cK], ["wrep0"])
+            tt(T.wrep[:, 0:192], T.wh[:, 0:192], dcw, A.add, ["wh", dB], ["wrep0"])
             spread_names()
-            w = window([Tb[0], Tb[2], aB, D[0], D[1], D[2], cB], PRE, win_n, win_x)
+            w = window([D[0], Tb[2], Tb[0], aB, D[1], D[2], cB], PRE, win_n, win_x)
+            next(w)
+            name_list()
+            mm(PB(Tb[1])[:], T.idh[:], ra[:], False, True, ["idh", "ra%d" % t, "ro%d" % t], [xB], inc=True)
             next(w)
             ts(T.x16[:], PB(Tb[1])[:], cen - 800.0 - CEN, -CEN, A.add, A.max, [xB], ["x16"])
-            name_list()
+            minus_x()
             next(w)
             aB, Tb = Tb[1], [Tb[0], aB, Tb[2]]
         else:
-            tt(T.t1[:], T.wh[:, 0:192], dcw, A.add, ["wh", cK], ["t1"])
-            ts(T.cj[:], T.t1[:], 7, None, A.bitwise_and, None, ["t1"], ["cj0", "cj1"])
-            ts(T.t4[:], T.t1[:], 0.125, 256.0, A.mult, A.add, ["t1"], ["t4"])
-            ts(dcw, T.cj[:], 511.875, None, A.mult, None, ["cj0", "cj1"], [cK])
-            tt(T.wf[:], T.t4[:], dcw, A.add, [cK, "t4"], ["wf"])
+            tt(T.wf[:], T.t4[:], dcw, A.add, [dB, "t4"], ["wf"])
             dma("a", T.dw[:], T.wf[:], ["wf"], ["dw"])
             dma("a", T.lw[r], T.wf[own, :], ["wf"], ["lw0"])
-            yB = BK(Tb[0])
-            mm(PB(Tb[0])[0:16, :], T.jf[:, 0:16], T.sg[:], True, True, ["jf", "sg"], [yB], inc=True)
-            cp(T.ydt[0:16, :], PB(Tb[0])[0:16, :], [yB], ["ydt"])
-            dma("s", T.yd[:], T.ydt[0:16, :], ["ydt"], ["yd"])
             send(lambda k: T.dw[k], T.lw[r], ["dw"], ["lw"])
+            yB = BK(Tb[0])
+            act(T.sq[:], T.sg[:], AF.Square, ["sg"], ["sq"], bias=cen / 64.0, scale=1.0 / 64.0)
+            dma("a", T.ye[:], T.sq[:], ["sq"], ["ye"])
+            mm(PB(Tb[0])[0:16, :], T.jf[:, 0:16], T.sq[:], True, True, ["jf", "sq"], [yB], inc=True)
+            cp(T.ydt[0:16, :], PB(Tb[0])[0:16, :], [yB], ["ydt"])
+            dma("a", T.yd[:], T.ydt[0:16, :], ["ydt"], ["yd"])
             dma("s", T.yn[:], T.lw[:], ["lw", "lw0"], ["yn"])
 
     for s, val in cnt.items():

@@ -4,41 +4,47 @@ from concourse.mybir import AluOpType as A, ActivationFunctionType as AF
 NR, F, NM, ROUNDS = 8, 512, 6, 3
 MAG = 12582912.0
 CEN = 1280.0
-PRE = 7
-MID = 0
-ZERO_FIRST = False
+BIG = 8192.0
+HEAD = "G0v G1a G2v G3a C0g C1v C3a C2v SV0 SV1 T1g T2g G4a C4a G5a C5a L1 L2 H0 AV0 AV1 SV2 SV3 U0a U1a SU0 L3 U2a SU1 L4 E "
+PLAN = HEAD + ("SU2 AV2 SV4 AV3 SV5 NA H1 CH AU0 U3v DC VD05 K0 AV4 SUM AU1 AV5 Ra VD10 VD21 U4v VE0v K1 VD35 AU2 AU3 "
+               "U5v VE1v VC0 K2 N0 VE3a VE2v AU4 XP0 VC1 VC2 K3 AU5 N1 VC3 XP1 K4 X K5 N2 W0 W1 W2 W3 NN W4 W5 W6 W7 WO")
+LAST = HEAD + ("SU2 AV2 SV4 AV3 SV5 NA H1 CH AU0 U3v VD05 K0 AV4 AU1 AV5 FL VD10 VD21 U4v VE0v K1 VD36 AU2 AU3 "
+               "U5v VE1v VC0 K2 N0 VE3a VE2v DC AU4 VC1 VC2 K3 AU5 ON N1 VC3 K4 K5 N2 NN SQ")
 STRICT = True
 
 SCRATCH = {
-    "dx": ("dram", [8, 128, 64], "bfloat16"), "lx": ("dram", [8, 128, 64], "bfloat16"),
+    "dx": ("dram", [8, 128, 64], "bfloat16"),
     "dn": ("dram", [8, 128, 24], "int32"), "ln": ("dram", [8, 128, 24], "int32"),
     "dm": ("dram", [128, 64], "bfloat16"), "lm": ("dram", [8, 128, 64], "bfloat16"),
-    "de": ("dram", [8, 128, 64], "float16"), "le": ("dram", [8, 128, 64], "float16"),
+    "de": ("dram", [8, 128, 64], "float16"),
     "dw": ("dram", [8, 128, 24], "float32"), "lw": ("dram", [8, 128, 24], "float32"),
     "io1": ("sbuf", [128, 128], "int32"), "io2": ("sbuf", [128, 128], "int32"), "io3": ("sbuf", [128, 32], "float32"),
+    "io4": ("sbuf", [128, 128], "int32"),
     "tq": ("sbuf", [128, 128], "int32"), "tk": ("sbuf", [128, 8], "int32"), "col": ("sbuf", [128, 8], "float32"),
     "b8": ("sbuf", [128, 8], "float32"), "jf": ("sbuf", [128, 128], "float32"),
     "idh": ("sbuf", [128, 128], "float16"), "idn": ("sbuf", [128, 128], "float16"),
-    "idn8": ("sbuf", [128, 128], "float16"),
+    "idh8": ("sbuf", [128, 128], "float16"), "id1": ("sbuf", [128, 128], "bfloat16"),
     "id8": ("sbuf", [128, 128], "bfloat16"), "idm16": ("sbuf", [128, 128], "bfloat16"),
     "idp": ("sbuf", [128, 128], "float16"), "selk": ("sbuf", [128, 1024], "float16"),
+    "selw": ("sbuf", [128, 1024], "bfloat16"),
     "idf": ("sbuf", [128, 128], "float32"), "idm": ("sbuf", [128, 128], "bfloat16"),
     "ip5": ("sbuf", [128, 128], "float16"), "in5": ("sbuf", [128, 128], "float16"),
     "ip4": ("sbuf", [128, 128], "float32"), "in4": ("sbuf", [128, 128], "float32"),
     "fl": ("sbuf", [128, 384], "float32"),
     "ones": ("sbuf", [128, 512], "bfloat16"),
     "zq": ("sbuf", [128, 144], "bfloat16"), "zero": ("sbuf", [128, 512], "float32"),
+    "cst": ("sbuf", [128, 2560], "float16"),
     "win": ("sbuf", [128, 4096], "float32"),
-    "xb": ("sbuf", [128, 512], "bfloat16"), "x16": ("sbuf", [128, 512], "float16"),
-    "na": ("sbuf", [128, 512], "float32"),
+    "xl": ("sbuf", [128, 512], "bfloat16"), "xb": ("sbuf", [128, 512], "bfloat16"),
     "nbi": ("sbuf", [128, 192], "int32"), "t1": ("sbuf", [128, 192], "int32"), "t2": ("sbuf", [128, 192], "float32"),
     "t3": ("sbuf", [128, 192], "float32"), "t4": ("sbuf", [128, 192], "float32"),
     "wh": ("sbuf", [128, 384], "float16"), "wl": ("sbuf", [128, 192], "uint16"),
     "wrep": ("sbuf", [128, 4096], "float16"),
-    "vv": ("sbuf", [128, 3072], "float32"), "uu": ("sbuf", [128, 3072], "float32"),
-    "net": ("sbuf", [128, 12 * 512], "float32"),
-    "sa": ("sbuf", [128, 1536], "float32"), "sb": ("sbuf", [128, 1536], "float32"),
-    "so": ("sbuf", [128, 1536], "float32"),
+    "vv": ("sbuf", [128, 3072], "float32"), "uu": ("sbuf", [128, 3072], "float16"),
+    "bv": ("sbuf", [128, 3072], "float32"), "uw": ("sbuf", [128, 3072], "float32"),
+    "na": ("sbuf", [128, 512], "float32"),
+    "pv": ("sbuf", [128, 2560], "float16"), "qv": ("sbuf", [128, 2568], "float16"),
+    "m1": ("sbuf", [128, 2568], "float16"), "m2": ("sbuf", [128, 2560], "float16"),
     "near": ("sbuf", [128, 3072], "bfloat16"),
     "ct": ("sbuf", [128, 192], "float32"), "cw": ("sbuf", [128, 192], "float32"),
     "cj": ("sbuf", [128, 192], "int32"), "ci": ("sbuf", [128, 192], "int32"), "cl": ("sbuf", [128, 192], "uint16"),
@@ -48,12 +54,12 @@ SCRATCH = {
     "lr0": ("sbuf", [128, 512], "float16"), "lr1": ("sbuf", [128, 512], "float16"),
     "ra0": ("sbuf", [128, 512], "float16"), "ra1": ("sbuf", [128, 512], "float16"),
     "e2": ("sbuf", [128, 512], "float16"), "sq": ("sbuf", [128, 512], "float32"),
-    "sg": ("sbuf", [128, 512], "float16"), "ydt": ("sbuf", [128, 512], "float32"),
+    "sg": ("sbuf", [128, 512], "float16"), "ydt": ("sbuf", [128, 64], "float32"),
     "wf": ("sbuf", [128, 192], "float32"),
 }
 for _b in range(8):
     SCRATCH["pb%d" % _b] = ("psum", [128, 512], "float32")
-SEMAPHORES = ["qv", "qa", "qp", "qg"] + ["s%d" % _i for _i in range(90)]
+SEMAPHORES = ["qv", "qa", "qp", "qg"] + ["s%d" % _i for _i in range(100)]
 
 
 def rank_program(g, core, T, topo):
@@ -162,20 +168,23 @@ def rank_program(g, core, T, topo):
 
     own = slice(16 * r, 16 * r + 16)
 
-    dma("s", T.dx[:], T.x[:], [], ["dx"])
-    dma("a", T.dn[:], T.nb[:], [], ["dn"])
-    dma("s", T.lx[r], T.x[own, :], [], ["lx0"])
-    dma("a", T.ln[r], T.nb[own, :], [], ["ln0"])
+    dma("s", T.dn[:], T.nb[:], [], ["dn"])
+    dma("a", T.dx[:], T.x[:], [], ["dx"])
+    dma("s", T.ln[r], T.nb[own, :], [], ["ln0"])
+    dma("a", blk(T.xl, r, 64), T.x[own, :], [], ["xl0"])
     dma("s", T.dm[:], T.mix[:], [], ["dm"])
     dma("a", T.lm[r], T.mix[:], [], ["lm0"])
     op("g", lambda: g.iota(T.io1[:], [[-1, 128]], 0, 1), [], ["io1"])
+    op("g", lambda: g.iota(T.io4[:], [[0, 8], [-8, 16]], 0, 1), [], ["io4"])
     op("g", lambda: g.iota(T.io2[:], [[-1, 16], [-16, 8]], 0, 1), [], ["io2"])
     op("g", lambda: g.iota(T.io3[:], [[128, 32]], -2048, 0, allow_small_or_imprecise_dtypes=True), [], ["io3"])
-    send(lambda k: T.dx[k], T.lx[r], ["dx"], ["lx"])
     send(lambda k: T.dn[k], T.ln[r], ["dn"], ["ln"])
+    send(lambda k: T.dx[k], blk(T.xl, r, 64), ["dx"], ["xl"])
     send(lambda k: T.dm[:], T.lm[r], ["dm"], ["lm"])
-    dma("a", T.xb[:], T.lx[:], ["lx", "lx0"], ["xb"])
     dma("s", T.nbi[:], T.ln[:], ["ln", "ln0"], ["nbi"])
+    xs = newsem()
+    for k in range(8):
+        dma("s", T.xb[16 * k:16 * k + 16, :], blk(T.xl, k, 64), ["xl", "xl0"], ["xb%d" % k], sem=xs, total=128)
     dma("s", T.mixc[:], T.lm[:, r::8, :], ["lm", "lm0"], ["mixc"])
 
     op("v", lambda: V.memset(T.zero[:], 0.0), [], ["zero"])
@@ -185,14 +194,13 @@ def rank_program(g, core, T, topo):
     cp(blk(T.wrep, 0), T.zero[:], ["zero"], ["wrep0"])
     ts(T.idh[:], T.io1[:], 0.0, None, A.is_equal, None, ["io1"], ["idh"])
     for k in range(1, 8):
-        cp(T.wrep[:, 512 * k + 192:512 * k + 512], T.wrep[:, 192:512], ["wrep0"], ["wrep%d" % k])
-    ts(T.idn[:], T.io1[:], 0.0, -1.0, A.is_equal, A.mult, ["io1"], ["idn"])
-    ts(T.idn8[:], T.io1[:], 0.0, -0.125, A.is_equal, A.mult, ["io1"], ["idn8"])
-    ts(T.id8[:], T.io1[:], 0.0, 8.0, A.is_equal, A.mult, ["io1"], ["id8"])
-    ts(T.idm16[:], T.io1[:], 0.0, -16.0, A.is_equal, A.mult, ["io1"], ["idm16"])
+        act(T.wrep[:, 512 * k + 192:512 * k + 512], T.wrep[:, 192:512], AF.Copy, ["wrep0"], ["wrep%d" % k])
+    for k in range(8):
+        ts(blk(T.selw, k, 128), T.io4[:], float(k), None, A.is_equal, None, ["io4"], ["selw%d" % k])
+    for nm, val in (("idn", -1.0), ("idh8", 8.0), ("id1", 1.0), ("id8", 8.0), ("idm16", -16.0), ("idf", 1.0),
+                    ("idm", -MAG), ("ip5", 512.0), ("in5", -512.0), ("ip4", 4095.0), ("in4", -4095.0)):
+        ts(T[nm][:], T.io1[:], 0.0, val, A.is_equal, A.mult, ["io1"], [nm])
     ts(T.idp[:], T.io2[:], 0.0, 2.0 ** -13, A.is_equal, A.mult, ["io2"], ["idp"])
-    ts(T.idf[:], T.io1[:], 0.0, None, A.is_equal, None, ["io1"], ["idf"])
-    ts(T.idm[:], T.io1[:], 0.0, -MAG, A.is_equal, A.mult, ["io1"], ["idm"])
     op("v", lambda: V.memset(T.ones[:], 1.0), [], ["ones"])
     ts(T.jf[:], T.tq[:], 0.0, None, A.is_equal, None, ["tq"], ["jf"])
     ts(T.b8[:], T.tk[:], 0.0, None, A.is_equal, None, ["tk"], ["b8"])
@@ -202,103 +210,93 @@ def rank_program(g, core, T, topo):
     for k in range(8):
         ts(blk(T.selk, k, 128), T.jf[:], T.b8[:, k:k + 1], None, A.mult, None, ["jf", "b8"], ["selk%d" % k])
     ts(T.wh[:, 192:224], T.io3[:], T.col[:, 0:1], T.col[:, 1:2], A.add, A.add, ["io3", "col0", "col1"], ["wF"])
-    for nm, val in (("ip5", 512.0), ("in5", -512.0), ("ip4", 4095.0), ("in4", -4095.0)):
-        ts(T[nm][:], T.io1[:], 0.0, val, A.is_equal, A.mult, ["io1"], [nm])
-    op("v", lambda: V.memset(T.sa[:, 0::3], 8192.0), [], ["big"])
+    for i in range(5):
+        act(T.cst[:, i::5], T.zero[:], AF.Identity, ["zero"], ["cst%d" % i], bias=BIG if i < 4 else -BIG)
+    act(T.m1[:, 0:8], T.zero[:, 0:8], AF.Identity, ["zero"], ["m1"], bias=-BIG)
+    act(T.qv[:, 0:1], T.zero[:, 0:1], AF.Copy, ["zero"], ["qpad"])
+    CST = ["cst%d" % k for k in range(5)]
+    pv = [(T.pv[:, i::5], "p%d" % i) for i in range(5)]
+    qv = [(T.qv[:, 1 + i:2561:5], "q%d" % i) for i in range(5)]
+    home = [pv[0], pv[1], pv[3], pv[4], qv[3], qv[4]]
+    xa = pv[2]
+
+    def twin(i, e):
+        if e == "g":
+            op("g", lambda: g.affine_select(qv[i][0], pv[i + 2][0], [[0, F]], A.is_ge, 0.0, 0, 0), [pv[i + 2][1]], [qv[i][1]])
+        elif e == "v":
+            cp(qv[i][0], pv[i + 2][0], [pv[i + 2][1]], [qv[i][1]])
+        else:
+            act(qv[i][0], pv[i + 2][0], AF.Copy, [pv[i + 2][1]], [qv[i][1]])
     SELK = ["selk%d" % k for k in range(8)]
+    SELW = ["selw%d" % k for k in range(8)]
     WREP = ["wrep%d" % k for k in range(8)]
     WIN = ["win%d" % m for m in range(8)]
 
-    def win_zero(b, first):
-        if ZERO_FIRST and first:
-            mm(PB(b)[:], T.wrep[:, 256:384], T.selk[:, 0:512], True, False, SELK + ["wrep0"], [BK(b)])
-        return first and not ZERO_FIRST
-
-    def win_n(m, b, first):
-        st = win_zero(b, first)
+    def win_n(m, b):
         for i in range(4):
-            end = i == 3 and not first
-            mm(blk(PB(b), i, 128), T.wrep[:, 4 * m + i::32], T.idp[:], i == 0 and st, end,
-               WREP + ["idp"], [BK(b)], inc=end)
+            mm(blk(PB(b), i, 128), T.wrep[:, 4 * m + i::32], T.idp[:], False, i == 3, WREP + ["idp"], [BK(b)], inc=i == 3)
 
-    def win_x(m, b, first):
-        st = win_zero(b, first)
+    def win_x(m, b):
         for k in range(8):
-            end = k == 7 and not first
-            mm(PB(b)[:, k::8], blk(T.selk, k, 128), blk(T.x16, m, 64), k == 0 and st, end,
-               ["x16"] + SELK, [BK(b)], inc=end)
+            mm(PB(b)[:, k::8], blk(T.selk, k, 128), T.pv[:, 320 * m + 2:320 * m + 320:5], k == 0, False, ["p2"] + SELK, [BK(b)])
 
-    def window(banks, pre, one, two):
-        for m in range(pre):
-            if m == MID:
-                yield
-            one(m, banks[m], True)
-        yield
+    def win_x0(m, b):
+        for k in range(8):
+            mm(PB(b)[:, k::8], blk(T.selw, m, 128), blk(T.xl, k, 64), k == 0, False, ["xl", "xl0"] + SELW, [BK(b)])
+
+    def win_out(banks, add):
         for m in range(8):
-            b = banks[m % len(banks)]
-            if m >= pre:
-                one(m, b, True)
-            two(m, b, False)
+            b = banks[m]
+            win_n(m, b)
             if m % 2 == 0:
-                act(blk(T.win, m), PB(b)[:], AF.Copy, [BK(b)], ["win%d" % m])
+                act(blk(T.win, m), PB(b)[:], AF.Identity, [BK(b)], ["win%d" % m], bias=add)
             else:
-                cp(blk(T.win, m), PB(b)[:], [BK(b)], ["win%d" % m])
-        yield
+                ts(blk(T.win, m), PB(b)[:], add, None, A.add, None, [BK(b)], ["win%d" % m])
 
     def spread_names():
         for k in range(1, 8):
             dst = T.wrep[:, 512 * k:512 * k + 192]
-            if k < 5:
+            if k < 6:
                 cp(dst, T.wrep[:, 0:192], ["wrep0"], ["wrep%d" % k])
             else:
                 act(dst, T.wrep[:, 0:192], AF.Copy, ["wrep0"], ["wrep%d" % k])
 
     def name_list():
-        ts(T.t4[:], T.wrep[:, 0:192], 2048.0, None, A.add, None, ["wrep0"], ["t4"])
+        ts(T.wl[:], T.wrep[:, 0:192], 2048.0, None, A.add, None, ["wrep0"], ["wl"])
         dma("s", T.wh[:, 0:192], T.wrep[:, 0:192], ["wrep0"], ["wh"])
         dma("s", T.wh[:, 224:384], T.wrep[:, 0:160], ["wrep0"], ["wh2"])
-        cp(T.wl[:], T.t4[:], ["t4"], ["wl"])
 
-    def minus_x():
-        ts(T.na[:], T.x16[:], -1.0, MAG, A.mult, A.add, ["x16"], ["na"])
-
-    aB, cB, D, Tb = 6, 7, [0, 1, 2], [3, 4, 5]
-    act(T.x16[:], T.xb[:], AF.Identity, ["xb"], ["x16"], scale=64.0)
-    w = window([0, 1, 2, 3, 4, 5, 7], 7, win_x, win_n)
-    next(w); next(w)
-    minus_x()
+    D, U, xB, sB, cB = [0, 1], [2, 3, 4], 5, 6, 7
+    for m in range(8):
+        win_x0(m, m)
     ts(T.t1[:], T.nbi[:], 9, None, A.arith_shift_right, None, ["nbi"], ["t1"])
     ts(T.t3[:], T.nbi[:], 8.0, -2048.0, A.mult, A.add, ["nbi"], ["t3"])
-    ts(PB(aB)[:, 0:192], T.t1[:], -4095.0, None, A.mult, None, ["t1"], [BK(aB)])
-    tt(T.wrep[:, 0:192], T.t3[:], PB(aB)[:, 0:192], A.add, [BK(aB), "t3"], ["wrep0"])
+    ts(T.t2[:], T.t1[:], -4095.0, None, A.mult, None, ["t1"], ["t2"])
+    tt(T.wrep[:, 0:192], T.t3[:], T.t2[:], A.add, ["t2", "t3"], ["wrep0"])
     spread_names()
     name_list()
-    next(w)
+    win_out(list(range(8)), CEN)
+    ts(xa[0], T.xb[:], CEN, None, A.add, None, ["xb%d" % k for k in range(8)], [xa[1]])
+    twin(0, "g")
+
+    def minus_x():
+        act(T.na[:], xa[0], AF.Identity, [xa[1]], ["na"], bias=MAG, scale=-1.0)
+
+    late = [minus_x]
 
     for t in range(ROUNDS):
         last = t == ROUNDS - 1
-        cen = 0.0 if t == 0 else CEN
-        aK, cK = BK(aB), BK(cB)
-        slot = {}
-
-        def S(name):
-            if name not in slot:
-                slot[name] = len(slot)
-            return blk(T.net, slot[name]), "n%d" % slot[name]
-
-        def P(b):
-            return PB(b)[:], BK(b)
-
-        def n2(o, a, b, fn):
-            tt(o[0], a[0], b[0], fn, [a[1], b[1]], [o[1]])
-
+        cK = BK(cB)
         v = [(blk(T.vv, j), "v%d" % j) for j in range(NM)]
         csem = [newsem(), newsem()]
-        AB = [cB, D[1], Tb[2], D[1], D[0], D[2]]
+        rough = set()
+        plan = (LAST if last else PLAN).split()
+        et = T["e%d" % t]
+        lr, ra = T["lr%d" % min(t, 1)], T["ra%d" % min(t, 1)]
 
-        def gather_v(j):
+        def gather_v(j, e):
             src = T.win[:, 0:4096].indirect(blk(T.wl, j, 32))
-            if j == 0:
+            if e == "v":
                 cp(v[j][0], src, WIN + ["wl"], [v[j][1]])
             else:
                 act(v[j][0], src, AF.Copy, WIN + ["wl"], [v[j][1]])
@@ -306,66 +304,101 @@ def rank_program(g, core, T, topo):
             for h in range(2):
                 dma("s", T.ct[:, 32 * j + 16 * h:32 * j + 16 * h + 16], T.vv[16 * h + b::32, j * F:(j + 1) * F],
                     [v[j][1]], ["ct%d_%d" % (j, h)], sem=csem[j // 3], total=96)
-            if j == 0:
-                sub_p(0)
-            if j in (3, 5):
-                mm(PB(D[j // 2])[:], T.idf[:], v[j][0], True, True, ["idf", v[j][1]], [BK(D[j // 2])], inc=True)
 
-        def sub_p(j):
-            mm(PB(AB[j])[:], T.idn[:], T.x16[:], True, False, ["idn", "x16"], [BK(AB[j])])
-            mm(PB(AB[j])[:], T.idm[:], T.ones[:], False, False, ["idm", "ones"], [BK(AB[j])])
-            mm(PB(AB[j])[:], T.idf[:], v[j][0], False, True, ["idf", v[j][1]], [BK(AB[j])], inc=True)
-
-        def abs_v(j):
-            if j in (0, 3, 5):
-                act(PB(AB[j])[:], PB(AB[j])[:], AF.Abs, [BK(AB[j])], [BK(AB[j])], bias=MAG)
+        def narrow(out, src, R, key, e):
+            if e != "v":
+                if e == "a":
+                    act(out, src, AF.Copy, R, [key])
+                else:
+                    op("g", lambda: g.affine_select(out, src, [[0, F]], A.is_ge, 0.0, 0, 0), R, [key])
+                if last:
+                    rough.add(key)
+            elif last:
+                ts(out, src, MAG, -MAG, A.add, A.add, R, [key])
             else:
-                act(PB(AB[j])[:], v[j][0], AF.Abs, [v[j][1]], [BK(AB[j])], bias=-MAG)
+                cp(out, src, R, [key])
+
+        def conv(j, e):
+            narrow(home[j][0], v[j][0], [v[j][1]], home[j][1], e)
+
+        def gather_u(j, e):
+            src, R = T.win[:, 0:4096].indirect(blk(T.cl, j, 32)), WIN + ["cl%d" % (j // 3)]
+            if e == "v":
+                tt(blk(T.uw, j), src, T.na[:], A.add, R + ["na"], ["u%d" % j])
+                wide.add(j)
+            else:
+                narrow(blk(T.uu, j), src, R, "u%d" % j, e)
+
+        def less_a(b, src, key):
+            if key in rough:
+                mm(PB(b)[:], T.idm[:], T.ones[:], True, False, ["idm", "ones"], [BK(b)])
+            mm(PB(b)[:], T.idh[:], src, key not in rough, False, ["idh", key], [BK(b)])
+            mm(PB(b)[:], T.idn[:], xa[0], False, True, ["idn", xa[1]], [BK(b)], inc=True)
+            return MAG if key in rough else 0.0
+
+        back_u, back_v, wide = {}, {}, set()
 
         def sub_v(j):
-            tt(v[j][0], v[j][0], PB(aB)[:], A.subtract, [v[j][1], aK], [v[j][1]])
+            back_v[j] = less_a(D[j % 2], *home[j])
 
-        def chain(h, step):
-            c = slice(96 * h, 96 * h + 96)
-            if step == 0:
-                op("v", lambda: V.transpose(T.cw[:, c], T.ct[:, c]),
-                   ["ct%d_%d" % (j, i) for j in range(3 * h, 3 * h + 3) for i in range(2)], ["cw%d" % h])
-            elif step == 1:
-                ts(T.cj[:, c], T.cw[:, c], 8192.0, 2048.0, A.mult, A.add, ["cw%d" % h], ["cj%d" % h])
-            elif step == 2:
-                ts(T.ci[:, c], T.cj[:, c], 8191, None, A.bitwise_and, None, ["cj%d" % h], ["ci%d" % h])
-            else:
-                cp(T.cl[:, c], T.ci[:, c], ["ci%d" % h], ["cl%d" % h])
+        def abs_v(j):
+            b = D[j % 2]
+            act(blk(T.bv, j), PB(b)[:], AF.Abs, [BK(b)], ["bv%d" % j], bias=back_v[j])
 
-        def gather_u(j):
-            act(blk(T.uu, j), T.win[:, 0:4096].indirect(blk(T.cl, j, 32)), AF.Copy,
-                WIN + ["cl%d" % (j // 3)], ["u%d" % j])
-            dma("g", blk(T.uu, j), T.na[:], ["na", "u%d" % j], ["u%d" % j], accum_op=A.add)
+        def sub_u(j):
+            back_u[j] = less_a(U[j % 3], blk(T.uu, j), "u%d" % j)
 
         def abs_u(j):
-            act(blk(T.uu, j), blk(T.uu, j), AF.Abs, ["u%d" % j], ["u%d" % j], bias=-MAG)
+            b = U[j % 3]
+            if j in wide:
+                act(PB(b)[:], blk(T.uw, j), AF.Abs, ["u%d" % j], [BK(b)], bias=-MAG)
+            else:
+                act(PB(b)[:], PB(b)[:], AF.Abs, [BK(b)], [BK(b)], bias=back_u[j])
 
         def cmp(j):
-            tt(blk(T.near, j), blk(T.uu, j), PB(AB[j])[:], A.is_lt, ["u%d" % j, BK(AB[j])], ["near%d" % j])
+            b = U[j % 3]
+            tt(blk(T.near, j), blk(T.bv, j), PB(b)[:], A.is_gt, ["bv%d" % j, BK(b)], ["near%d" % j])
+
+        def level(k):
+            n = 5 * F
+            out, d0, d1, R, W = [
+                (T.m1[:, 1:n + 1], T.pv[:], T.cst[:], CST, "m1"), (T.m2[:], T.pv[:], T.m1[:, 0:n], ["m1"], "m2"),
+                (T.m1[:, 0:n], T.qv[:, 0:n], T.m2[:], ["m2", "qpad"], "m1"),
+                (T.m2[:], T.qv[:, 1:n + 1], T.m1[:, 0:n], ["m1"], "m2")][k - 1]
+            op("v", lambda: V.tensor_tensor_scan(out, d0, d1, -BIG, A.max, A.min),
+               R + [p[1] for p in (pv if k < 3 else qv)], [W])
+
+        def chain(h):
+            c = slice(96 * h, 96 * h + 96)
+            op("v", lambda: V.transpose(T.cw[:, c], T.ct[:, c]),
+               ["ct%d_%d" % (j, i) for j in range(3 * h, 3 * h + 3) for i in range(2)], ["cw%d" % h])
+            ts(T.cj[:, c], T.cw[:, c], 8192.0, 2048.0, A.mult, A.add, ["cw%d" % h], ["cj%d" % h])
+            ts(T.ci[:, c], T.cj[:, c], 8191, None, A.bitwise_and, None, ["cj%d" % h], ["ci%d" % h])
+            cp(T.cl[:, c], T.ci[:, c], ["ci%d" % h], ["cl%d" % h])
+
+        sums = [w for w in plan if w[:2] in ("N0", "N1", "N2", "VC")]
 
         def count(h):
+            w = "N%d" % h
             for q in range(16):
                 mm(PB(cB)[:, 64 * h:64 * h + 64], T.zq[:, 15 - q:143 - q], T.near[:, 1024 * h + q:1024 * h + 1024:16],
-                   False, h == 0 and q == 15, ["zq", "near%d" % (2 * h), "near%d" % (2 * h + 1)], [cK], inc=(q == 15))
+                   w == sums[0] and q == 0, w == sums[-1] and q == 15,
+                   ["zq", "near%d" % (2 * h), "near%d" % (2 * h + 1)], [cK], inc=(q == 15))
 
         pairs = [[(192, T.ch[:], T.wh[:, 32 * i:32 * i + 192], 0) for i in (2 * c + 1, 2 * c + 2)] for c in range(3)]
         pairs.append([(192 - 32 * d, T.ch[:, 0:192 - 32 * d], T.ch[:, 32 * d:192], 32 * d) for d in range(1, 6)])
+        VB = {}
 
         def void_diff(c, b):
-            pos = 0
+            pos, VB[c] = 0, b
             for i, (wd, lf, rt, _) in enumerate(pairs[c]):
                 end = i == len(pairs[c]) - 1
                 mm(PB(b)[:, pos:pos + wd], T.idh[:], lf, True, False, ["idh", "ch"], [BK(b)])
                 mm(PB(b)[:, pos:pos + wd], T.idn[:], rt, False, True, ["idn", "ch", "wh", "wh2", "wF"], [BK(b)], inc=end)
                 pos += wd
-            return pos
 
-        def void_eq(c, b, wd, e):
+        def void_eq(c, e):
+            b, wd = VB[c], sum(p[0] for p in pairs[c])
             dst = T.eq[:, 384 * c:384 * c + wd]
             if e == "v":
                 ts(dst, PB(b)[:, 0:wd], 0.0, None, A.is_equal, None, [BK(b)], ["eq%d" % c])
@@ -373,133 +406,105 @@ def rank_program(g, core, T, topo):
                 act(PB(b)[:, 0:wd], PB(b)[:, 0:wd], AF.Abs, [BK(b)], [BK(b)])
                 act(dst, PB(b)[:, 0:wd], AF.Relu, [BK(b)], ["eq%d" % c], bias=1.0, scale=-1.0)
 
-        def void(c):
-            void_eq(c, D[0], void_diff(c, D[0]), "a")
+        def void_count(c):
+            pos, w = 384 * c, "VC%d" % c
+            for i, (wd, _, _, c0) in enumerate(pairs[c]):
+                end = i == len(pairs[c]) - 1
+                mm(PB(cB)[:, c0:192], T.idm16[:], T.eq[:, pos:pos + wd], w == sums[0] and i == 0, w == sums[-1] and end,
+                   ["eq%d" % c, "idm16"], [cK], inc=end)
+                pos += wd
 
-        def void_count():
-            for c in range(4):
-                pos = 384 * c
-                for i, (wd, _, _, c0) in enumerate(pairs[c]):
-                    mm(PB(cB)[:, c0:192], T.idm16[:], T.eq[:, pos:pos + wd], c == 0 and i == 0, False,
-                       ["eq%d" % c, "idm16"], [cK])
-                    pos += wd
+        def median_out():
+            ts(et[:], T.m2[:, 4::5], MAG, -MAG, A.add, A.add, ["m2"], ["e"])
+            if not last:
+                send(lambda k: blk(et, k, 64), blk(lr, r, 64), ["e"], ["lr%d" % t])
+            else:
+                dma("s", T.de[:], et[:], ["e"], ["de"])
+                dma("s", blk(T.sg, r, 64), et[own, :], ["e"], ["sg0"])
+                send(lambda k: T.de[k], blk(T.sg, r, 64), ["de"], ["sg"])
 
-        T0, T1, T2, D0, D1, D2 = P(Tb[0]), P(Tb[1]), P(Tb[2]), P(D[0]), P(D[1]), P(D[2])
-        mm(PB(aB)[:], T.idh[:], T.x16[:], True, True, ["idh", "x16"], [aK], inc=True)
-        for j in range(NM):
-            gather_v(j)
-        n2(D0, v[0], P(aB), A.min)
-        n2(T0, v[0], P(aB), A.max)
-        mm(PB(aB)[:], T.idh[:], T.x16[:], True, False, ["idh", "x16"], [aK])
-        mm(PB(aB)[:], T.idm[:], T.ones[:], False, True, ["idm", "ones"], [aK], inc=True)
-        n2(S("b3"), v[1], D0, A.max)
-        n2(T2, v[1], D0, A.min)
-        n2((T.sb[:, 0::3], "c3"), S("b3"), T0, A.min)
-        chain(0, 0); chain(0, 1); chain(0, 2); chain(0, 3)
-        gather_u(0); gather_u(1); gather_u(2)
-        n2(D0, v[1], T0, A.max)
-        n2(S("a1"), v[2], D1, A.min)
-        n2(T0, v[2], D1, A.max)
-        n2(S("c1"), S("a1"), T2, A.max)
-        sub_p(3)
-        chain(1, 0); chain(1, 1); chain(1, 2); chain(1, 3)
-        gather_u(3); gather_u(5); gather_u(4)
-        ts(T.ch[:], T.ci[:], -2048.0, None, A.add, None, ["ci0", "ci1"], ["ch"])
-        w0 = void_diff(0, Tb[1])
-        n2(S("a4"), v[4], D2, A.max)
-        n2(S("a2"), v[4], D2, A.min)
-        n2(T2, S("a4"), D0, A.min)
-        w1 = void_diff(1, D[0])
-        sub_p(5)
-        void_eq(0, Tb[1], w0, "a")
-        abs_v(3)
-        w2 = void_diff(2, Tb[1])
-        abs_v(0); abs_u(0); abs_v(5); abs_u(2); abs_u(3)
-        if last:
+        def challengers():
+            ts(T.ch[:], T.ci[:], -2048.0, None, A.add, None, ["ci0", "ci1"], ["ch"])
+
+        dB, dcw, wn = (BK(xB), PB(xB)[:, 0:192], PB(sB)[:, 0:192]) if last else (cK, PB(cB)[:, 192:384], None)
+
+        def eighths():
             act(T.fl[:, 0:192], T.wh[:, 0:192], AF.Identity, ["wh"], ["fl0"], bias=255.5625, scale=0.125)
             act(T.fl[:, 192:384], T.ch[:], AF.Identity, ["ch"], ["fl1"], bias=255.5625, scale=0.125)
-            act(T.fl[:], T.fl[:], AF.Identity, ["fl0", "fl1"], ["fl0", "fl1"], bias=MAG)
-            act(T.fl[:], T.fl[:], AF.Identity, ["fl0", "fl1"], ["fl0", "fl1"], bias=-MAG)
-        n2((T.sa[:, 1::3], "c2"), S("a2"), T0, A.min)
-        n2((T.sb[:, 1::3], "c6"), S("a2"), T0, A.max)
-        w3 = void_diff(3, Tb[0])
-        n2((T.sa[:, 2::3], "f1"), S("c1"), T2, A.min)
-        n2((T.sb[:, 2::3], "f4"), S("c1"), T2, A.max)
-        op("v", lambda: V.tensor_tensor_scan(T.so[:], T.sa[:], T.sb[:], 0.0, A.max, A.min),
-           ["big", "c2", "c3", "c6", "f1", "f4"], ["so"])
-        et = T["e%d" % t]
-        ts(et[:], T.so[:, 2::3], MAG, -MAG, A.add, A.add, ["so"], ["e"])
-        if not last:
-            lr, ra = T["lr%d" % t], T["ra%d" % t]
-            send(lambda k: blk(et, k, 64), blk(lr, r, 64), ["e"], ["lr%d" % t])
-        else:
-            dma("s", T.de[:], et[:], ["e"], ["de"])
-            dma("s", T.le[r], et[own, :], ["e"], ["le0"])
-            send(lambda k: T.de[k], T.le[r], ["de"], ["le"])
-            dma("s", T.sg[:], T.le[:], ["le", "le0"], ["sg"])
-        dB, dcw = cK, PB(cB)[:, 192:384]
-        sub_v(2); abs_v(2); abs_u(5)
-        cmp(0)
-        if not last:
-            mm(dcw, T.idh[:], T.ch[:], True, False, ["idh", "ch"], [cK])
-            mm(dcw, T.idn[:], T.wh[:, 0:192], False, True, ["idn", "wh"], [cK])
-        void_eq(1, D[0], w1, "v")
-        sub_v(4); abs_v(4); abs_u(4)
-        void_eq(3, Tb[0], w3, "v")
-        void_eq(2, Tb[1], w2, "v")
-        void_count()
-        cmp(3); sub_v(1); abs_u(1); abs_v(1)
-        if last:
-            dB, dcw, wn = BK(Tb[1]), PB(Tb[1])[:, 0:192], PB(Tb[0])[:, 0:192]
-            mm(wn, T.ip5[:], T.wh[:, 0:192], True, False, ["ip5", "wh"], [BK(Tb[0])])
-            mm(wn, T.in4[:], T.fl[:, 0:192], False, True, ["in4", "fl0"], [BK(Tb[0])], inc=True)
-            act(T.t4[:], wn, AF.Identity, [BK(Tb[0])], ["t4"], bias=512.0 * 2048.0)
+
+        def change():
+            if not last:
+                mm(dcw, T.idh[:], T.ch[:], True, False, ["idh", "ch"], [dB])
+                mm(dcw, T.idn[:], T.wh[:, 0:192], False, True, ["idn", "wh"], [dB])
+                return
+            ts(T.fl[:], T.fl[:], MAG, -MAG, A.add, A.add, ["fl0", "fl1"], ["fl0", "fl1"])
+            mm(wn, T.ip5[:], T.wh[:, 0:192], True, False, ["ip5", "wh"], [BK(sB)])
+            mm(wn, T.in4[:], T.fl[:, 0:192], False, True, ["in4", "fl0"], [BK(sB)], inc=True)
             mm(dcw, T.ip5[:], T.ch[:], True, False, ["ip5", "ch"], [dB])
             mm(dcw, T.in5[:], T.wh[:, 0:192], False, False, ["in5", "wh"], [dB])
             mm(dcw, T.in4[:], T.fl[:, 192:384], False, False, ["in4", "fl1"], [dB])
             mm(dcw, T.ip4[:], T.fl[:, 0:192], False, True, ["ip4", "fl0"], [dB], inc=True)
-        else:
-            sB, xB = BK(Tb[0]), BK(Tb[1])
-            mm(PB(Tb[0])[:, 0:64], T.id8[:], T.mixc[:], True, False, ["id8", "mixc"], [sB])
+
+        def old_names():
+            act(T.t4[:], wn, AF.Identity, [BK(sB)], ["t4"], bias=512.0 * 2048.0)
+
+        def sum_e():
+            mm(PB(sB)[:, 0:64], (T.id1 if t == 0 else T.id8)[:], T.mixc[:], True, False, ["id1", "id8", "mixc"], [BK(sB)])
             for k in range(8):
                 src = blk(et, r, 64) if k == r else blk(lr, k, 64)
-                mm(PB(Tb[0])[:, 0:64], T.idn8[:], src, False, k == 7, ["idn8", "e", "lr%d" % t], [sB], inc=(k == 7))
-            mm(PB(Tb[1])[:], T.idh[:], et[:], True, False, ["idh", "e"], [xB])
-        cmp(2)
-        if not last:
-            ts(blk(ra, r, 64), PB(Tb[0])[:, 0:64], 800.0 - cen, None, A.add, None, [sB], ["ro%d" % t])
+                mm(PB(sB)[:, 0:64], T.idn[:], src, False, k == 7, ["idn", "e", "lr%d" % t], [BK(sB)], inc=(k == 7))
+
+        def rest(e):
+            if e == "a":
+                act(blk(ra, r, 64), PB(sB)[:, 0:64], AF.Identity, [BK(sB)], ["ro%d" % t], bias=8 * CEN)
+            else:
+                ts(blk(ra, r, 64), PB(sB)[:, 0:64], 8 * CEN, None, A.add, None, [BK(sB)], ["ro%d" % t])
             send(lambda k: blk(ra, r, 64), blk(ra, r, 64), ["ro%d" % t], ["ra%d" % t])
-        count(1)
-        cmp(5); cmp(4)
-        count(2)
-        cmp(1)
-        count(0)
-        ts(T.t2[:], PB(cB)[:, 0:192], 7.5, None, A.is_ge, None, [cK], ["t2"])
-        tt(dcw, T.t2[:], dcw, A.mult, ["t2", dB], [dB])
-        if not last:
-            tt(T.wrep[:, 0:192], T.wh[:, 0:192], dcw, A.add, ["wh", dB], ["wrep0"])
-            spread_names()
-            w = window([D[0], Tb[2], Tb[0], aB, D[1], D[2], cB], PRE, win_n, win_x)
-            next(w)
-            name_list()
-            mm(PB(Tb[1])[:], T.idh[:], ra[:], False, True, ["idh", "ra%d" % t, "ro%d" % t], [xB], inc=True)
-            next(w)
-            ts(T.x16[:], PB(Tb[1])[:], cen - 800.0 - CEN, -CEN, A.add, A.max, [xB], ["x16"])
-            minus_x()
-            next(w)
-            aB, Tb = Tb[1], [Tb[0], aB, Tb[2]]
-        else:
-            tt(T.wf[:], T.t4[:], dcw, A.add, [dB, "t4"], ["wf"])
-            dma("a", T.dw[:], T.wf[:], ["wf"], ["dw"])
-            dma("a", T.lw[r], T.wf[own, :], ["wf"], ["lw0"])
-            send(lambda k: T.dw[k], T.lw[r], ["dw"], ["lw"])
-            yB = BK(Tb[0])
-            act(T.sq[:], T.sg[:], AF.Square, ["sg"], ["sq"], bias=cen / 64.0, scale=1.0 / 64.0)
-            dma("a", T.ye[:], T.sq[:], ["sq"], ["ye"])
-            mm(PB(Tb[0])[0:16, :], T.jf[:, 0:16], T.sq[:], True, True, ["jf", "sq"], [yB], inc=True)
-            cp(T.ydt[0:16, :], PB(Tb[0])[0:16, :], [yB], ["ydt"])
-            dma("a", T.yd[:], T.ydt[0:16, :], ["ydt"], ["yd"])
-            dma("s", T.yn[:], T.lw[:], ["lw", "lw0"], ["yn"])
+
+        def x_part(i):
+            if i == 0:
+                mm(PB(xB)[:], T.idh8[:], et[:], True, False, ["idh8", "e"], [BK(xB)])
+            else:
+                mm(PB(xB)[:], T.idh[:], ra[:], False, True, ["idh", "ra%d" % t, "ro%d" % t], [BK(xB)], inc=True)
+
+        def new_x():
+            off = CEN if t == 0 else -CEN
+            ts(xa[0], PB(xB)[:], off - 8 * CEN, off, A.add, A.max, [BK(xB)], [xa[1]])
+            twin(0, "g")
+
+        banks = [D[0], D[1], sB, xB, U[0], U[1], U[2], cB]
+
+        def new_names():
+            ts(T.t2[:], PB(cB)[:, 0:192], 7.5, None, A.is_ge, None, [cK], ["t2"])
+            tt(dcw, T.t2[:], dcw, A.mult, ["t2", dB], [dB])
+            if not last:
+                tt(T.wrep[:, 0:192], T.wh[:, 0:192], dcw, A.add, ["wh", dB], ["wrep0"])
+                spread_names()
+                name_list()
+            else:
+                tt(T.wf[:], T.t4[:], dcw, A.add, [dB, "t4"], ["wf"])
+                dma("s", T.dw[:], T.wf[:], ["wf"], ["dw"])
+                dma("s", T.lw[r], T.wf[own, :], ["wf"], ["lw0"])
+                send(lambda k: T.dw[k], T.lw[r], ["dw"], ["lw"])
+                dma("s", T.yn[:], T.lw[:], ["lw", "lw0"], ["yn"])
+
+        def squares():
+            act(T.sq[:], T.sg[:], AF.Square, ["sg", "sg0"], ["sq"], bias=CEN / 64.0, scale=1.0 / 64.0)
+            for k in range(8):
+                dma("a", T.ye[16 * k:16 * k + 16, :], blk(T.sq, k, 64), ["sq"], ["ye%d" % k])
+            for k in range(8):
+                mm(PB(D[0])[:, 0:64], T.idf[:], blk(T.sq, k, 64), k == 0, k == 7, ["idf", "sq"], [BK(D[0])], inc=(k == 7))
+            act(T.ydt[:], PB(D[0])[:, 0:64], AF.Copy, [BK(D[0])], ["ydt"])
+            dma("a", T.yd[:], T.ydt[:], ["ydt"], ["yd"])
+
+        steps = {"G": gather_v, "C": conv, "T": twin, "L": level, "E": median_out, "H": chain, "CH": challengers,
+                 "SV": sub_v, "AV": abs_v, "U": gather_u, "SU": sub_u, "AU": abs_u, "K": cmp, "N": count,
+                 "VD": void_diff, "VE": void_eq, "VC": void_count, "FL": eighths, "DC": change, "ON": old_names,
+                 "SUM": sum_e, "R": rest, "XP": x_part, "X": new_x, "NA": minus_x, "NN": new_names, "SQ": squares,
+                 "W": lambda m: win_x(m, banks[m]), "WO": lambda: win_out(banks, 0.0)}
+        for w in plan:
+            name = w.rstrip("0123456789avg")
+            steps[name](*[int(c) if c.isdigit() else c for c in w[len(name):]])
 
     for s, val in cnt.items():
         if val:

@@ -5,11 +5,14 @@ NR, F, NM, ROUNDS = 8, 512, 6, 3
 MAG = 12582912.0
 CEN = 1280.0
 BIG = 8192.0
-HEAD = "G0v G1a G2v G3a C0g C1v C3a C2v SV0 SV1 T1g T2g G4a C4a G5a C5a L1 L2 H0 AV0 AV1 SV2 SV3 U0a U1a SU0 L3 U2a SU1 L4 E "
-PLAN = HEAD + ("SU2 AV2 SV4 AV3 SV5 NA H1 CH AU0 U3v DC VD05 K0 AV4 SUM AU1 AV5 Ra VD10 VD21 U4v VE0v K1 VD35 AU2 AU3 "
-               "U5v VE1v VC0 K2 N0 VE3a VE2v AU4 XP0 VC1 VC2 K3 AU5 N1 VC3 XP1 K4 X K5 N2 W0 W1 W2 W3 NN W4 W5 W6 W7 WO")
-LAST = HEAD + ("SU2 AV2 SV4 AV3 SV5 NA H1 CH AU0 U3v VD05 K0 AV4 AU1 AV5 FL VD10 VD21 U4v VE0v K1 VD36 AU2 AU3 "
-               "U5v VE1v VC0 K2 N0 VE3a VE2v DC AU4 VC1 VC2 K3 AU5 ON N1 VC3 K4 K5 N2 NN SQ")
+PLAN = ("G0v G3a G1a G2v C2v C3a C1v C0g L10 SV1 SV0 G4a G5a L20 T2g H0 HP05 T1g C4a C5a L11 AV1 HO0 SV3 AV0 L30 L40 SV2 "
+        "H1 E0 CH0v L21 U1a L31 U0a HP15 HO1 L41 E1 SU0 CH1v U5v AV2 AU0 SU1 VD5 VE4 VE2 SUM0 R0v AV3 U2a VE1 SV5 DC SU2 "
+        "AU1 VE3 VE0 VE5 SV4 VC2 SUM1 U3a VC0 K0 AU2 AV4 K1 R1v VC3 SU3 XP00 N0 AU3 VC5 U4v AV5 VC1 XP01 K2 K3 VC4 X0 N1 "
+        "XP10 W2 AU4 W3 AU5 K4 K5 N2 XP11 W1 W0 X1 W6 W5 NA W4 NN W7 O4 NL O7 O6 PX0g O3 O0 O1 PX1g O2 O5")
+LAST = ("G2v G3a G0v C0g C2v G1a C1v SV0 SV1 H0 G5a HP05 G4a C3a C5a L12 AV0 C4a HO0 H1 U0a L22 SV2 AV2 HP16 SU0 T1g HO1 "
+        "U1a SV4 T2g L32 AU0 CH1v AV1 AV4 CH0v U2a L42 SU1 SV3 AV3 VD0 K0 VE5 VE2 U3a AU1 SU2 VC2 VE0 FL VC0 VE4 VE3 SV5 "
+        "SU3 VC3 AU2 VC4 U5v K1 N0 E2 AV5 DC U4v AU3 VC5 K2 VE1 AU5 K3 N1 K5 VC1 AU4 K4 N2 ON NN SQ")
+BANKS = [0, 1, 6, 2, 4, 3, 5, 7]
 STRICT = True
 
 SCRATCH = {
@@ -30,6 +33,8 @@ SCRATCH = {
     "idf": ("sbuf", [128, 128], "float32"), "idm": ("sbuf", [128, 128], "bfloat16"),
     "ip5": ("sbuf", [128, 128], "float16"), "in5": ("sbuf", [128, 128], "float16"),
     "ip4": ("sbuf", [128, 128], "float32"), "in4": ("sbuf", [128, 128], "float32"),
+    "ipm": ("sbuf", [128, 128], "bfloat16"), "inm": ("sbuf", [128, 128], "bfloat16"),
+    "ipk": ("sbuf", [128, 128], "float32"), "ink": ("sbuf", [128, 128], "float32"),
     "fl": ("sbuf", [128, 384], "float32"),
     "ones": ("sbuf", [128, 512], "bfloat16"),
     "zq": ("sbuf", [128, 144], "bfloat16"), "zero": ("sbuf", [128, 512], "float32"),
@@ -38,11 +43,11 @@ SCRATCH = {
     "xl": ("sbuf", [128, 512], "bfloat16"), "xb": ("sbuf", [128, 512], "bfloat16"),
     "nbi": ("sbuf", [128, 192], "int32"), "t1": ("sbuf", [128, 192], "int32"), "t2": ("sbuf", [128, 192], "float32"),
     "t3": ("sbuf", [128, 192], "float32"), "t4": ("sbuf", [128, 192], "float32"),
-    "wh": ("sbuf", [128, 384], "float16"), "wl": ("sbuf", [128, 192], "uint16"),
+    "wh": ("sbuf", [128, 576], "float16"), "wl": ("sbuf", [128, 192], "uint16"),
     "wrep": ("sbuf", [128, 4096], "float16"),
     "vv": ("sbuf", [128, 3072], "float32"), "uu": ("sbuf", [128, 3072], "float16"),
     "bv": ("sbuf", [128, 3072], "float32"), "uw": ("sbuf", [128, 3072], "float32"),
-    "na": ("sbuf", [128, 512], "float32"),
+    "na": ("sbuf", [128, 512], "float32"), "xn": ("sbuf", [128, 512], "float16"),
     "pv": ("sbuf", [128, 2560], "float16"), "qv": ("sbuf", [128, 2568], "float16"),
     "m1": ("sbuf", [128, 2568], "float16"), "m2": ("sbuf", [128, 2560], "float16"),
     "near": ("sbuf", [128, 3072], "bfloat16"),
@@ -125,19 +130,23 @@ def rank_program(g, core, T, topo):
         cnt[s] += 16
         note((s, total, "d"), R, W)
 
-    def send(src, dst, R, W):
-        deps("g", R, [], True)
+    def send(src, dst, R, W, frm=range(NR), to=range(NR)):
         rs, ls = newsem(), newsem()
-        tr = []
-        for i, k in enumerate(peers):
-            rid, pid, _ = topo.addr(cores[k])
-            eng = topo.engines(core, cores[k])
-            tr.append(RemoteDMATransfer(dst_ids=[DstId(rid=rid, pnc=pid)], dma_engine_mask=1 << eng[i],
-                                        remote_sem=T.sem[rs], src=src(k), dst=dst))
-        g.remote_dma_fused(tr, local_sem=T.sem[ls])
-        cnt[rs] = cnt[ls] = NR - 1
-        note((ls, NR - 1, "d"), R, [])
-        note((rs, NR - 1, "d"), [], W)
+        ne = len(topo.engines(core, cores[peers[0]])) // len(to)
+        if r in frm:
+            deps("g", R, [], True)
+            tr = []
+            for i, k in enumerate(k for k in peers if k in to):
+                rid, pid, _ = topo.addr(cores[k])
+                eng = topo.engines(core, cores[k])[i::len(to)]
+                tr.append(RemoteDMATransfer(dst_ids=[DstId(rid=rid, pnc=pid)], dma_engine_mask=sum(1 << e for e in eng),
+                                            remote_sem=T.sem[rs], src=src(k), dst=dst))
+            g.remote_dma_fused(tr, local_sem=T.sem[ls])
+            cnt[ls] = ne * len(tr)
+            note((ls, cnt[ls], "d"), R, [])
+        if r in to:
+            cnt[rs] = ne * len([k for k in peers if k in frm])
+            note((rs, cnt[rs], "d"), [], W)
 
     def ts(out, in0, s1, s2, o0, o1, R, W):
         if s2 is None:
@@ -198,6 +207,7 @@ def rank_program(g, core, T, topo):
     for k in range(8):
         ts(blk(T.selw, k, 128), T.io4[:], float(k), None, A.is_equal, None, ["io4"], ["selw%d" % k])
     for nm, val in (("idn", -1.0), ("idh8", 8.0), ("id1", 1.0), ("id8", 8.0), ("idm16", -16.0), ("idf", 1.0),
+                    ("ipm", 8192 * MAG), ("inm", -8192 * MAG), ("ipk", 8192.0), ("ink", -8192.0),
                     ("idm", -MAG), ("ip5", 512.0), ("in5", -512.0), ("ip4", 4095.0), ("in4", -4095.0)):
         ts(T[nm][:], T.io1[:], 0.0, val, A.is_equal, A.mult, ["io1"], [nm])
     ts(T.idp[:], T.io2[:], 0.0, 2.0 ** -13, A.is_equal, A.mult, ["io2"], ["idp"])
@@ -209,7 +219,8 @@ def rank_program(g, core, T, topo):
     cp(T.zq[:, 15:128:16], T.b8[:], ["b8", "zq"], ["zq"])
     for k in range(8):
         ts(blk(T.selk, k, 128), T.jf[:], T.b8[:, k:k + 1], None, A.mult, None, ["jf", "b8"], ["selk%d" % k])
-    ts(T.wh[:, 192:224], T.io3[:], T.col[:, 0:1], T.col[:, 1:2], A.add, A.add, ["io3", "col0", "col1"], ["wF"])
+    for c in (192, 416):
+        ts(T.wh[:, c:c + 32], T.io3[:], T.col[:, 0:1], T.col[:, 1:2], A.add, A.add, ["io3", "col0", "col1"], ["wF"])
     for i in range(5):
         act(T.cst[:, i::5], T.zero[:], AF.Identity, ["zero"], ["cst%d" % i], bias=BIG if i < 4 else -BIG)
     act(T.m1[:, 0:8], T.zero[:, 0:8], AF.Identity, ["zero"], ["m1"], bias=-BIG)
@@ -238,20 +249,18 @@ def rank_program(g, core, T, topo):
 
     def win_x(m, b):
         for k in range(8):
-            mm(PB(b)[:, k::8], blk(T.selk, k, 128), T.pv[:, 320 * m + 2:320 * m + 320:5], k == 0, False, ["p2"] + SELK, [BK(b)])
+            mm(PB(b)[:, k::8], blk(T.selk, k, 128), blk(T.xn, m, 64), k == 0, False, ["xn%d" % (m // 4)] + SELK, [BK(b)])
 
     def win_x0(m, b):
         for k in range(8):
             mm(PB(b)[:, k::8], blk(T.selw, m, 128), blk(T.xl, k, 64), k == 0, False, ["xl", "xl0"] + SELW, [BK(b)])
 
-    def win_out(banks, add):
-        for m in range(8):
-            b = banks[m]
-            win_n(m, b)
-            if m % 2 == 0:
-                act(blk(T.win, m), PB(b)[:], AF.Identity, [BK(b)], ["win%d" % m], bias=add)
-            else:
-                ts(blk(T.win, m), PB(b)[:], add, None, A.add, None, [BK(b)], ["win%d" % m])
+    def win_out(m, b, add):
+        win_n(m, b)
+        if m % 2 == 0:
+            act(blk(T.win, m), PB(b)[:], AF.Identity, [BK(b)], ["win%d" % m], bias=add)
+        else:
+            ts(blk(T.win, m), PB(b)[:], add, None, A.add, None, [BK(b)], ["win%d" % m])
 
     def spread_names():
         for k in range(1, 8):
@@ -264,7 +273,8 @@ def rank_program(g, core, T, topo):
     def name_list():
         ts(T.wl[:], T.wrep[:, 0:192], 2048.0, None, A.add, None, ["wrep0"], ["wl"])
         dma("s", T.wh[:, 0:192], T.wrep[:, 0:192], ["wrep0"], ["wh"])
-        dma("s", T.wh[:, 224:384], T.wrep[:, 0:160], ["wrep0"], ["wh2"])
+        dma("s", T.wh[:, 224:416], T.wrep[:, 0:192], ["wrep0"], ["wh2"])
+        dma("s", T.wh[:, 448:576], T.wrep[:, 0:128], ["wrep0"], ["wh3"])
 
     D, U, xB, sB, cB = [0, 1], [2, 3, 4], 5, 6, 7
     for m in range(8):
@@ -275,14 +285,18 @@ def rank_program(g, core, T, topo):
     tt(T.wrep[:, 0:192], T.t3[:], T.t2[:], A.add, ["t2", "t3"], ["wrep0"])
     spread_names()
     name_list()
-    win_out(list(range(8)), CEN)
-    ts(xa[0], T.xb[:], CEN, None, A.add, None, ["xb%d" % k for k in range(8)], [xa[1]])
-    twin(0, "g")
+    XB = ["xb%d" % k for k in range(8)]
+    for m in range(8):
+        win_out(m, m, CEN)
+        if m == 3:
+            ts(T.xn[:], T.xb[:], CEN, None, A.add, None, XB, ["xn0", "xn1"])
+    for dst in (xa, qv[0]):
+        op("g", lambda: g.affine_select(dst[0], T.xn[:], [[0, F]], A.is_ge, 0.0, 0, 0), ["xn0", "xn1"], [dst[1]])
 
     def minus_x():
-        act(T.na[:], xa[0], AF.Identity, [xa[1]], ["na"], bias=MAG, scale=-1.0)
+        act(T.na[:], T.xn[:], AF.Identity, ["xn0", "xn1"], ["na"], bias=MAG, scale=-1.0)
 
-    late = [minus_x]
+    minus_x()
 
     for t in range(ROUNDS):
         last = t == ROUNDS - 1
@@ -359,12 +373,13 @@ def rank_program(g, core, T, topo):
             b = U[j % 3]
             tt(blk(T.near, j), blk(T.bv, j), PB(b)[:], A.is_gt, ["bv%d" % j, BK(b)], ["near%d" % j])
 
-        def level(k):
-            n = 5 * F
+        def level(k, h):
+            lo, hi = [(0, 5 * F // 2), (5 * F // 2, 5 * F), (0, 5 * F)][h]
+            c0, c1 = slice(lo, hi), slice(lo + 1, hi + 1)
             out, d0, d1, R, W = [
-                (T.m1[:, 1:n + 1], T.pv[:], T.cst[:], CST, "m1"), (T.m2[:], T.pv[:], T.m1[:, 0:n], ["m1"], "m2"),
-                (T.m1[:, 0:n], T.qv[:, 0:n], T.m2[:], ["m2", "qpad"], "m1"),
-                (T.m2[:], T.qv[:, 1:n + 1], T.m1[:, 0:n], ["m1"], "m2")][k - 1]
+                (T.m1[:, c1], T.pv[:, c0], T.cst[:, c0], CST, "m1"), (T.m2[:, c0], T.pv[:, c0], T.m1[:, c0], ["m1"], "m2"),
+                (T.m1[:, c0], T.qv[:, c0], T.m2[:, c0], ["m2", "qpad"], "m1"),
+                (T.m2[:, c0], T.qv[:, c1], T.m1[:, c0], ["m1"], "m2")][k - 1]
             op("v", lambda: V.tensor_tensor_scan(out, d0, d1, -BIG, A.max, A.min),
                R + [p[1] for p in (pv if k < 3 else qv)], [W])
 
@@ -372,9 +387,26 @@ def rank_program(g, core, T, topo):
             c = slice(96 * h, 96 * h + 96)
             op("v", lambda: V.transpose(T.cw[:, c], T.ct[:, c]),
                ["ct%d_%d" % (j, i) for j in range(3 * h, 3 * h + 3) for i in range(2)], ["cw%d" % h])
-            ts(T.cj[:, c], T.cw[:, c], 8192.0, 2048.0, A.mult, A.add, ["cw%d" % h], ["cj%d" % h])
-            ts(T.ci[:, c], T.cj[:, c], 8191, None, A.bitwise_and, None, ["cj%d" % h], ["ci%d" % h])
-            cp(T.cl[:, c], T.ci[:, c], ["ci%d" % h], ["cl%d" % h])
+
+        HB = {}
+
+        def name_part(h, b):
+            c, HB[h] = slice(96 * h, 96 * h + 96), b
+            for i, (lhs, rhs) in enumerate(((T.ipm, T.ones[:, 0:96]), (T.ipk, T.cw[:, c]),
+                                            (T.inm, T.ones[:, 0:96]), (T.ink, T.cw[:, c]))):
+                mm(PB(b)[:, 0:96], lhs[:], rhs, i == 0, i == 3, ["ipm", "ipk", "inm", "ink", "ones", "cw%d" % h], [BK(b)],
+                   inc=(i == 3))
+
+        def offsets(h):
+            ts(blk(T.cl, h, 96), PB(HB[h])[:, 0:96], -1.0, 2048.0, A.mult, A.add, [BK(HB[h])], ["cl%d" % h])
+
+        def challengers(h, e):
+            if e == "a":
+                act(blk(T.ch, h, 96), PB(HB[h])[:, 0:96], AF.Identity, [BK(HB[h])], ["ch%d" % h], scale=-1.0)
+            else:
+                ts(blk(T.ch, h, 96), blk(T.cl, h, 96), -2048.0, None, A.add, None, ["cl%d" % h], ["ch%d" % h])
+
+        CH = ["ch0", "ch1"]
 
         sums = [w for w in plan if w[:2] in ("N0", "N1", "N2", "VC")]
 
@@ -385,62 +417,60 @@ def rank_program(g, core, T, topo):
                    w == sums[0] and q == 0, w == sums[-1] and q == 15,
                    ["zq", "near%d" % (2 * h), "near%d" % (2 * h + 1)], [cK], inc=(q == 15))
 
-        pairs = [[(192, T.ch[:], T.wh[:, 32 * i:32 * i + 192], 0) for i in (2 * c + 1, 2 * c + 2)] for c in range(3)]
-        pairs.append([(192 - 32 * d, T.ch[:, 0:192 - 32 * d], T.ch[:, 32 * d:192], 32 * d) for d in range(1, 6)])
-        VB = {}
+        VB = []
 
-        def void_diff(c, b):
-            pos, VB[c] = 0, b
-            for i, (wd, lf, rt, _) in enumerate(pairs[c]):
-                end = i == len(pairs[c]) - 1
-                mm(PB(b)[:, pos:pos + wd], T.idh[:], lf, True, False, ["idh", "ch"], [BK(b)])
-                mm(PB(b)[:, pos:pos + wd], T.idn[:], rt, False, True, ["idn", "ch", "wh", "wh2", "wF"], [BK(b)], inc=end)
-                pos += wd
+        def void_twice(b):
+            VB.append(b)
+            for i in range(2):
+                mm(blk(PB(b), i, 192), T.idh[:], T.ch[:], True, True, ["idh"] + CH, [BK(b)], inc=(i == 1))
 
-        def void_eq(c, e):
-            b, wd = VB[c], sum(p[0] for p in pairs[c])
-            dst = T.eq[:, 384 * c:384 * c + wd]
-            if e == "v":
-                ts(dst, PB(b)[:, 0:wd], 0.0, None, A.is_equal, None, [BK(b)], ["eq%d" % c])
+        def eq_at(c):
+            return (384 * c, 384) if c < 3 else (576 + 192 * c, 192 if c < 5 else 96)
+
+        def void_eq(c):
+            b, (pos, wd) = VB[0], eq_at(c)
+            if c < 3:
+                tt(T.eq[:, pos:pos + wd], T.wh[:, 64 * c + 64:64 * c + 448], PB(b)[:, 0:384], A.is_equal,
+                   ["wh", "wh2", "wh3", "wF", BK(b)], ["eq%d" % c])
             else:
-                act(PB(b)[:, 0:wd], PB(b)[:, 0:wd], AF.Abs, [BK(b)], [BK(b)])
-                act(dst, PB(b)[:, 0:wd], AF.Relu, [BK(b)], ["eq%d" % c], bias=1.0, scale=-1.0)
+                d = 32 * (c - 2)
+                tt(T.eq[:, pos:pos + wd], T.ch[:, 0:wd], PB(b)[:, d:d + wd], A.is_equal, CH + [BK(b)], ["eq%d" % c])
 
         def void_count(c):
-            pos, w = 384 * c, "VC%d" % c
-            for i, (wd, _, _, c0) in enumerate(pairs[c]):
-                end = i == len(pairs[c]) - 1
-                mm(PB(cB)[:, c0:192], T.idm16[:], T.eq[:, pos:pos + wd], w == sums[0] and i == 0, w == sums[-1] and end,
-                   ["eq%d" % c, "idm16"], [cK], inc=end)
-                pos += wd
+            pos, w, d = eq_at(c)[0], "VC%d" % c, 32 * (c - 2)
+            parts = [(0, 0, 192), (192, 0, 192)] if c < 3 else [(0, d, 192 - d), (192 - d, 192 - d, d)][:1 if c == 5 else 2]
+            for i, (src, dst, wd) in enumerate(parts):
+                end = i == len(parts) - 1
+                mm(PB(cB)[:, dst:dst + wd], T.idm16[:], T.eq[:, pos + src:pos + src + wd], w == sums[0] and i == 0,
+                   w == sums[-1] and end, ["eq%d" % c, "idm16"], [cK], inc=end)
 
-        def median_out():
-            ts(et[:], T.m2[:, 4::5], MAG, -MAG, A.add, A.add, ["m2"], ["e"])
+        half = [range(0, NR // 2), range(NR // 2, NR)]
+
+        def median_out(h):
             if not last:
-                send(lambda k: blk(et, k, 64), blk(lr, r, 64), ["e"], ["lr%d" % t])
+                ts(blk(et, h, 256), T.m2[:, 1280 * h + 4:1280 * h + 1280:5], MAG, -MAG, A.add, A.add, ["m2"], ["e%d" % h])
+                send(lambda k: blk(et, k, 64), blk(lr, r, 64), ["e%d" % h], ["lr%d" % t], to=half[h])
             else:
+                ts(et[:], T.m2[:, 4::5], MAG, -MAG, A.add, A.add, ["m2"], ["e"])
                 dma("s", T.de[:], et[:], ["e"], ["de"])
                 dma("s", blk(T.sg, r, 64), et[own, :], ["e"], ["sg0"])
                 send(lambda k: T.de[k], blk(T.sg, r, 64), ["de"], ["sg"])
-
-        def challengers():
-            ts(T.ch[:], T.ci[:], -2048.0, None, A.add, None, ["ci0", "ci1"], ["ch"])
 
         dB, dcw, wn = (BK(xB), PB(xB)[:, 0:192], PB(sB)[:, 0:192]) if last else (cK, PB(cB)[:, 192:384], None)
 
         def eighths():
             act(T.fl[:, 0:192], T.wh[:, 0:192], AF.Identity, ["wh"], ["fl0"], bias=255.5625, scale=0.125)
-            act(T.fl[:, 192:384], T.ch[:], AF.Identity, ["ch"], ["fl1"], bias=255.5625, scale=0.125)
+            act(T.fl[:, 192:384], T.ch[:], AF.Identity, CH, ["fl1"], bias=255.5625, scale=0.125)
 
         def change():
             if not last:
-                mm(dcw, T.idh[:], T.ch[:], True, False, ["idh", "ch"], [dB])
+                mm(dcw, T.idh[:], T.ch[:], True, False, ["idh"] + CH, [dB])
                 mm(dcw, T.idn[:], T.wh[:, 0:192], False, True, ["idn", "wh"], [dB])
                 return
             ts(T.fl[:], T.fl[:], MAG, -MAG, A.add, A.add, ["fl0", "fl1"], ["fl0", "fl1"])
             mm(wn, T.ip5[:], T.wh[:, 0:192], True, False, ["ip5", "wh"], [BK(sB)])
             mm(wn, T.in4[:], T.fl[:, 0:192], False, True, ["in4", "fl0"], [BK(sB)], inc=True)
-            mm(dcw, T.ip5[:], T.ch[:], True, False, ["ip5", "ch"], [dB])
+            mm(dcw, T.ip5[:], T.ch[:], True, False, ["ip5"] + CH, [dB])
             mm(dcw, T.in5[:], T.wh[:, 0:192], False, False, ["in5", "wh"], [dB])
             mm(dcw, T.in4[:], T.fl[:, 192:384], False, False, ["in4", "fl1"], [dB])
             mm(dcw, T.ip4[:], T.fl[:, 0:192], False, True, ["ip4", "fl0"], [dB], inc=True)
@@ -448,31 +478,43 @@ def rank_program(g, core, T, topo):
         def old_names():
             act(T.t4[:], wn, AF.Identity, [BK(sB)], ["t4"], bias=512.0 * 2048.0)
 
-        def sum_e():
+        def sum_e(h):
+            if r not in half[h]:
+                return
             mm(PB(sB)[:, 0:64], (T.id1 if t == 0 else T.id8)[:], T.mixc[:], True, False, ["id1", "id8", "mixc"], [BK(sB)])
             for k in range(8):
                 src = blk(et, r, 64) if k == r else blk(lr, k, 64)
-                mm(PB(sB)[:, 0:64], T.idn[:], src, False, k == 7, ["idn", "e", "lr%d" % t], [BK(sB)], inc=(k == 7))
+                mm(PB(sB)[:, 0:64], T.idn[:], src, False, k == 7, ["idn", "e%d" % h, "lr%d" % t], [BK(sB)], inc=(k == 7))
 
-        def rest(e):
-            if e == "a":
-                act(blk(ra, r, 64), PB(sB)[:, 0:64], AF.Identity, [BK(sB)], ["ro%d" % t], bias=8 * CEN)
-            else:
-                ts(blk(ra, r, 64), PB(sB)[:, 0:64], 8 * CEN, None, A.add, None, [BK(sB)], ["ro%d" % t])
-            send(lambda k: blk(ra, r, 64), blk(ra, r, 64), ["ro%d" % t], ["ra%d" % t])
+        def rest(h, e):
+            if r in half[h]:
+                if e == "a":
+                    act(blk(ra, r, 64), PB(sB)[:, 0:64], AF.Identity, [BK(sB)], ["ro%d" % h], bias=8 * CEN)
+                else:
+                    ts(blk(ra, r, 64), PB(sB)[:, 0:64], 8 * CEN, None, A.add, None, [BK(sB)], ["ro%d" % h])
+            send(lambda k: blk(ra, r, 64), blk(ra, r, 64), ["ro%d" % h], ["ra%d" % h], frm=half[h])
 
-        def x_part(i):
+        def x_part(h, i):
+            out = blk(PB(xB), h, 256)
             if i == 0:
-                mm(PB(xB)[:], T.idh8[:], et[:], True, False, ["idh8", "e"], [BK(xB)])
+                mm(out, T.idh8[:], blk(et, h, 256), True, False, ["idh8", "e%d" % h], [BK(xB)])
             else:
-                mm(PB(xB)[:], T.idh[:], ra[:], False, True, ["idh", "ra%d" % t, "ro%d" % t], [BK(xB)], inc=True)
+                mm(out, T.idh[:], blk(ra, h, 256), False, True, ["idh", "ra%d" % h, "ro%d" % h], [BK(xB)], inc=True)
 
-        def new_x():
+        def new_x(h):
             off = CEN if t == 0 else -CEN
-            ts(xa[0], PB(xB)[:], off - 8 * CEN, off, A.add, A.max, [BK(xB)], [xa[1]])
-            twin(0, "g")
+            ts(T.xn[:, 256 * h:256 * h + 256], blk(PB(xB), h, 256), off - 8 * CEN, off, A.add, A.max, [BK(xB)], ["xn%d" % h])
 
-        banks = [D[0], D[1], sB, xB, U[0], U[1], U[2], cB]
+        def place_x(i, e):
+            dst = (xa, qv[0])[i]
+            if e == "g":
+                op("g", lambda: g.affine_select(dst[0], T.xn[:], [[0, F]], A.is_ge, 0.0, 0, 0), ["xn0", "xn1"], [dst[1]])
+            elif e == "v":
+                cp(dst[0], T.xn[:], ["xn0", "xn1"], [dst[1]])
+            else:
+                act(dst[0], T.xn[:], AF.Copy, ["xn0", "xn1"], [dst[1]])
+
+        banks = BANKS
 
         def new_names():
             ts(T.t2[:], PB(cB)[:, 0:192], 7.5, None, A.is_ge, None, [cK], ["t2"])
@@ -480,7 +522,6 @@ def rank_program(g, core, T, topo):
             if not last:
                 tt(T.wrep[:, 0:192], T.wh[:, 0:192], dcw, A.add, ["wh", dB], ["wrep0"])
                 spread_names()
-                name_list()
             else:
                 tt(T.wf[:], T.t4[:], dcw, A.add, [dB, "t4"], ["wf"])
                 dma("s", T.dw[:], T.wf[:], ["wf"], ["dw"])
@@ -498,10 +539,11 @@ def rank_program(g, core, T, topo):
             dma("a", T.yd[:], T.ydt[:], ["ydt"], ["yd"])
 
         steps = {"G": gather_v, "C": conv, "T": twin, "L": level, "E": median_out, "H": chain, "CH": challengers,
+                 "HP": name_part, "HO": offsets, "NL": name_list,
                  "SV": sub_v, "AV": abs_v, "U": gather_u, "SU": sub_u, "AU": abs_u, "K": cmp, "N": count,
-                 "VD": void_diff, "VE": void_eq, "VC": void_count, "FL": eighths, "DC": change, "ON": old_names,
+                 "VD": void_twice, "VE": void_eq, "VC": void_count, "FL": eighths, "DC": change, "ON": old_names,
                  "SUM": sum_e, "R": rest, "XP": x_part, "X": new_x, "NA": minus_x, "NN": new_names, "SQ": squares,
-                 "W": lambda m: win_x(m, banks[m]), "WO": lambda: win_out(banks, 0.0)}
+                 "W": lambda m: win_x(m, banks[m]), "O": lambda m: win_out(m, banks[m], 0.0), "PX": place_x}
         for w in plan:
             name = w.rstrip("0123456789avg")
             steps[name](*[int(c) if c.isdigit() else c for c in w[len(name):]])

@@ -5,14 +5,18 @@ NR, F, NM, ROUNDS = 8, 512, 6, 3
 MAG = 12582912.0
 CEN = 1280.0
 BIG = 8192.0
-PLAN = ("G0v G3a G1a G2v C2v C3a C1v C0g L10 SV1 SV0 G4a G5a L20 T2g H0 HP05 T1g C4a C5a L11 AV1 HO0 SV3 AV0 L30 L40 SV2 "
-        "H1 E0 CH0v L21 U1a L31 U0a HP15 HO1 L41 E1 SU0 CH1v U5v AV2 AU0 SU1 VD5 VE4 VE2 SUM0 R0v AV3 U2a VE1 SV5 DC SU2 "
-        "AU1 VE3 VE0 VE5 SV4 VC2 SUM1 U3a VC0 K0 AU2 AV4 K1 R1v VC3 SU3 XP00 N0 AU3 VC5 U4v AV5 VC1 XP01 K2 K3 VC4 X0 N1 "
-        "XP10 W2 AU4 W3 AU5 K4 K5 N2 XP11 W1 W0 X1 W6 W5 NA W4 NN W7 O4 NL O7 O6 PX0g O3 O0 O1 PX1g O2 O5")
-LAST = ("G2v G3a G0v C0g C2v G1a C1v SV0 SV1 H0 G5a HP05 G4a C3a C5a L12 AV0 C4a HO0 H1 U0a L22 SV2 AV2 HP16 SU0 T1g HO1 "
-        "U1a SV4 T2g L32 AU0 CH1v AV1 AV4 CH0v U2a L42 SU1 SV3 AV3 VD0 K0 VE5 VE2 U3a AU1 SU2 VC2 VE0 FL VC0 VE4 VE3 SV5 "
-        "SU3 VC3 AU2 VC4 U5v K1 N0 E2 AV5 DC U4v AU3 VC5 K2 VE1 AU5 K3 N1 K5 VC1 AU4 K4 N2 ON NN SQ")
-BANKS = [0, 1, 6, 2, 4, 3, 5, 7]
+PLAN = ("G02v G12a C02g G22v C12v C22v G32a C32a L10 L11 L20 H0 T20g T10g G42a C41g T11g G52a C51g T21g C40a C50a L30 "
+        "SV1 SV0 AV0 AV1 HP05 HO0 U1a SV2 AV2 U0a U2a L40 E0 L21 SU1 H1 HP15 SV3 AV3 L31 SU0 CH0v L41 HO1 E1 CH1v DC "
+        "SUM0 Z1 AU0 SV5 SU2 VDg U4v AU1 AU2 R0v U3v VE2 AU3 VE1 VE5 VE4 XP00 Z0 VC2 AU4 AV5 VC1 VC4 SUM1 SV4 AV4 K1 "
+        "VE3 K0 N0 R1v K3 K2 U5v VE0 N1 XP01 VC3 VC5 VC0 AU5 X0 W3 W0 K4 K5 N2 XP10 W2 NN0 XP11 W1 NN1 X1 S01a S05a "
+        "S16a W5 W6 S15v S13v S14v S12v NL S11v S17a S06a S02a S03g S07a S04g M2 M1 O2a M6 M3 O1v O3v W4 M5 O5v O6a "
+        "NA M4 O4a W7 M0 O0a PX1g PX0g M7 O7v ")
+LAST = ("G12a G02v C02g SV0 G22v C22v FL0v C12v SV1 T12g G32a G52a C32a C52g T22g L12 H0 G42a AV0 SV2 AV1 C42a HP05 "
+        "SV3 AV2 L22 HO0 U0a SV4 L32 H1 SU0 HP16 L42 HO1 CH0v U1a SU1 AU0 AV3 SV5 U2a U3a SU2 K0 CH1v U5v VDg E2 VE2 "
+        "FL1v VE0 VE4 U4v AV5 AU1 VE5 K1 SU3 AU3 K3 AU2 K2 AU4 AV4 VE3 VE1 DC Z0 N0 Z1 VC2 VC5 VC4 VC3 N1 VC1 VC0 K4 "
+        "AU5 K5 ON N2 NN0 NH0 NN1 NH1 SQ NO0 NO1 ")
+BANKS = [0, 1, 2, 3, 6, 7, 5, 4]
+SPLIT = [3, 3]
 STRICT = True
 
 SCRATCH = {
@@ -20,7 +24,8 @@ SCRATCH = {
     "dn": ("dram", [8, 128, 24], "int32"), "ln": ("dram", [8, 128, 24], "int32"),
     "dm": ("dram", [128, 64], "bfloat16"), "lm": ("dram", [8, 128, 64], "bfloat16"),
     "de": ("dram", [8, 128, 64], "float16"),
-    "dw": ("dram", [8, 128, 24], "float32"), "lw": ("dram", [8, 128, 24], "float32"),
+    "dw0": ("dram", [8, 128, 16], "float32"), "lw0": ("dram", [8, 128, 16], "float32"),
+    "dw1": ("dram", [8, 128, 8], "float32"), "lw1": ("dram", [8, 128, 8], "float32"),
     "io1": ("sbuf", [128, 128], "int32"), "io2": ("sbuf", [128, 128], "int32"), "io3": ("sbuf", [128, 32], "float32"),
     "io4": ("sbuf", [128, 128], "int32"),
     "tq": ("sbuf", [128, 128], "int32"), "tk": ("sbuf", [128, 8], "int32"), "col": ("sbuf", [128, 8], "float32"),
@@ -32,10 +37,10 @@ SCRATCH = {
     "selw": ("sbuf", [128, 1024], "bfloat16"),
     "idf": ("sbuf", [128, 128], "float32"), "idm": ("sbuf", [128, 128], "bfloat16"),
     "ip5": ("sbuf", [128, 128], "float16"), "in5": ("sbuf", [128, 128], "float16"),
-    "ip4": ("sbuf", [128, 128], "float32"), "in4": ("sbuf", [128, 128], "float32"),
+    "ip4": ("sbuf", [128, 128], "float16"), "in4": ("sbuf", [128, 128], "float16"),
     "ipm": ("sbuf", [128, 128], "bfloat16"), "inm": ("sbuf", [128, 128], "bfloat16"),
     "ipk": ("sbuf", [128, 128], "float32"), "ink": ("sbuf", [128, 128], "float32"),
-    "fl": ("sbuf", [128, 384], "float32"),
+    "fl": ("sbuf", [128, 384], "float16"),
     "ones": ("sbuf", [128, 512], "bfloat16"),
     "zq": ("sbuf", [128, 144], "bfloat16"), "zero": ("sbuf", [128, 512], "float32"),
     "cst": ("sbuf", [128, 2560], "float16"),
@@ -47,13 +52,14 @@ SCRATCH = {
     "wrep": ("sbuf", [128, 4096], "float16"),
     "vv": ("sbuf", [128, 3072], "float32"), "uu": ("sbuf", [128, 3072], "float16"),
     "bv": ("sbuf", [128, 3072], "float32"), "uw": ("sbuf", [128, 3072], "float32"),
+    "bh": ("sbuf", [128, 3072], "float16"), "ah": ("sbuf", [128, 3072], "float16"),
     "na": ("sbuf", [128, 512], "float32"), "xn": ("sbuf", [128, 512], "float16"),
     "pv": ("sbuf", [128, 2560], "float16"), "qv": ("sbuf", [128, 2568], "float16"),
     "m1": ("sbuf", [128, 2568], "float16"), "m2": ("sbuf", [128, 2560], "float16"),
     "near": ("sbuf", [128, 3072], "bfloat16"),
     "ct": ("sbuf", [128, 192], "float32"), "cw": ("sbuf", [128, 192], "float32"),
     "cj": ("sbuf", [128, 192], "int32"), "ci": ("sbuf", [128, 192], "int32"), "cl": ("sbuf", [128, 192], "uint16"),
-    "ch": ("sbuf", [128, 192], "float16"), "eq": ("sbuf", [128, 1632], "bfloat16"),
+    "ch": ("sbuf", [128, 384], "float16"), "eq": ("sbuf", [128, 1632], "bfloat16"),
     "mixc": ("sbuf", [128, 64], "bfloat16"),
     "e0": ("sbuf", [128, 512], "float16"), "e1": ("sbuf", [128, 512], "float16"),
     "lr0": ("sbuf", [128, 512], "float16"), "lr1": ("sbuf", [128, 512], "float16"),
@@ -77,7 +83,7 @@ def rank_program(g, core, T, topo):
     V, ACT, PE = g.vector, g.scalar, g.tensor
     cnt = {"qv": 0, "qa": 0, "qp": 0, "qg": 0}
     seen = {e: {} for e in Q}
-    wr, rd, nsem = {}, {}, [0]
+    wr, rd, known, nsem = {}, {}, {}, [0]
 
     def newsem():
         nsem[0] += 1
@@ -101,10 +107,18 @@ def rank_program(g, core, T, topo):
         for k in W:
             for tok in wr.get(k, []) + rd.get(k, []):
                 add(tok, False)
-        for s, val in need.items():
-            if seen[e].get(s, 0) < val:
+        todo = {s: val for s, val in need.items() if seen[e].get(s, 0) < val}
+        for s, val in todo.items():
+            if not any(known.get((o, w), {}).get(s, 0) >= val for o, w in todo.items() if o != s):
                 Q[e].wait_ge(T.sem[s], val)
-                seen[e][s] = val
+        for s, val in todo.items():
+            for o, w in list(known.get((s, val), {}).items()) + [(s, val)]:
+                seen[e][o] = max(seen[e].get(o, 0), w)
+
+    def vouch(tok, e):
+        old = known.setdefault(tok[:2], {})
+        for o, w in seen[e].items():
+            old[o] = max(old.get(o, 0), w)
 
     def note(tok, R, W):
         for k in R:
@@ -121,6 +135,7 @@ def rank_program(g, core, T, topo):
         if inc:
             ins.then_inc(T.sem[s], 1)
             cnt[s] += 1
+        vouch(tok, e)
         note(tok, R, W)
 
     def dma(e, out, in_, R, W, sem=None, total=16, **kw):
@@ -128,6 +143,7 @@ def rank_program(g, core, T, topo):
         s = sem or newsem()
         Q[e].dma_start(out, in_, **kw).then_inc(T.sem[s], 16)
         cnt[s] += 16
+        vouch((s, total), e)
         note((s, total, "d"), R, W)
 
     def send(src, dst, R, W, frm=range(NR), to=range(NR)):
@@ -189,7 +205,7 @@ def rank_program(g, core, T, topo):
     op("g", lambda: g.iota(T.io3[:], [[128, 32]], -2048, 0, allow_small_or_imprecise_dtypes=True), [], ["io3"])
     send(lambda k: T.dn[k], T.ln[r], ["dn"], ["ln"])
     send(lambda k: T.dx[k], blk(T.xl, r, 64), ["dx"], ["xl"])
-    send(lambda k: T.dm[:], T.lm[r], ["dm"], ["lm"])
+    send(lambda k: T.dm[:], T.lm[r], ["dm", "xl"], ["lm"])
     dma("s", T.nbi[:], T.ln[:], ["ln", "ln0"], ["nbi"])
     xs = newsem()
     for k in range(8):
@@ -200,15 +216,15 @@ def rank_program(g, core, T, topo):
     op("v", lambda: V.memset(T.zq[:], 0.0), [], ["zq"])
     ts(T.tq[:], T.io1[:], 15, None, A.bitwise_and, None, ["io1"], ["tq"])
     ts(T.tk[:], T.io1[:, 0::16], 4, None, A.arith_shift_right, None, ["io1"], ["tk"])
-    cp(blk(T.wrep, 0), T.zero[:], ["zero"], ["wrep0"])
+    cp(T.wrep[:, 192:512], T.zero[:, 192:512], ["zero"], ["wpad0"])
     ts(T.idh[:], T.io1[:], 0.0, None, A.is_equal, None, ["io1"], ["idh"])
     for k in range(1, 8):
-        act(T.wrep[:, 512 * k + 192:512 * k + 512], T.wrep[:, 192:512], AF.Copy, ["wrep0"], ["wrep%d" % k])
+        act(T.wrep[:, 512 * k + 192:512 * k + 512], T.wrep[:, 192:512], AF.Copy, ["wpad0"], ["wpad%d" % k])
     for k in range(8):
         ts(blk(T.selw, k, 128), T.io4[:], float(k), None, A.is_equal, None, ["io4"], ["selw%d" % k])
     for nm, val in (("idn", -1.0), ("idh8", 8.0), ("id1", 1.0), ("id8", 8.0), ("idm16", -16.0), ("idf", 1.0),
                     ("ipm", 8192 * MAG), ("inm", -8192 * MAG), ("ipk", 8192.0), ("ink", -8192.0),
-                    ("idm", -MAG), ("ip5", 512.0), ("in5", -512.0), ("ip4", 4095.0), ("in4", -4095.0)):
+                    ("idm", -MAG), ("ip5", 512.0), ("in5", -512.0), ("ip4", 4096.0), ("in4", -4096.0)):
         ts(T[nm][:], T.io1[:], 0.0, val, A.is_equal, A.mult, ["io1"], [nm])
     ts(T.idp[:], T.io2[:], 0.0, 2.0 ** -13, A.is_equal, A.mult, ["io2"], ["idp"])
     op("v", lambda: V.memset(T.ones[:], 1.0), [], ["ones"])
@@ -224,259 +240,302 @@ def rank_program(g, core, T, topo):
     for i in range(5):
         act(T.cst[:, i::5], T.zero[:], AF.Identity, ["zero"], ["cst%d" % i], bias=BIG if i < 4 else -BIG)
     act(T.m1[:, 0:8], T.zero[:, 0:8], AF.Identity, ["zero"], ["m1"], bias=-BIG)
+    note(wr["m1"][0], [], ["m1_0"])
     act(T.qv[:, 0:1], T.zero[:, 0:1], AF.Copy, ["zero"], ["qpad"])
     CST = ["cst%d" % k for k in range(5)]
-    pv = [(T.pv[:, i::5], "p%d" % i) for i in range(5)]
-    qv = [(T.qv[:, 1 + i:2561:5], "q%d" % i) for i in range(5)]
-    home = [pv[0], pv[1], pv[3], pv[4], qv[3], qv[4]]
-    xa = pv[2]
+    span = [(0, F // 2), (F // 2, F), (0, F)]
 
-    def twin(i, e):
+    def halves(key, h):
+        return [key + "_%d" % i for i in ((0, 1) if h == 2 else (h,))]
+
+    def place(w, h=2):
+        buf, i = w
+        lo, hi = span[h]
+        c = i + (buf == "qv")
+        return T[buf][:, 5 * lo + c:5 * hi + (buf == "qv"):5], halves("%s%d" % w, h)
+
+    home = [("pv", 0), ("pv", 1), ("pv", 3), ("pv", 4), ("qv", 3), ("qv", 4)]
+    xa = place(("pv", 2))
+
+    for w in (("pv", 4), ("qv", 4)):
+        act(place(w)[0], T.zero[:], AF.Copy, ["zero"], place(w)[1])
+
+    def copy(e, out, src, n, R, W):
         if e == "g":
-            op("g", lambda: g.affine_select(qv[i][0], pv[i + 2][0], [[0, F]], A.is_ge, 0.0, 0, 0), [pv[i + 2][1]], [qv[i][1]])
+            op("g", lambda: g.affine_select(out, src, [[0, n]], A.is_ge, 0.0, 0, 0), R, W)
         elif e == "v":
-            cp(qv[i][0], pv[i + 2][0], [pv[i + 2][1]], [qv[i][1]])
+            cp(out, src, R, W)
         else:
-            act(qv[i][0], pv[i + 2][0], AF.Copy, [pv[i + 2][1]], [qv[i][1]])
+            act(out, src, AF.Copy, R, W)
+
+    def twin(i, h, e):
+        src, dst = place(("pv", i + 2), h), place(("qv", i), h)
+        copy(e, dst[0], src[0], span[h][1] - span[h][0], src[1], dst[1])
+
     SELK = ["selk%d" % k for k in range(8)]
     SELW = ["selw%d" % k for k in range(8)]
-    WREP = ["wrep%d" % k for k in range(8)]
+    WREP = ["wpad%d" % k for k in range(8)] + [key for k in range(8) for key in halves("wrep%d" % k, 2)]
     WIN = ["win%d" % m for m in range(8)]
 
-    def win_n(m, b):
+    def win_n(m, b, first):
         for i in range(4):
-            mm(blk(PB(b), i, 128), T.wrep[:, 4 * m + i::32], T.idp[:], False, i == 3, WREP + ["idp"], [BK(b)], inc=i == 3)
+            end = i == 3 and not first
+            mm(blk(PB(b), i, 128), T.wrep[:, 4 * m + i::32], T.idp[:], first and i == 0, end, WREP + ["idp"], [BK(b)], inc=end)
 
-    def win_x(m, b):
+    def win_x(m, b, first):
         for k in range(8):
-            mm(PB(b)[:, k::8], blk(T.selk, k, 128), blk(T.xn, m, 64), k == 0, False, ["xn%d" % (m // 4)] + SELK, [BK(b)])
+            end = k == 7 and not first
+            mm(PB(b)[:, k::8], blk(T.selk, k, 128), blk(T.xn, m, 64), first and k == 0, end,
+               ["xn%d" % (m // 4)] + SELK, [BK(b)], inc=end)
 
     def win_x0(m, b):
         for k in range(8):
             mm(PB(b)[:, k::8], blk(T.selw, m, 128), blk(T.xl, k, 64), k == 0, False, ["xl", "xl0"] + SELW, [BK(b)])
 
-    def win_out(m, b, add):
-        win_n(m, b)
-        if m % 2 == 0:
+    def win_out(m, b, e, add=0.0):
+        if e == "a":
             act(blk(T.win, m), PB(b)[:], AF.Identity, [BK(b)], ["win%d" % m], bias=add)
         else:
             ts(blk(T.win, m), PB(b)[:], add, None, A.add, None, [BK(b)], ["win%d" % m])
 
-    def spread_names():
-        for k in range(1, 8):
-            dst = T.wrep[:, 512 * k:512 * k + 192]
-            if k < 6:
-                cp(dst, T.wrep[:, 0:192], ["wrep0"], ["wrep%d" % k])
-            else:
-                act(dst, T.wrep[:, 0:192], AF.Copy, ["wrep0"], ["wrep%d" % k])
+    def spread(p, k, e):
+        lo, hi = [(0, 128), (128, 192), (0, 192)][p]
+        copy(e, T.wrep[:, 512 * k + lo:512 * k + hi], T.wrep[:, lo:hi], hi - lo, halves("wrep0", p), halves("wrep%d" % k, p))
 
     def name_list():
-        ts(T.wl[:], T.wrep[:, 0:192], 2048.0, None, A.add, None, ["wrep0"], ["wl"])
-        dma("s", T.wh[:, 0:192], T.wrep[:, 0:192], ["wrep0"], ["wh"])
-        dma("s", T.wh[:, 224:416], T.wrep[:, 0:192], ["wrep0"], ["wh2"])
-        dma("s", T.wh[:, 448:576], T.wrep[:, 0:128], ["wrep0"], ["wh3"])
+        R = halves("wrep0", 2)
+        ts(T.wl[:], T.wrep[:, 0:192], 2048.0, None, A.add, None, R, ["wl"])
+        dma("s", T.wh[:, 0:192], T.wrep[:, 0:192], R, ["wh"])
+        dma("s", T.wh[:, 224:416], T.wrep[:, 0:192], R, ["wh2"])
+        dma("s", T.wh[:, 448:576], T.wrep[:, 0:128], R, ["wh3"])
 
     D, U, xB, sB, cB = [0, 1], [2, 3, 4], 5, 6, 7
-    for m in range(8):
+    for m in range(7):
         win_x0(m, m)
     ts(T.t1[:], T.nbi[:], 9, None, A.arith_shift_right, None, ["nbi"], ["t1"])
     ts(T.t3[:], T.nbi[:], 8.0, -2048.0, A.mult, A.add, ["nbi"], ["t3"])
-    ts(T.t2[:], T.t1[:], -4095.0, None, A.mult, None, ["t1"], ["t2"])
-    tt(T.wrep[:, 0:192], T.t3[:], T.t2[:], A.add, ["t2", "t3"], ["wrep0"])
-    spread_names()
+    ts(PB(7)[:, 0:192], T.t1[:], -4095.0, None, A.mult, None, ["t1"], [BK(7)])
+    tt(T.wrep[:, 0:192], T.t3[:], PB(7)[:, 0:192], A.add, [BK(7), "t3"], halves("wrep0", 2))
+    win_x0(7, 7)
+    for k in range(1, 8):
+        spread(2, k, "v" if k < 6 else "a")
     name_list()
     XB = ["xb%d" % k for k in range(8)]
+    ts(T.xn[:], T.xb[:], CEN, None, A.add, None, XB, ["xn0", "xn1"])
+    act(T.na[:], T.xb[:], AF.Identity, XB, ["na"], bias=MAG - CEN, scale=-1.0)
     for m in range(8):
-        win_out(m, m, CEN)
-        if m == 3:
-            ts(T.xn[:], T.xb[:], CEN, None, A.add, None, XB, ["xn0", "xn1"])
-    for dst in (xa, qv[0]):
-        op("g", lambda: g.affine_select(dst[0], T.xn[:], [[0, F]], A.is_ge, 0.0, 0, 0), ["xn0", "xn1"], [dst[1]])
+        win_n(m, m, False)
+        win_out(m, m, "av"[m % 2], CEN)
+
+    def place_x(i, e):
+        dst = (xa, place(("qv", 0)))[i]
+        copy(e, dst[0], T.xn[:], F, ["xn0", "xn1"], dst[1])
+
+    place_x(0, "g")
+    place_x(1, "g")
 
     def minus_x():
         act(T.na[:], T.xn[:], AF.Identity, ["xn0", "xn1"], ["na"], bias=MAG, scale=-1.0)
 
-    minus_x()
-
     for t in range(ROUNDS):
         last = t == ROUNDS - 1
         cK = BK(cB)
-        v = [(blk(T.vv, j), "v%d" % j) for j in range(NM)]
         csem = [newsem(), newsem()]
         rough = set()
         plan = (LAST if last else PLAN).split()
         et = T["e%d" % t]
         lr, ra = T["lr%d" % min(t, 1)], T["ra%d" % min(t, 1)]
 
-        def gather_v(j, e):
-            src = T.win[:, 0:4096].indirect(blk(T.wl, j, 32))
-            if e == "v":
-                cp(v[j][0], src, WIN + ["wl"], [v[j][1]])
-            else:
-                act(v[j][0], src, AF.Copy, WIN + ["wl"], [v[j][1]])
+        got = {}
+        sp = SPLIT[last]
+        cut = [slice(0, 32 * sp), slice(32 * sp, 192)]
+        DV = [D[j % 2] for j in range(NM)]
+        DU = [U[j % (3 if last else 2)] for j in range(NM)]
+
+        def gather_v(j, h, e):
+            lo, hi = span[h]
+            src = T.win[:, 0:4096].indirect(T.wl[:, 32 * j + lo // 16:32 * j + hi // 16])
+            copy(e, T.vv[:, F * j + lo:F * j + hi], src, hi - lo, WIN + ["wl"], halves("v%d" % j, h))
+            got[j] = got.get(j, 0) + hi - lo
             b = (j + t) % NM
-            for h in range(2):
-                dma("s", T.ct[:, 32 * j + 16 * h:32 * j + 16 * h + 16], T.vv[16 * h + b::32, j * F:(j + 1) * F],
-                    [v[j][1]], ["ct%d_%d" % (j, h)], sem=csem[j // 3], total=96)
+            for i in range(2 if got[j] == F else 0):
+                dma("s", T.ct[:, 32 * j + 16 * i:32 * j + 16 * i + 16], T.vv[16 * i + b::32, j * F:(j + 1) * F],
+                    halves("v%d" % j, 2), ["ct%d_%d" % (j, i)], sem=csem[j // sp], total=32 * (sp, NM - sp)[j // sp])
 
-        def narrow(out, src, R, key, e):
-            if e != "v":
-                if e == "a":
-                    act(out, src, AF.Copy, R, [key])
-                else:
-                    op("g", lambda: g.affine_select(out, src, [[0, F]], A.is_ge, 0.0, 0, 0), R, [key])
-                if last:
-                    rough.add(key)
-            elif last:
-                ts(out, src, MAG, -MAG, A.add, A.add, R, [key])
+        def narrow(out, src, n, R, W, e):
+            if last and e == "v":
+                ts(out, src, MAG, -MAG, A.add, A.add, R, W)
             else:
-                cp(out, src, R, [key])
+                copy(e, out, src, n, R, W)
+                rough.update(W if last else [])
 
-        def conv(j, e):
-            narrow(home[j][0], v[j][0], [v[j][1]], home[j][1], e)
+        def conv(j, h, e):
+            lo, hi = span[h]
+            dst = place(home[j], h)
+            narrow(dst[0], T.vv[:, F * j + lo:F * j + hi], hi - lo, halves("v%d" % j, h), dst[1], e)
 
         def gather_u(j, e):
-            src, R = T.win[:, 0:4096].indirect(blk(T.cl, j, 32)), WIN + ["cl%d" % (j // 3)]
+            src, R = T.win[:, 0:4096].indirect(blk(T.cl, j, 32)), WIN + ["cl%d" % (j // sp)]
             if e == "v":
                 tt(blk(T.uw, j), src, T.na[:], A.add, R + ["na"], ["u%d" % j])
                 wide.add(j)
             else:
-                narrow(blk(T.uu, j), src, R, "u%d" % j, e)
+                narrow(blk(T.uu, j), src, F, R, ["u%d" % j], e)
 
-        def less_a(b, src, key):
-            if key in rough:
+        def less_a(b, src, keys):
+            ro = bool(rough & set(keys))
+            if ro:
                 mm(PB(b)[:], T.idm[:], T.ones[:], True, False, ["idm", "ones"], [BK(b)])
-            mm(PB(b)[:], T.idh[:], src, key not in rough, False, ["idh", key], [BK(b)])
-            mm(PB(b)[:], T.idn[:], xa[0], False, True, ["idn", xa[1]], [BK(b)], inc=True)
-            return MAG if key in rough else 0.0
+            mm(PB(b)[:], T.idh[:], src, not ro, False, ["idh"] + keys, [BK(b)])
+            mm(PB(b)[:], T.idn[:], xa[0], False, True, ["idn"] + xa[1], [BK(b)], inc=True)
+            return MAG if ro else 0.0
 
         back_u, back_v, wide = {}, {}, set()
 
         def sub_v(j):
-            back_v[j] = less_a(D[j % 2], *home[j])
+            back_v[j] = less_a(DV[j], *place(home[j]))
 
         def abs_v(j):
-            b = D[j % 2]
-            act(blk(T.bv, j), PB(b)[:], AF.Abs, [BK(b)], ["bv%d" % j], bias=back_v[j])
+            b = DV[j]
+            act(blk(T.bv if last else T.bh, j), PB(b)[:], AF.Abs, [BK(b)], ["bv%d" % j], bias=back_v[j])
 
         def sub_u(j):
-            back_u[j] = less_a(U[j % 3], blk(T.uu, j), "u%d" % j)
+            back_u[j] = less_a(DU[j], blk(T.uu, j), ["u%d" % j])
 
         def abs_u(j):
-            b = U[j % 3]
+            b = DU[j]
+            out, W = (PB(b)[:], [BK(b)]) if last else (blk(T.ah, j), ["au%d" % j])
             if j in wide:
-                act(PB(b)[:], blk(T.uw, j), AF.Abs, ["u%d" % j], [BK(b)], bias=-MAG)
+                act(out, blk(T.uw, j), AF.Abs, ["u%d" % j], W, bias=-MAG)
             else:
-                act(PB(b)[:], PB(b)[:], AF.Abs, [BK(b)], [BK(b)], bias=back_u[j])
+                act(out, PB(b)[:], AF.Abs, [BK(b)], W, bias=back_u[j])
 
         def cmp(j):
-            b = U[j % 3]
-            tt(blk(T.near, j), blk(T.bv, j), PB(b)[:], A.is_gt, ["bv%d" % j, BK(b)], ["near%d" % j])
+            b = DU[j]
+            if last:
+                tt(blk(T.near, j), blk(T.bv, j), PB(b)[:], A.is_gt, ["bv%d" % j, BK(b)], ["near%d" % j])
+            else:
+                tt(blk(T.near, j), blk(T.bh, j), blk(T.ah, j), A.is_gt, ["bv%d" % j, "au%d" % j], ["near%d" % j])
 
         def level(k, h):
-            lo, hi = [(0, 5 * F // 2), (5 * F // 2, 5 * F), (0, 5 * F)][h]
-            c0, c1 = slice(lo, hi), slice(lo + 1, hi + 1)
+            lo, hi = span[h]
+            c0, c1 = slice(5 * lo, 5 * hi), slice(5 * lo + 1, 5 * hi + 1)
+            m1, m2, seam = halves("m1", h), halves("m2", h), ["seam"]
             out, d0, d1, R, W = [
-                (T.m1[:, c1], T.pv[:, c0], T.cst[:, c0], CST, "m1"), (T.m2[:, c0], T.pv[:, c0], T.m1[:, c0], ["m1"], "m2"),
-                (T.m1[:, c0], T.qv[:, c0], T.m2[:, c0], ["m2", "qpad"], "m1"),
-                (T.m2[:, c0], T.qv[:, c1], T.m1[:, c0], ["m1"], "m2")][k - 1]
-            op("v", lambda: V.tensor_tensor_scan(out, d0, d1, -BIG, A.max, A.min),
-               R + [p[1] for p in (pv if k < 3 else qv)], [W])
+                (T.m1[:, c1], T.pv[:, c0], T.cst[:, c0], CST, m1 + seam * (h == 0)),
+                (T.m2[:, c0], T.pv[:, c0], T.m1[:, c0], m1 + seam * (h == 1), m2),
+                (T.m1[:, c0], T.qv[:, c0], T.m2[:, c0], m2 + ["qpad", "qv4_0"], m1 + seam * (h == 1)),
+                (T.m2[:, c0], T.qv[:, c1], T.m1[:, c0], m1, m2)][k - 1]
+            data = [key for i in range(5) for key in place(("pv" if k < 3 else "qv", i), h)[1]]
+            op("v", lambda: V.tensor_tensor_scan(out, d0, d1, -BIG, A.max, A.min), R + data, W)
 
         def chain(h):
-            c = slice(96 * h, 96 * h + 96)
+            c = cut[h]
             op("v", lambda: V.transpose(T.cw[:, c], T.ct[:, c]),
-               ["ct%d_%d" % (j, i) for j in range(3 * h, 3 * h + 3) for i in range(2)], ["cw%d" % h])
+               ["ct%d_%d" % (j, i) for j in range(NM) if j // sp == h for i in range(2)], ["cw%d" % h])
 
         HB = {}
 
         def name_part(h, b):
-            c, HB[h] = slice(96 * h, 96 * h + 96), b
-            for i, (lhs, rhs) in enumerate(((T.ipm, T.ones[:, 0:96]), (T.ipk, T.cw[:, c]),
-                                            (T.inm, T.ones[:, 0:96]), (T.ink, T.cw[:, c]))):
-                mm(PB(b)[:, 0:96], lhs[:], rhs, i == 0, i == 3, ["ipm", "ipk", "inm", "ink", "ones", "cw%d" % h], [BK(b)],
+            c, HB[h] = cut[h], b
+            for i, (lhs, rhs) in enumerate(((T.ipm, T.ones[:, c]), (T.ipk, T.cw[:, c]),
+                                            (T.inm, T.ones[:, c]), (T.ink, T.cw[:, c]))):
+                mm(PB(b)[:, c], lhs[:], rhs, i == 0, i == 3, ["ipm", "ipk", "inm", "ink", "ones", "cw%d" % h], [BK(b)],
                    inc=(i == 3))
 
         def offsets(h):
-            ts(blk(T.cl, h, 96), PB(HB[h])[:, 0:96], -1.0, 2048.0, A.mult, A.add, [BK(HB[h])], ["cl%d" % h])
+            ts(T.cl[:, cut[h]], PB(HB[h])[:, cut[h]], -1.0, 2048.0, A.mult, A.add, [BK(HB[h])], ["cl%d" % h])
 
         def challengers(h, e):
             if e == "a":
-                act(blk(T.ch, h, 96), PB(HB[h])[:, 0:96], AF.Identity, [BK(HB[h])], ["ch%d" % h], scale=-1.0)
+                act(T.ch[:, cut[h]], PB(HB[h])[:, cut[h]], AF.Identity, [BK(HB[h])], ["ch%d" % h], scale=-1.0)
             else:
-                ts(blk(T.ch, h, 96), blk(T.cl, h, 96), -2048.0, None, A.add, None, ["cl%d" % h], ["ch%d" % h])
+                ts(T.ch[:, cut[h]], T.cl[:, cut[h]], -2048.0, None, A.add, None, ["cl%d" % h], ["ch%d" % h])
 
         CH = ["ch0", "ch1"]
 
-        sums = [w for w in plan if w[:2] in ("N0", "N1", "N2", "VC")]
+        parts = [(0, 128, cB), (128, 192, D[1] if last else U[2])]
+        sums = [[w for w in plan if w[:2] in ("VC",) + n] for n in (("N0", "N1"), ("N2",))]
+
+        def zero_count(p):
+            lo, hi, b = parts[p]
+            mm(PB(b)[:, lo:hi], T.idh[:], T.wrep[:, 192 + lo:192 + hi], True, False, ["idh", "wpad0"], [BK(b)])
 
         def count(h):
-            w = "N%d" % h
+            w, p = "N%d" % h, h // 2
+            b = parts[p][2]
             for q in range(16):
-                mm(PB(cB)[:, 64 * h:64 * h + 64], T.zq[:, 15 - q:143 - q], T.near[:, 1024 * h + q:1024 * h + 1024:16],
-                   w == sums[0] and q == 0, w == sums[-1] and q == 15,
-                   ["zq", "near%d" % (2 * h), "near%d" % (2 * h + 1)], [cK], inc=(q == 15))
+                mm(PB(b)[:, 64 * h:64 * h + 64], T.zq[:, 15 - q:143 - q], T.near[:, 1024 * h + q:1024 * h + 1024:16],
+                   False, w == sums[p][-1] and q == 15,
+                   ["zq", "near%d" % (2 * h), "near%d" % (2 * h + 1)], [BK(b)], inc=(q == 15))
 
-        VB = []
-
-        def void_twice(b):
-            VB.append(b)
-            for i in range(2):
-                mm(blk(PB(b), i, 192), T.idh[:], T.ch[:], True, True, ["idh"] + CH, [BK(b)], inc=(i == 1))
+        def void_twice(e):
+            copy(e, T.ch[:, 192:384], T.ch[:, 0:192], 192, CH, ["chh"])
 
         def eq_at(c):
             return (384 * c, 384) if c < 3 else (576 + 192 * c, 192 if c < 5 else 96)
 
         def void_eq(c):
-            b, (pos, wd) = VB[0], eq_at(c)
+            pos, wd = eq_at(c)
             if c < 3:
-                tt(T.eq[:, pos:pos + wd], T.wh[:, 64 * c + 64:64 * c + 448], PB(b)[:, 0:384], A.is_equal,
-                   ["wh", "wh2", "wh3", "wF", BK(b)], ["eq%d" % c])
+                tt(T.eq[:, pos:pos + wd], T.wh[:, 64 * c + 64:64 * c + 448], T.ch[:], A.is_equal,
+                   ["wh", "wh2", "wh3", "wF", "chh"] + CH, ["eq%d" % c])
             else:
                 d = 32 * (c - 2)
-                tt(T.eq[:, pos:pos + wd], T.ch[:, 0:wd], PB(b)[:, d:d + wd], A.is_equal, CH + [BK(b)], ["eq%d" % c])
+                tt(T.eq[:, pos:pos + wd], T.ch[:, 0:wd], T.ch[:, d:d + wd], A.is_equal, CH + ["chh"], ["eq%d" % c])
 
         def void_count(c):
             pos, w, d = eq_at(c)[0], "VC%d" % c, 32 * (c - 2)
-            parts = [(0, 0, 192), (192, 0, 192)] if c < 3 else [(0, d, 192 - d), (192 - d, 192 - d, d)][:1 if c == 5 else 2]
-            for i, (src, dst, wd) in enumerate(parts):
-                end = i == len(parts) - 1
-                mm(PB(cB)[:, dst:dst + wd], T.idm16[:], T.eq[:, pos + src:pos + src + wd], w == sums[0] and i == 0,
-                   w == sums[-1] and end, ["eq%d" % c, "idm16"], [cK], inc=end)
+            runs = [(0, 0), (192, 0)] if c < 3 else [(0, d), (192 - d, 192 - d)][:1 if c == 5 else 2]
+            for p, (lo, hi, b) in enumerate(parts):
+                cut = [(src + max(lo, dst) - dst, max(lo, dst)) for src, dst in runs if dst < hi]
+                for i, (src, dst) in enumerate(cut):
+                    end = i == len(cut) - 1
+                    mm(PB(b)[:, dst:hi], T.idm16[:], T.eq[:, pos + src:pos + src + hi - dst], False,
+                       w == sums[p][-1] and end, ["eq%d" % c, "idm16"], [BK(b)], inc=end)
 
         half = [range(0, NR // 2), range(NR // 2, NR)]
 
-        def median_out(h):
+        def median_out(h, e="v"):
             if not last:
-                ts(blk(et, h, 256), T.m2[:, 1280 * h + 4:1280 * h + 1280:5], MAG, -MAG, A.add, A.add, ["m2"], ["e%d" % h])
+                src = T.m2[:, 1280 * h + 4:1280 * h + 1280:5]
+                if e == "a":
+                    act(blk(et, h, 256), src, AF.Identity, halves("m2", h), ["e%d" % h], bias=-CEN)
+                else:
+                    ts(blk(et, h, 256), src, -CEN, None, A.add, None, halves("m2", h), ["e%d" % h])
                 send(lambda k: blk(et, k, 64), blk(lr, r, 64), ["e%d" % h], ["lr%d" % t], to=half[h])
             else:
-                ts(et[:], T.m2[:, 4::5], MAG, -MAG, A.add, A.add, ["m2"], ["e"])
+                ts(et[:], T.m2[:, 4::5], MAG, -MAG, A.add, A.add, halves("m2", 2), ["e"])
                 dma("s", T.de[:], et[:], ["e"], ["de"])
                 dma("s", blk(T.sg, r, 64), et[own, :], ["e"], ["sg0"])
                 send(lambda k: T.de[k], blk(T.sg, r, 64), ["de"], ["sg"])
 
-        dB, dcw, wn = (BK(xB), PB(xB)[:, 0:192], PB(sB)[:, 0:192]) if last else (cK, PB(cB)[:, 192:384], None)
+        dB, wn = BK(xB), PB(sB)[:, 0:192]
+        dcw = [PB(xB)[:, lo:hi] if last else PB(b)[:, 192 + lo:192 + hi] for lo, hi, b in parts]
 
-        def eighths():
-            act(T.fl[:, 0:192], T.wh[:, 0:192], AF.Identity, ["wh"], ["fl0"], bias=255.5625, scale=0.125)
-            act(T.fl[:, 192:384], T.ch[:], AF.Identity, CH, ["fl1"], bias=255.5625, scale=0.125)
+        def eighths(i, e):
+            src, R = ((T.wh[:, 0:192], ["wh"]), (T.ch[:, 0:192], CH))[i]
+            if e == "a":
+                act(blk(T.fl, i, 192), src, AF.Identity, R, ["fl%d" % i], bias=CEN + 255.5625, scale=0.125)
+            else:
+                ts(blk(T.fl, i, 192), src, 0.125, CEN + 255.5625, A.mult, A.add, R, ["fl%d" % i])
 
         def change():
             if not last:
-                mm(dcw, T.idh[:], T.ch[:], True, False, ["idh"] + CH, [dB])
-                mm(dcw, T.idn[:], T.wh[:, 0:192], False, True, ["idn", "wh"], [dB])
+                for p, (lo, hi, b) in enumerate(parts):
+                    mm(dcw[p], T.idh[:], T.ch[:, lo:hi], True, False, ["idh"] + CH, [BK(b)])
+                    mm(dcw[p], T.idn[:], T.wh[:, lo:hi], False, True, ["idn", "wh"], [BK(b)], inc=True)
                 return
-            ts(T.fl[:], T.fl[:], MAG, -MAG, A.add, A.add, ["fl0", "fl1"], ["fl0", "fl1"])
-            mm(wn, T.ip5[:], T.wh[:, 0:192], True, False, ["ip5", "wh"], [BK(sB)])
-            mm(wn, T.in4[:], T.fl[:, 0:192], False, True, ["in4", "fl0"], [BK(sB)], inc=True)
-            mm(dcw, T.ip5[:], T.ch[:], True, False, ["ip5"] + CH, [dB])
-            mm(dcw, T.in5[:], T.wh[:, 0:192], False, False, ["in5", "wh"], [dB])
-            mm(dcw, T.in4[:], T.fl[:, 192:384], False, False, ["in4", "fl1"], [dB])
-            mm(dcw, T.ip4[:], T.fl[:, 0:192], False, True, ["ip4", "fl0"], [dB], inc=True)
+            dall = PB(xB)[:, 0:192]
+            f0, f1, w0 = T.fl[:, 0:192], T.fl[:, 192:384], T.wh[:, 0:192]
+            for out, b, terms in ((wn, BK(sB), (("ip5", w0), ("in4", f0), ("idh", f0))),
+                                  (dall, dB, (("ip5", T.ch[:, 0:192]), ("in5", w0), ("in4", f1), ("idh", f1), ("ip4", f0), ("idn", f0)))):
+                for i, (nm, rhs) in enumerate(terms):
+                    end = i == len(terms) - 1
+                    mm(out, T[nm][:], rhs, i == 0, end, [nm, "wh", "fl0", "fl1"] + CH, [b], inc=end)
 
         def old_names():
-            act(T.t4[:], wn, AF.Identity, [BK(sB)], ["t4"], bias=512.0 * 2048.0)
+            act(T.t4[:], wn, AF.Identity, [BK(sB)], ["t4"], bias=512.0 * 2048.0 + 4095.0 * CEN)
 
         def sum_e(h):
             if r not in half[h]:
@@ -488,10 +547,7 @@ def rank_program(g, core, T, topo):
 
         def rest(h, e):
             if r in half[h]:
-                if e == "a":
-                    act(blk(ra, r, 64), PB(sB)[:, 0:64], AF.Identity, [BK(sB)], ["ro%d" % h], bias=8 * CEN)
-                else:
-                    ts(blk(ra, r, 64), PB(sB)[:, 0:64], 8 * CEN, None, A.add, None, [BK(sB)], ["ro%d" % h])
+                copy(e, blk(ra, r, 64), PB(sB)[:, 0:64], 64, [BK(sB)], ["ro%d" % h])
             send(lambda k: blk(ra, r, 64), blk(ra, r, 64), ["ro%d" % h], ["ra%d" % h], frm=half[h])
 
         def x_part(h, i):
@@ -503,31 +559,36 @@ def rank_program(g, core, T, topo):
 
         def new_x(h):
             off = CEN if t == 0 else -CEN
-            ts(T.xn[:, 256 * h:256 * h + 256], blk(PB(xB), h, 256), off - 8 * CEN, off, A.add, A.max, [BK(xB)], ["xn%d" % h])
+            ts(T.xn[:, 256 * h:256 * h + 256], blk(PB(xB), h, 256), off, off, A.add, A.max, [BK(xB)], ["xn%d" % h])
 
-        def place_x(i, e):
-            dst = (xa, qv[0])[i]
-            if e == "g":
-                op("g", lambda: g.affine_select(dst[0], T.xn[:], [[0, F]], A.is_ge, 0.0, 0, 0), ["xn0", "xn1"], [dst[1]])
-            elif e == "v":
-                cp(dst[0], T.xn[:], ["xn0", "xn1"], [dst[1]])
-            else:
-                act(dst[0], T.xn[:], AF.Copy, ["xn0", "xn1"], [dst[1]])
+        banks, opened = BANKS, set()
 
-        banks = BANKS
+        def win_part(fn, m):
+            fn(m, banks[m], m not in opened)
+            opened.add(m)
 
-        def new_names():
-            ts(T.t2[:], PB(cB)[:, 0:192], 7.5, None, A.is_ge, None, [cK], ["t2"])
-            tt(dcw, T.t2[:], dcw, A.mult, ["t2", dB], [dB])
+        def new_names(p):
+            lo, hi, b = parts[p]
+            d, dK = (dcw[p], dB) if last else (dcw[p], BK(b))
+            ts(T.t2[:, lo:hi], PB(b)[:, lo:hi], 7.5, None, A.is_ge, None, [BK(b)], ["t2_%d" % p])
+            tt(d, T.t2[:, lo:hi], d, A.mult, ["t2_%d" % p, dK], [dK])
             if not last:
-                tt(T.wrep[:, 0:192], T.wh[:, 0:192], dcw, A.add, ["wh", dB], ["wrep0"])
-                spread_names()
+                tt(T.wrep[:, lo:hi], T.wh[:, lo:hi], d, A.add, ["wh", dK], ["wrep0_%d" % p])
             else:
-                tt(T.wf[:], T.t4[:], dcw, A.add, [dB, "t4"], ["wf"])
-                dma("s", T.dw[:], T.wf[:], ["wf"], ["dw"])
-                dma("s", T.lw[r], T.wf[own, :], ["wf"], ["lw0"])
-                send(lambda k: T.dw[k], T.lw[r], ["dw"], ["lw"])
-                dma("s", T.yn[:], T.lw[:], ["lw", "lw0"], ["yn"])
+                tt(T.wf[:, lo:hi], T.t4[:, lo:hi], d, A.add, [dK, "t4"], ["wf%d" % p])
+
+        def names_home(p):
+            lo, hi, _ = parts[p]
+            dw, lw = T["dw%d" % p], T["lw%d" % p]
+            dma("s", dw[:], T.wf[:, lo:hi], ["wf%d" % p], ["dw%d" % p])
+            dma("s", T.yn[own, lo:hi], T.wf[own, lo:hi], ["wf%d" % p], ["yo%d" % p])
+            send(lambda k: dw[k], lw[r], ["dw%d" % p], ["lw%d" % p])
+
+        def names_out(p):
+            lo, hi, _ = parts[p]
+            for a, b in ((0, r), (r + 1, NR)):
+                if a < b:
+                    dma("sa"[a > 0], T.yn[16 * a:16 * b, lo:hi], T["lw%d" % p][a:b], ["lw%d" % p], ["yn%d_%d" % (p, a)])
 
         def squares():
             act(T.sq[:], T.sg[:], AF.Square, ["sg", "sg0"], ["sq"], bias=CEN / 64.0, scale=1.0 / 64.0)
@@ -539,11 +600,12 @@ def rank_program(g, core, T, topo):
             dma("a", T.yd[:], T.ydt[:], ["ydt"], ["yd"])
 
         steps = {"G": gather_v, "C": conv, "T": twin, "L": level, "E": median_out, "H": chain, "CH": challengers,
-                 "HP": name_part, "HO": offsets, "NL": name_list,
+                 "Z": zero_count, "HP": name_part, "HO": offsets, "NL": name_list,
                  "SV": sub_v, "AV": abs_v, "U": gather_u, "SU": sub_u, "AU": abs_u, "K": cmp, "N": count,
                  "VD": void_twice, "VE": void_eq, "VC": void_count, "FL": eighths, "DC": change, "ON": old_names,
-                 "SUM": sum_e, "R": rest, "XP": x_part, "X": new_x, "NA": minus_x, "NN": new_names, "SQ": squares,
-                 "W": lambda m: win_x(m, banks[m]), "O": lambda m: win_out(m, banks[m], 0.0), "PX": place_x}
+                 "SUM": sum_e, "R": rest, "XP": x_part, "X": new_x, "NA": minus_x, "NN": new_names, "S": spread, "NH": names_home, "NO": names_out, "SQ": squares,
+                 "W": lambda m: win_part(win_x, m), "M": lambda m: win_part(win_n, m),
+                 "O": lambda m, e: win_out(m, banks[m], e), "PX": place_x}
         for w in plan:
             name = w.rstrip("0123456789avg")
             steps[name](*[int(c) if c.isdigit() else c for c in w[len(name):]])

from concourse.bass import DstId, RemoteDMATransfer
from concourse.mybir import AluOpType as A, ActivationFunctionType as AF

NR, F, NM, ROUNDS = 8, 512, 6, 3
MAG = 12582912.0
CEN = 1280.0
BIG = 8192.0
PLAN = ("G02v G12a C02g G22v C12v C22v G32a C32a L10 L11 L20 H0 T20g T10g G42a C41g T11g G52a C51g T21g C40a C50a L30 "
        "SV1 SV0 AV0 AV1 HP05 HO0 U1a SV2 AV2 U0a U2a L40 E0 L21 SU1 H1 HP15 SV3 AV3 L31 SU0 CH0v L41 HO1 E1 CH1v DC "
        "SUM0 Z1 AU0 SV5 SU2 VDg U4v AU1 AU2 R0v U3v VE2 AU3 VE1 VE5 VE4 XP00 Z0 VC2 AU4 AV5 VC1 VC4 SUM1 SV4 AV4 K1 "
        "VE3 K0 N0 R1v K3 K2 U5v VE0 N1 XP01 VC3 VC5 VC0 AU5 X0 W3 W0 K4 K5 N2 XP10 W2 NN0 XP11 W1 NN1 X1 S01a S05a "
        "S16a W5 W6 S15v S13v S14v S12v NL S11v S17a S06a S02a S03g S07a S04g M2 M1 O2a M6 M3 O1v O3v W4 M5 O5v O6a "
        "NA M4 O4a W7 M0 O0a PX1g PX0g M7 O7v ")
LAST = ("G12a G02v C02g SV0 G22v C22v FL0v C12v SV1 T12g G32a G52a C32a C52g T22g L12 H0 G42a AV0 SV2 AV1 C42a HP05 "
        "SV3 AV2 L22 HO0 U0a SV4 L32 H1 SU0 HP16 L42 HO1 CH0v U1a SU1 AU0 AV3 SV5 U2a U3a SU2 K0 CH1v U5v VDg E2 VE2 "
        "FL1v VE0 VE4 U4v AV5 AU1 VE5 K1 SU3 AU3 K3 AU2 K2 AU4 AV4 VE3 VE1 DC Z0 N0 Z1 VC2 VC5 VC4 VC3 N1 VC1 VC0 K4 "
        "AU5 K5 ON N2 NN0 NH0 NN1 NH1 SQ NO0 NO1 ")
BANKS = [0, 1, 2, 3, 6, 7, 5, 4]
SPLIT = [3, 3]
STRICT = True

SCRATCH = {
    "dx": ("dram", [8, 128, 64], "bfloat16"),
    "dn": ("dram", [8, 128, 24], "int32"), "ln": ("dram", [8, 128, 24], "int32"),
    "dm": ("dram", [128, 64], "bfloat16"), "lm": ("dram", [8, 128, 64], "bfloat16"),
    "de": ("dram", [8, 128, 64], "float16"),
    "dw0": ("dram", [8, 128, 16], "float32"), "lw0": ("dram", [8, 128, 16], "float32"),
    "dw1": ("dram", [8, 128, 8], "float32"), "lw1": ("dram", [8, 128, 8], "float32"),
    "io1": ("sbuf", [128, 128], "int32"), "io2": ("sbuf", [128, 128], "int32"), "io3": ("sbuf", [128, 32], "float32"),
    "io4": ("sbuf", [128, 128], "int32"),
    "tq": ("sbuf", [128, 128], "int32"), "tk": ("sbuf", [128, 8], "int32"), "col": ("sbuf", [128, 8], "float32"),
    "b8": ("sbuf", [128, 8], "float32"), "jf": ("sbuf", [128, 128], "float32"),
    "idh": ("sbuf", [128, 128], "float16"), "idn": ("sbuf", [128, 128], "float16"),
    "idh8": ("sbuf", [128, 128], "float16"), "id1": ("sbuf", [128, 128], "bfloat16"),
    "id8": ("sbuf", [128, 128], "bfloat16"), "idm16": ("sbuf", [128, 128], "bfloat16"),
    "idp": ("sbuf", [128, 128], "float16"), "selk": ("sbuf", [128, 1024], "float16"),
    "selw": ("sbuf", [128, 1024], "bfloat16"),
    "idf": ("sbuf", [128, 128], "float32"), "idm": ("sbuf", [128, 128], "bfloat16"),
    "ip5": ("sbuf", [128, 128], "float16"), "in5": ("sbuf", [128, 128], "float16"),
    "ip4": ("sbuf", [128, 128], "float16"), "in4": ("sbuf", [128, 128], "float16"),
    "ipm": ("sbuf", [128, 128], "bfloat16"), "inm": ("sbuf", [128, 128], "bfloat16"),
    "ipk": ("sbuf", [128, 128], "float32"), "ink": ("sbuf", [128, 128], "float32"),
    "fl": ("sbuf", [128, 384], "float16"),
    "ones": ("sbuf", [128, 512], "bfloat16"),
    "zq": ("sbuf", [128, 144], "bfloat16"), "zero": ("sbuf", [128, 512], "float32"),
    "cst": ("sbuf", [128, 2560], "float16"),
    "win": ("sbuf", [128, 4096], "float32"),
    "xl": ("sbuf", [128, 512], "bfloat16"), "xb": ("sbuf", [128, 512], "bfloat16"),
    "nbi": ("sbuf", [128, 192], "int32"), "t1": ("sbuf", [128, 192], "int32"), "t2": ("sbuf", [128, 192], "float32"),
    "t3": ("sbuf", [128, 192], "float32"), "t4": ("sbuf", [128, 192], "float32"),
    "wh": ("sbuf", [128, 576], "float16"), "wl": ("sbuf", [128, 192], "uint16"),
    "wrep": ("sbuf", [128, 4096], "float16"),
    "vv": ("sbuf", [128, 3072], "float32"), "uu": ("sbuf", [128, 3072], "float16"),
    "bv": ("sbuf", [128, 3072], "float32"), "uw": ("sbuf", [128, 3072], "float32"),
    "bh": ("sbuf", [128, 3072], "float16"), "ah": ("sbuf", [128, 3072], "float16"),
    "na": ("sbuf", [128, 512], "float32"), "xn": ("sbuf", [128, 512], "float16"),
    "pv": ("sbuf", [128, 2560], "float16"), "qv": ("sbuf", [128, 2568], "float16"),
    "m1": ("sbuf", [128, 2568], "float16"), "m2": ("sbuf", [128, 2560], "float16"),
    "near": ("sbuf", [128, 3072], "bfloat16"),
    "ct": ("sbuf", [128, 192], "float32"), "cw": ("sbuf", [128, 192], "float32"),
    "cj": ("sbuf", [128, 192], "int32"), "ci": ("sbuf", [128, 192], "int32"), "cl": ("sbuf", [128, 192], "uint16"),
    "ch": ("sbuf", [128, 384], "float16"), "eq": ("sbuf", [128, 1632], "bfloat16"),
    "mixc": ("sbuf", [128, 64], "bfloat16"),
    "e0": ("sbuf", [128, 512], "float16"), "e1": ("sbuf", [128, 512], "float16"),
    "lr0": ("sbuf", [128, 512], "float16"), "lr1": ("sbuf", [128, 512], "float16"),
    "ra0": ("sbuf", [128, 512], "float16"), "ra1": ("sbuf", [128, 512], "float16"),
    "e2": ("sbuf", [128, 512], "float16"), "sq": ("sbuf", [128, 512], "float32"),
    "sg": ("sbuf", [128, 512], "float16"), "ydt": ("sbuf", [128, 64], "float32"),
    "wf": ("sbuf", [128, 192], "float32"),
}
for _b in range(8):
    SCRATCH["pb%d" % _b] = ("psum", [128, 512], "float32")
SEMAPHORES = ["qv", "qa", "qp", "qg"] + ["s%d" % _i for _i in range(100)]


def rank_program(g, core, T, topo):
    r = T.rank_of(core)
    if r is None:
        return
    cores = list(T.cores)
    peers = [(r + d) % NR for d in range(1, NR)]
    Q = {"v": g.vector, "a": g.scalar, "p": g.tensor, "g": g, "s": g.sync}
    V, ACT, PE = g.vector, g.scalar, g.tensor
    cnt = {"qv": 0, "qa": 0, "qp": 0, "qg": 0}
    seen = {e: {} for e in Q}
    wr, rd, known, nsem = {}, {}, {}, [0]

    def newsem():
        nsem[0] += 1
        cnt["s%d" % (nsem[0] - 1)] = 0
        return "s%d" % (nsem[0] - 1)

    def deps(e, R, W, dma):
        need = {}

        def add(tok, raw):
            if tok[2] == e and not dma and (e == "p" or not (raw or STRICT)):
                return
            need[tok[0]] = max(need.get(tok[0], 0), tok[1])
        for k in R:
            for tok in wr.get(k, []):
                add(tok, True)
            if k[0] == "B":
                for tok in rd.get(k, []):
                    if tok[2] != e:
                        add(tok, False)
        for k in W:
            for tok in wr.get(k, []) + rd.get(k, []):
                add(tok, False)
        todo = {s: val for s, val in need.items() if seen[e].get(s, 0) < val}
        for s, val in todo.items():
            if not any(known.get((o, w), {}).get(s, 0) >= val for o, w in todo.items() if o != s):
                Q[e].wait_ge(T.sem[s], val)
        for s, val in todo.items():
            for o, w in list(known.get((s, val), {}).items()) + [(s, val)]:
                seen[e][o] = max(seen[e].get(o, 0), w)

    def vouch(tok, e):
        old = known.setdefault(tok[:2], {})
        for o, w in seen[e].items():
            old[o] = max(old.get(o, 0), w)

    def note(tok, R, W):
        for k in R:
            rd.setdefault(k, []).append(tok)
        for k in W:
            wr[k] = [tok]
            rd[k] = []

    def op(e, f, R, W, inc=True):
        deps(e, R, W, False)
        ins = f()
        s = "q" + e
        tok = (s, cnt[s] + 1, e)
        if inc:
            ins.then_inc(T.sem[s], 1)
            cnt[s] += 1
        vouch(tok, e)
        note(tok, R, W)

    def dma(e, out, in_, R, W, sem=None, total=16, **kw):
        deps(e, R, W, True)
        s = sem or newsem()
        Q[e].dma_start(out, in_, **kw).then_inc(T.sem[s], 16)
        cnt[s] += 16
        vouch((s, total), e)
        note((s, total, "d"), R, W)

    def send(src, dst, R, W, frm=range(NR), to=range(NR)):
        rs, ls = newsem(), newsem()
        ne = len(topo.engines(core, cores[peers[0]])) // len(to)
        if r in frm:
            deps("g", R, [], True)
            tr = []
            for i, k in enumerate(k for k in peers if k in to):
                rid, pid, _ = topo.addr(cores[k])
                eng = topo.engines(core, cores[k])[i::len(to)]
                tr.append(RemoteDMATransfer(dst_ids=[DstId(rid=rid, pnc=pid)], dma_engine_mask=sum(1 << e for e in eng),
                                            remote_sem=T.sem[rs], src=src(k), dst=dst))
            g.remote_dma_fused(tr, local_sem=T.sem[ls])
            cnt[ls] = ne * len(tr)
            note((ls, cnt[ls], "d"), R, [])
        if r in to:
            cnt[rs] = ne * len([k for k in peers if k in frm])
            note((rs, cnt[rs], "d"), [], W)

    def ts(out, in0, s1, s2, o0, o1, R, W):
        if s2 is None:
            op("v", lambda: V.tensor_scalar(out, in0, s1, None, o0), R, W)
        else:
            op("v", lambda: V.tensor_scalar(out, in0, s1, s2, o0, o1), R, W)

    def tt(out, in0, in1, o, R, W):
        op("v", lambda: V.tensor_tensor(out, in0, in1, o), R, W)

    def cp(out, in_, R, W):
        op("v", lambda: V.tensor_copy(out, in_), R, W)

    def act(out, in_, fn, R, W, bias=0.0, scale=1.0):
        op("a", lambda: ACT.activation(out, in_, fn, bias=bias, scale=scale), R, W)

    def mm(out, lhsT, rhs, start, stop, R, W, inc=False):
        op("p", lambda: PE.matmul(out, lhsT, rhs, start, stop), R, W, inc)

    def blk(t, j, w=F):
        return t[:, j * w:(j + 1) * w]

    def PB(b):
        return T["pb%d" % b]

    def BK(b):
        return "B%d" % b

    own = slice(16 * r, 16 * r + 16)

    dma("s", T.dn[:], T.nb[:], [], ["dn"])
    dma("a", T.dx[:], T.x[:], [], ["dx"])
    dma("s", T.ln[r], T.nb[own, :], [], ["ln0"])
    dma("a", blk(T.xl, r, 64), T.x[own, :], [], ["xl0"])
    dma("s", T.dm[:], T.mix[:], [], ["dm"])
    dma("a", T.lm[r], T.mix[:], [], ["lm0"])
    op("g", lambda: g.iota(T.io1[:], [[-1, 128]], 0, 1), [], ["io1"])
    op("g", lambda: g.iota(T.io4[:], [[0, 8], [-8, 16]], 0, 1), [], ["io4"])
    op("g", lambda: g.iota(T.io2[:], [[-1, 16], [-16, 8]], 0, 1), [], ["io2"])
    op("g", lambda: g.iota(T.io3[:], [[128, 32]], -2048, 0, allow_small_or_imprecise_dtypes=True), [], ["io3"])
    send(lambda k: T.dn[k], T.ln[r], ["dn"], ["ln"])
    send(lambda k: T.dx[k], blk(T.xl, r, 64), ["dx"], ["xl"])
    send(lambda k: T.dm[:], T.lm[r], ["dm", "xl"], ["lm"])
    dma("s", T.nbi[:], T.ln[:], ["ln", "ln0"], ["nbi"])
    xs = newsem()
    for k in range(8):
        dma("s", T.xb[16 * k:16 * k + 16, :], blk(T.xl, k, 64), ["xl", "xl0"], ["xb%d" % k], sem=xs, total=128)
    dma("s", T.mixc[:], T.lm[:, r::8, :], ["lm", "lm0"], ["mixc"])

    op("v", lambda: V.memset(T.zero[:], 0.0), [], ["zero"])
    op("v", lambda: V.memset(T.zq[:], 0.0), [], ["zq"])
    ts(T.tq[:], T.io1[:], 15, None, A.bitwise_and, None, ["io1"], ["tq"])
    ts(T.tk[:], T.io1[:, 0::16], 4, None, A.arith_shift_right, None, ["io1"], ["tk"])
    cp(T.wrep[:, 192:512], T.zero[:, 192:512], ["zero"], ["wpad0"])
    ts(T.idh[:], T.io1[:], 0.0, None, A.is_equal, None, ["io1"], ["idh"])
    for k in range(1, 8):
        act(T.wrep[:, 512 * k + 192:512 * k + 512], T.wrep[:, 192:512], AF.Copy, ["wpad0"], ["wpad%d" % k])
    for k in range(8):
        ts(blk(T.selw, k, 128), T.io4[:], float(k), None, A.is_equal, None, ["io4"], ["selw%d" % k])
    for nm, val in (("idn", -1.0), ("idh8", 8.0), ("id1", 1.0), ("id8", 8.0), ("idm16", -16.0), ("idf", 1.0),
                    ("ipm", 8192 * MAG), ("inm", -8192 * MAG), ("ipk", 8192.0), ("ink", -8192.0),
                    ("idm", -MAG), ("ip5", 512.0), ("in5", -512.0), ("ip4", 4096.0), ("in4", -4096.0)):
        ts(T[nm][:], T.io1[:], 0.0, val, A.is_equal, A.mult, ["io1"], [nm])
    ts(T.idp[:], T.io2[:], 0.0, 2.0 ** -13, A.is_equal, A.mult, ["io2"], ["idp"])
    op("v", lambda: V.memset(T.ones[:], 1.0), [], ["ones"])
    ts(T.jf[:], T.tq[:], 0.0, None, A.is_equal, None, ["tq"], ["jf"])
    ts(T.b8[:], T.tk[:], 0.0, None, A.is_equal, None, ["tk"], ["b8"])
    ts(T.col[:, 0:1], T.tq[:, 0:1], 8.0, None, A.mult, None, ["tq"], ["col0"])
    cp(T.col[:, 1:2], T.tk[:, 0:1], ["tk"], ["col1"])
    cp(T.zq[:, 15:128:16], T.b8[:], ["b8", "zq"], ["zq"])
    for k in range(8):
        ts(blk(T.selk, k, 128), T.jf[:], T.b8[:, k:k + 1], None, A.mult, None, ["jf", "b8"], ["selk%d" % k])
    for c in (192, 416):
        ts(T.wh[:, c:c + 32], T.io3[:], T.col[:, 0:1], T.col[:, 1:2], A.add, A.add, ["io3", "col0", "col1"], ["wF"])
    for i in range(5):
        act(T.cst[:, i::5], T.zero[:], AF.Identity, ["zero"], ["cst%d" % i], bias=BIG if i < 4 else -BIG)
    act(T.m1[:, 0:8], T.zero[:, 0:8], AF.Identity, ["zero"], ["m1"], bias=-BIG)
    note(wr["m1"][0], [], ["m1_0"])
    act(T.qv[:, 0:1], T.zero[:, 0:1], AF.Copy, ["zero"], ["qpad"])
    CST = ["cst%d" % k for k in range(5)]
    span = [(0, F // 2), (F // 2, F), (0, F)]

    def halves(key, h):
        return [key + "_%d" % i for i in ((0, 1) if h == 2 else (h,))]

    def place(w, h=2):
        buf, i = w
        lo, hi = span[h]
        c = i + (buf == "qv")
        return T[buf][:, 5 * lo + c:5 * hi + (buf == "qv"):5], halves("%s%d" % w, h)

    home = [("pv", 0), ("pv", 1), ("pv", 3), ("pv", 4), ("qv", 3), ("qv", 4)]
    xa = place(("pv", 2))

    for w in (("pv", 4), ("qv", 4)):
        act(place(w)[0], T.zero[:], AF.Copy, ["zero"], place(w)[1])

    def copy(e, out, src, n, R, W):
        if e == "g":
            op("g", lambda: g.affine_select(out, src, [[0, n]], A.is_ge, 0.0, 0, 0), R, W)
        elif e == "v":
            cp(out, src, R, W)
        else:
            act(out, src, AF.Copy, R, W)

    def twin(i, h, e):
        src, dst = place(("pv", i + 2), h), place(("qv", i), h)
        copy(e, dst[0], src[0], span[h][1] - span[h][0], src[1], dst[1])

    SELK = ["selk%d" % k for k in range(8)]
    SELW = ["selw%d" % k for k in range(8)]
    WREP = ["wpad%d" % k for k in range(8)] + [key for k in range(8) for key in halves("wrep%d" % k, 2)]
    WIN = ["win%d" % m for m in range(8)]

    def win_n(m, b, first):
        for i in range(4):
            end = i == 3 and not first
            mm(blk(PB(b), i, 128), T.wrep[:, 4 * m + i::32], T.idp[:], first and i == 0, end, WREP + ["idp"], [BK(b)], inc=end)

    def win_x(m, b, first):
        for k in range(8):
            end = k == 7 and not first
            mm(PB(b)[:, k::8], blk(T.selk, k, 128), blk(T.xn, m, 64), first and k == 0, end,
               ["xn%d" % (m // 4)] + SELK, [BK(b)], inc=end)

    def win_x0(m, b):
        for k in range(8):
            mm(PB(b)[:, k::8], blk(T.selw, m, 128), blk(T.xl, k, 64), k == 0, False, ["xl", "xl0"] + SELW, [BK(b)])

    def win_out(m, b, e, add=0.0):
        if e == "a":
            act(blk(T.win, m), PB(b)[:], AF.Identity, [BK(b)], ["win%d" % m], bias=add)
        else:
            ts(blk(T.win, m), PB(b)[:], add, None, A.add, None, [BK(b)], ["win%d" % m])

    def spread(p, k, e):
        lo, hi = [(0, 128), (128, 192), (0, 192)][p]
        copy(e, T.wrep[:, 512 * k + lo:512 * k + hi], T.wrep[:, lo:hi], hi - lo, halves("wrep0", p), halves("wrep%d" % k, p))

    def name_list():
        R = halves("wrep0", 2)
        ts(T.wl[:], T.wrep[:, 0:192], 2048.0, None, A.add, None, R, ["wl"])
        dma("s", T.wh[:, 0:192], T.wrep[:, 0:192], R, ["wh"])
        dma("s", T.wh[:, 224:416], T.wrep[:, 0:192], R, ["wh2"])
        dma("s", T.wh[:, 448:576], T.wrep[:, 0:128], R, ["wh3"])

    D, U, xB, sB, cB = [0, 1], [2, 3, 4], 5, 6, 7
    for m in range(7):
        win_x0(m, m)
    ts(T.t1[:], T.nbi[:], 9, None, A.arith_shift_right, None, ["nbi"], ["t1"])
    ts(T.t3[:], T.nbi[:], 8.0, -2048.0, A.mult, A.add, ["nbi"], ["t3"])
    ts(PB(7)[:, 0:192], T.t1[:], -4095.0, None, A.mult, None, ["t1"], [BK(7)])
    tt(T.wrep[:, 0:192], T.t3[:], PB(7)[:, 0:192], A.add, [BK(7), "t3"], halves("wrep0", 2))
    win_x0(7, 7)
    for k in range(1, 8):
        spread(2, k, "v" if k < 6 else "a")
    name_list()
    XB = ["xb%d" % k for k in range(8)]
    ts(T.xn[:], T.xb[:], CEN, None, A.add, None, XB, ["xn0", "xn1"])
    act(T.na[:], T.xb[:], AF.Identity, XB, ["na"], bias=MAG - CEN, scale=-1.0)
    for m in range(8):
        win_n(m, m, False)
        win_out(m, m, "av"[m % 2], CEN)

    def place_x(i, e):
        dst = (xa, place(("qv", 0)))[i]
        copy(e, dst[0], T.xn[:], F, ["xn0", "xn1"], dst[1])

    place_x(0, "g")
    place_x(1, "g")

    def minus_x():
        act(T.na[:], T.xn[:], AF.Identity, ["xn0", "xn1"], ["na"], bias=MAG, scale=-1.0)

    for t in range(ROUNDS):
        last = t == ROUNDS - 1
        cK = BK(cB)
        csem = [newsem(), newsem()]
        rough = set()
        plan = (LAST if last else PLAN).split()
        et = T["e%d" % t]
        lr, ra = T["lr%d" % min(t, 1)], T["ra%d" % min(t, 1)]

        got = {}
        sp = SPLIT[last]
        cut = [slice(0, 32 * sp), slice(32 * sp, 192)]
        DV = [D[j % 2] for j in range(NM)]
        DU = [U[j % (3 if last else 2)] for j in range(NM)]

        def gather_v(j, h, e):
            lo, hi = span[h]
            src = T.win[:, 0:4096].indirect(T.wl[:, 32 * j + lo // 16:32 * j + hi // 16])
            copy(e, T.vv[:, F * j + lo:F * j + hi], src, hi - lo, WIN + ["wl"], halves("v%d" % j, h))
            got[j] = got.get(j, 0) + hi - lo
            b = (j + t) % NM
            for i in range(2 if got[j] == F else 0):
                dma("s", T.ct[:, 32 * j + 16 * i:32 * j + 16 * i + 16], T.vv[16 * i + b::32, j * F:(j + 1) * F],
                    halves("v%d" % j, 2), ["ct%d_%d" % (j, i)], sem=csem[j // sp], total=32 * (sp, NM - sp)[j // sp])

        def narrow(out, src, n, R, W, e):
            if last and e == "v":
                ts(out, src, MAG, -MAG, A.add, A.add, R, W)
            else:
                copy(e, out, src, n, R, W)
                rough.update(W if last else [])

        def conv(j, h, e):
            lo, hi = span[h]
            dst = place(home[j], h)
            narrow(dst[0], T.vv[:, F * j + lo:F * j + hi], hi - lo, halves("v%d" % j, h), dst[1], e)

        def gather_u(j, e):
            src, R = T.win[:, 0:4096].indirect(blk(T.cl, j, 32)), WIN + ["cl%d" % (j // sp)]
            if e == "v":
                tt(blk(T.uw, j), src, T.na[:], A.add, R + ["na"], ["u%d" % j])
                wide.add(j)
            else:
                narrow(blk(T.uu, j), src, F, R, ["u%d" % j], e)

        def less_a(b, src, keys):
            ro = bool(rough & set(keys))
            if ro:
                mm(PB(b)[:], T.idm[:], T.ones[:], True, False, ["idm", "ones"], [BK(b)])
            mm(PB(b)[:], T.idh[:], src, not ro, False, ["idh"] + keys, [BK(b)])
            mm(PB(b)[:], T.idn[:], xa[0], False, True, ["idn"] + xa[1], [BK(b)], inc=True)
            return MAG if ro else 0.0

        back_u, back_v, wide = {}, {}, set()

        def sub_v(j):
            back_v[j] = less_a(DV[j], *place(home[j]))

        def abs_v(j):
            b = DV[j]
            act(blk(T.bv if last else T.bh, j), PB(b)[:], AF.Abs, [BK(b)], ["bv%d" % j], bias=back_v[j])

        def sub_u(j):
            back_u[j] = less_a(DU[j], blk(T.uu, j), ["u%d" % j])

        def abs_u(j):
            b = DU[j]
            out, W = (PB(b)[:], [BK(b)]) if last else (blk(T.ah, j), ["au%d" % j])
            if j in wide:
                act(out, blk(T.uw, j), AF.Abs, ["u%d" % j], W, bias=-MAG)
            else:
                act(out, PB(b)[:], AF.Abs, [BK(b)], W, bias=back_u[j])

        def cmp(j):
            b = DU[j]
            if last:
                tt(blk(T.near, j), blk(T.bv, j), PB(b)[:], A.is_gt, ["bv%d" % j, BK(b)], ["near%d" % j])
            else:
                tt(blk(T.near, j), blk(T.bh, j), blk(T.ah, j), A.is_gt, ["bv%d" % j, "au%d" % j], ["near%d" % j])

        def level(k, h):
            lo, hi = span[h]
            c0, c1 = slice(5 * lo, 5 * hi), slice(5 * lo + 1, 5 * hi + 1)
            m1, m2, seam = halves("m1", h), halves("m2", h), ["seam"]
            out, d0, d1, R, W = [
                (T.m1[:, c1], T.pv[:, c0], T.cst[:, c0], CST, m1 + seam * (h == 0)),
                (T.m2[:, c0], T.pv[:, c0], T.m1[:, c0], m1 + seam * (h == 1), m2),
                (T.m1[:, c0], T.qv[:, c0], T.m2[:, c0], m2 + ["qpad", "qv4_0"], m1 + seam * (h == 1)),
                (T.m2[:, c0], T.qv[:, c1], T.m1[:, c0], m1, m2)][k - 1]
            data = [key for i in range(5) for key in place(("pv" if k < 3 else "qv", i), h)[1]]
            op("v", lambda: V.tensor_tensor_scan(out, d0, d1, -BIG, A.max, A.min), R + data, W)

        def chain(h):
            c = cut[h]
            op("v", lambda: V.transpose(T.cw[:, c], T.ct[:, c]),
               ["ct%d_%d" % (j, i) for j in range(NM) if j // sp == h for i in range(2)], ["cw%d" % h])

        HB = {}

        def name_part(h, b):
            c, HB[h] = cut[h], b
            for i, (lhs, rhs) in enumerate(((T.ipm, T.ones[:, c]), (T.ipk, T.cw[:, c]),
                                            (T.inm, T.ones[:, c]), (T.ink, T.cw[:, c]))):
                mm(PB(b)[:, c], lhs[:], rhs, i == 0, i == 3, ["ipm", "ipk", "inm", "ink", "ones", "cw%d" % h], [BK(b)],
                   inc=(i == 3))

        def offsets(h):
            ts(T.cl[:, cut[h]], PB(HB[h])[:, cut[h]], -1.0, 2048.0, A.mult, A.add, [BK(HB[h])], ["cl%d" % h])

        def challengers(h, e):
            if e == "a":
                act(T.ch[:, cut[h]], PB(HB[h])[:, cut[h]], AF.Identity, [BK(HB[h])], ["ch%d" % h], scale=-1.0)
            else:
                ts(T.ch[:, cut[h]], T.cl[:, cut[h]], -2048.0, None, A.add, None, ["cl%d" % h], ["ch%d" % h])

        CH = ["ch0", "ch1"]

        parts = [(0, 128, cB), (128, 192, D[1] if last else U[2])]
        sums = [[w for w in plan if w[:2] in ("VC",) + n] for n in (("N0", "N1"), ("N2",))]

        def zero_count(p):
            lo, hi, b = parts[p]
            mm(PB(b)[:, lo:hi], T.idh[:], T.wrep[:, 192 + lo:192 + hi], True, False, ["idh", "wpad0"], [BK(b)])

        def count(h):
            w, p = "N%d" % h, h // 2
            b = parts[p][2]
            for q in range(16):
                mm(PB(b)[:, 64 * h:64 * h + 64], T.zq[:, 15 - q:143 - q], T.near[:, 1024 * h + q:1024 * h + 1024:16],
                   False, w == sums[p][-1] and q == 15,
                   ["zq", "near%d" % (2 * h), "near%d" % (2 * h + 1)], [BK(b)], inc=(q == 15))

        def void_twice(e):
            copy(e, T.ch[:, 192:384], T.ch[:, 0:192], 192, CH, ["chh"])

        def eq_at(c):
            return (384 * c, 384) if c < 3 else (576 + 192 * c, 192 if c < 5 else 96)

        def void_eq(c):
            pos, wd = eq_at(c)
            if c < 3:
                tt(T.eq[:, pos:pos + wd], T.wh[:, 64 * c + 64:64 * c + 448], T.ch[:], A.is_equal,
                   ["wh", "wh2", "wh3", "wF", "chh"] + CH, ["eq%d" % c])
            else:
                d = 32 * (c - 2)
                tt(T.eq[:, pos:pos + wd], T.ch[:, 0:wd], T.ch[:, d:d + wd], A.is_equal, CH + ["chh"], ["eq%d" % c])

        def void_count(c):
            pos, w, d = eq_at(c)[0], "VC%d" % c, 32 * (c - 2)
            runs = [(0, 0), (192, 0)] if c < 3 else [(0, d), (192 - d, 192 - d)][:1 if c == 5 else 2]
            for p, (lo, hi, b) in enumerate(parts):
                cut = [(src + max(lo, dst) - dst, max(lo, dst)) for src, dst in runs if dst < hi]
                for i, (src, dst) in enumerate(cut):
                    end = i == len(cut) - 1
                    mm(PB(b)[:, dst:hi], T.idm16[:], T.eq[:, pos + src:pos + src + hi - dst], False,
                       w == sums[p][-1] and end, ["eq%d" % c, "idm16"], [BK(b)], inc=end)

        half = [range(0, NR // 2), range(NR // 2, NR)]

        def median_out(h, e="v"):
            if not last:
                src = T.m2[:, 1280 * h + 4:1280 * h + 1280:5]
                if e == "a":
                    act(blk(et, h, 256), src, AF.Identity, halves("m2", h), ["e%d" % h], bias=-CEN)
                else:
                    ts(blk(et, h, 256), src, -CEN, None, A.add, None, halves("m2", h), ["e%d" % h])
                send(lambda k: blk(et, k, 64), blk(lr, r, 64), ["e%d" % h], ["lr%d" % t], to=half[h])
            else:
                ts(et[:], T.m2[:, 4::5], MAG, -MAG, A.add, A.add, halves("m2", 2), ["e"])
                dma("s", T.de[:], et[:], ["e"], ["de"])
                dma("s", blk(T.sg, r, 64), et[own, :], ["e"], ["sg0"])
                send(lambda k: T.de[k], blk(T.sg, r, 64), ["de"], ["sg"])

        dB, wn = BK(xB), PB(sB)[:, 0:192]
        dcw = [PB(xB)[:, lo:hi] if last else PB(b)[:, 192 + lo:192 + hi] for lo, hi, b in parts]

        def eighths(i, e):
            src, R = ((T.wh[:, 0:192], ["wh"]), (T.ch[:, 0:192], CH))[i]
            if e == "a":
                act(blk(T.fl, i, 192), src, AF.Identity, R, ["fl%d" % i], bias=CEN + 255.5625, scale=0.125)
            else:
                ts(blk(T.fl, i, 192), src, 0.125, CEN + 255.5625, A.mult, A.add, R, ["fl%d" % i])

        def change():
            if not last:
                for p, (lo, hi, b) in enumerate(parts):
                    mm(dcw[p], T.idh[:], T.ch[:, lo:hi], True, False, ["idh"] + CH, [BK(b)])
                    mm(dcw[p], T.idn[:], T.wh[:, lo:hi], False, True, ["idn", "wh"], [BK(b)], inc=True)
                return
            dall = PB(xB)[:, 0:192]
            f0, f1, w0 = T.fl[:, 0:192], T.fl[:, 192:384], T.wh[:, 0:192]
            for out, b, terms in ((wn, BK(sB), (("ip5", w0), ("in4", f0), ("idh", f0))),
                                  (dall, dB, (("ip5", T.ch[:, 0:192]), ("in5", w0), ("in4", f1), ("idh", f1), ("ip4", f0), ("idn", f0)))):
                for i, (nm, rhs) in enumerate(terms):
                    end = i == len(terms) - 1
                    mm(out, T[nm][:], rhs, i == 0, end, [nm, "wh", "fl0", "fl1"] + CH, [b], inc=end)

        def old_names():
            act(T.t4[:], wn, AF.Identity, [BK(sB)], ["t4"], bias=512.0 * 2048.0 + 4095.0 * CEN)

        def sum_e(h):
            if r not in half[h]:
                return
            mm(PB(sB)[:, 0:64], (T.id1 if t == 0 else T.id8)[:], T.mixc[:], True, False, ["id1", "id8", "mixc"], [BK(sB)])
            for k in range(8):
                src = blk(et, r, 64) if k == r else blk(lr, k, 64)
                mm(PB(sB)[:, 0:64], T.idn[:], src, False, k == 7, ["idn", "e%d" % h, "lr%d" % t], [BK(sB)], inc=(k == 7))

        def rest(h, e):
            if r in half[h]:
                copy(e, blk(ra, r, 64), PB(sB)[:, 0:64], 64, [BK(sB)], ["ro%d" % h])
            send(lambda k: blk(ra, r, 64), blk(ra, r, 64), ["ro%d" % h], ["ra%d" % h], frm=half[h])

        def x_part(h, i):
            out = blk(PB(xB), h, 256)
            if i == 0:
                mm(out, T.idh8[:], blk(et, h, 256), True, False, ["idh8", "e%d" % h], [BK(xB)])
            else:
                mm(out, T.idh[:], blk(ra, h, 256), False, True, ["idh", "ra%d" % h, "ro%d" % h], [BK(xB)], inc=True)

        def new_x(h):
            off = CEN if t == 0 else -CEN
            ts(T.xn[:, 256 * h:256 * h + 256], blk(PB(xB), h, 256), off, off, A.add, A.max, [BK(xB)], ["xn%d" % h])

        banks, opened = BANKS, set()

        def win_part(fn, m):
            fn(m, banks[m], m not in opened)
            opened.add(m)

        def new_names(p):
            lo, hi, b = parts[p]
            d, dK = (dcw[p], dB) if last else (dcw[p], BK(b))
            ts(T.t2[:, lo:hi], PB(b)[:, lo:hi], 7.5, None, A.is_ge, None, [BK(b)], ["t2_%d" % p])
            tt(d, T.t2[:, lo:hi], d, A.mult, ["t2_%d" % p, dK], [dK])
            if not last:
                tt(T.wrep[:, lo:hi], T.wh[:, lo:hi], d, A.add, ["wh", dK], ["wrep0_%d" % p])
            else:
                tt(T.wf[:, lo:hi], T.t4[:, lo:hi], d, A.add, [dK, "t4"], ["wf%d" % p])

        def names_home(p):
            lo, hi, _ = parts[p]
            dw, lw = T["dw%d" % p], T["lw%d" % p]
            dma("s", dw[:], T.wf[:, lo:hi], ["wf%d" % p], ["dw%d" % p])
            dma("s", T.yn[own, lo:hi], T.wf[own, lo:hi], ["wf%d" % p], ["yo%d" % p])
            send(lambda k: dw[k], lw[r], ["dw%d" % p], ["lw%d" % p])

        def names_out(p):
            lo, hi, _ = parts[p]
            for a, b in ((0, r), (r + 1, NR)):
                if a < b:
                    dma("sa"[a > 0], T.yn[16 * a:16 * b, lo:hi], T["lw%d" % p][a:b], ["lw%d" % p], ["yn%d_%d" % (p, a)])

        def squares():
            act(T.sq[:], T.sg[:], AF.Square, ["sg", "sg0"], ["sq"], bias=CEN / 64.0, scale=1.0 / 64.0)
            for k in range(8):
                dma("a", T.ye[16 * k:16 * k + 16, :], blk(T.sq, k, 64), ["sq"], ["ye%d" % k])
            for k in range(8):
                mm(PB(D[0])[:, 0:64], T.idf[:], blk(T.sq, k, 64), k == 0, k == 7, ["idf", "sq"], [BK(D[0])], inc=(k == 7))
            act(T.ydt[:], PB(D[0])[:, 0:64], AF.Copy, [BK(D[0])], ["ydt"])
            dma("a", T.yd[:], T.ydt[:], ["ydt"], ["yd"])

        steps = {"G": gather_v, "C": conv, "T": twin, "L": level, "E": median_out, "H": chain, "CH": challengers,
                 "Z": zero_count, "HP": name_part, "HO": offsets, "NL": name_list,
                 "SV": sub_v, "AV": abs_v, "U": gather_u, "SU": sub_u, "AU": abs_u, "K": cmp, "N": count,
                 "VD": void_twice, "VE": void_eq, "VC": void_count, "FL": eighths, "DC": change, "ON": old_names,
                 "SUM": sum_e, "R": rest, "XP": x_part, "X": new_x, "NA": minus_x, "NN": new_names, "S": spread, "NH": names_home, "NO": names_out, "SQ": squares,
                 "W": lambda m: win_part(win_x, m), "M": lambda m: win_part(win_n, m),
                 "O": lambda m, e: win_out(m, banks[m], e), "PX": place_x}
        for w in plan:
            name = w.rstrip("0123456789avg")
            steps[name](*[int(c) if c.isdigit() else c for c in w[len(name):]])

    for s, val in cnt.items():
        if val:
            g.sync.wait_ge(T.sem[s], val)
